import numpy as np
import ml_dtypes


def mxq(x, axis, fmt="e4m3"):
    dtype, down = {"e4m3": (ml_dtypes.float8_e4m3fn, 7), "e5m2": (ml_dtypes.float8_e5m2, 14)}[fmt]
    v = np.moveaxis(np.asarray(x, np.float32).astype(ml_dtypes.bfloat16).astype(np.float64), axis, -1)
    blocks = v.reshape(v.shape[:-1] + (-1, 32))
    amax = np.abs(blocks).max(-1, keepdims=True)
    byte = np.maximum(np.where(amax > 0, np.frexp(amax)[1] - 1 + 127, 0) - down, 1)
    scale = np.exp2(byte - 127.0)
    codes = (blocks / scale).astype(np.float32).astype(dtype).astype(np.float64)
    return np.moveaxis((codes * scale).reshape(v.shape), -1, axis)


WIDE = False


def mx_kscale(k):
    if not WIDE:
        return np.ones(k)
    levels = np.array([10, -10, 5, -5, 0])
    if k % 512:
        return np.exp2(np.random.permutation(np.resize(levels, k // 32))).repeat(32)
    a = np.empty((k // 512, 16))
    for p in range(k // 512):
        a[p, :8] = np.random.permutation(np.resize(levels, 8))
        for g in range(8):
            far = levels[np.abs(levels - a[p, g]) >= 10]
            a[p, g + 8] = far[np.random.randint(len(far))]
    return np.exp2(a.ravel()).repeat(32)


def f64(x):
    return np.asarray(x).astype(np.float64)


def striped(idx):
    return np.tile(idx.reshape(-1, 16).T, (8, 1)).astype(np.uint16)


def unstriped(offs):
    return offs[:16].T.reshape(-1).astype(np.int64)


E2M1 = np.array([0.0, 0.5, 1.0, 1.5, 2.0, 3.0, 4.0, 6.0, -0.0, -0.5, -1.0, -1.5, -2.0, -3.0, -4.0, -6.0])


def pack_weight(w, fmt):
    k, n = w.shape
    w = f64(np.asarray(w, np.float32).astype(ml_dtypes.bfloat16)).reshape(k // 32, 32, n)
    amax = np.abs(w).max(1)
    if fmt == "e4m3":
        byte = np.frexp(amax)[1] - 1 + 127 - 7
    else:
        mant, ex = np.frexp(amax / 6.0)
        byte = np.where(mant > 0.5, ex, ex - 1) + 127
    byte = np.clip(np.where(amax > 0, byte, 1), 1, 254)
    scaled = (w * np.exp2(127.0 - byte)[:, None, :]).reshape(k, n).astype(np.float32)
    by_word = np.ascontiguousarray(scaled.reshape(k // 512, 128, 4, n).transpose(0, 1, 3, 2))
    if fmt == "e4m3":
        words = by_word.astype(ml_dtypes.float8_e4m3fn).view(np.uint8)
    else:
        c = by_word.astype(ml_dtypes.float4_e2m1fn).view(np.uint8) & 0xF
        words = (c[..., 0::2] | (c[..., 1::2] << 4)).reshape(k // 512, 128, 2 * n)
    return np.ascontiguousarray(words), np.ascontiguousarray(byte.astype(np.uint8).reshape(k // 512, 16, n))


def unpack_weight(words, scales, fmt):
    g, _, n = scales.shape
    words = np.ascontiguousarray(words).reshape(g, 128, n, -1)
    if fmt == "e4m3":
        vals = words.view(ml_dtypes.float8_e4m3fn).astype(np.float64)
    else:
        nib = np.empty((g, 128, n, 4), np.uint8)
        nib[..., 0::2] = words & 0xF
        nib[..., 1::2] = words >> 4
        vals = E2M1[nib]
    vals = vals * np.repeat(np.exp2(scales.astype(np.float64) - 127.0), 8, axis=1)[..., None]
    return vals.transpose(0, 1, 3, 2).reshape(g * 512, n)


def gelu(v):
    return 0.5 * v * (1.0 + np.tanh(np.sqrt(2.0 / np.pi) * (v + 0.044715 * v**3)))


def striped8(idx):
    return np.concatenate([v.reshape(-1, 16).T for v in idx]).astype(np.uint16)


def unstriped8(offs):
    return np.stack([offs[16 * g:16 * g + 16].T.reshape(-1) for g in range(8)]).astype(np.int64)


def put_heads(h, wgs, idx8, t2):
    r = np.arange(h.shape[0])
    page = np.zeros((h.shape[0], t2))
    page[r[:, None], idx8[r % 512 // 64]] = wgs[r // 4 % 128] * h
    return page


K1, K, H, N, T, S, T2 = 512, 1024, 1024, 512, 2048, 1024, 2048

def setup_inputs():
    n = np.random.standard_normal
    s = mx_kscale(K)[:, None]
    u = mx_kscale(H)[:, None]
    cur = n((K1, T))
    tab_words, tab_scales = pack_weight(np.concatenate([cur, cur * cur], axis=0) * s, "e4m3")
    offs = striped(np.random.permutation(T)[:S])
    w1 = (n((K1, H)) / np.sqrt(K1) / s[:K1]).astype(np.float32)
    w2_words, w2_scales = pack_weight(0.5 * n((K1, H)) / np.sqrt(K1) / s[K1:], "e2m1")
    wgs = np.repeat(np.random.uniform(0.5, 2.0, (8, S)), 16, axis=0).astype(np.float32)
    offs2 = striped8(np.stack([np.random.permutation(T2)[:S] for _ in range(8)]))
    gain = (np.exp(0.3 * n((H, T2))) * u).astype(np.float32)
    w3 = (n((H, N)) / np.sqrt(H) / u).astype(np.float32)
    amb = (0.5 * n((N, T2))).astype(np.float32)
    return {"tab_words": tab_words, "tab_scales": tab_scales, "offs": offs, "w1": w1,
            "w2_words": w2_words, "w2_scales": w2_scales, "wgs": wgs, "offs2": offs2,
            "gain": gain, "w3": w3, "amb": amb}

def reference(tab_words, tab_scales, offs, w1, w2_words, w2_scales, wgs, offs2, gain, w3, amb):
    v = unpack_weight(tab_words, tab_scales, "e4m3")[:, unstriped(offs)]
    w2 = unpack_weight(w2_words, w2_scales, "e2m1")
    e = mxq(f64(w1), 0, "e4m3").T @ v[:K1] + w2.T @ v[K1:]
    h = 0.5 * e * (1.0 + np.tanh(np.sqrt(2.0 / np.pi) * (e + 0.044715 * e * e * e)))
    page = put_heads(h, f64(wgs), unstriped8(offs2), T2)
    z = page * f64(gain)
    y = mxq(f64(w3), 0, "e4m3").T @ mxq(z, 0, "e4m3")
    return y + f64(amb)

@@ -1,0 +1,278 @@
+from contextlib import ExitStack
+
+import concourse.mybir as mybir
+
+K1, H, N, T, S, T2 = 512, 1024, 512, 2048, 1024, 2048
+FLOPS = 2 * (2 * K1) * H * S + 2 * H * N * T2
+
+F32 = mybir.dt.float32
+BF16 = mybir.dt.bfloat16
+I32 = mybir.dt.int32
+U32 = mybir.dt.uint32
+U16 = mybir.dt.uint16
+U8 = mybir.dt.uint8
+FP8X4 = mybir.dt.float8_e4m3fn_x4
+FP4X4 = mybir.dt.float4_e2m1fn_x4
+MULT = mybir.AluOpType.mult
+ADD = mybir.AluOpType.add
+GELU = mybir.ActivationFunctionType.Gelu_apprx_tanh
+
+P = 128
+PACK = 4
+K_PASS = P * PACK
+BANK = 512
+BANKS = 8
+HALVES = S // BANK
+CHUNKS = T2 // BANK
+N_TILES = N // P
+PAGES = 3
+SCALE_ROW = (4, 0)
+SLICES = [(0, 0), (0, 1), (0, 2), (0, 3), (1, 2), (1, 0), (1, 1), (1, 3)]
+
+
+def tile_list_transformer_overload_board_kernel(
+    tc, tab_words, tab_scales, offs, w1, w2_words, w2_scales, wgs, offs2, gain, w3, amb, out
+):
+    nc = tc.nc
+    with ExitStack() as ctx:
+        keep = ctx.enter_context(tc.tile_pool(name="keep", bufs=1))
+        stage = ctx.enter_context(tc.tile_pool(name="stage", bufs=8))
+        ring = ctx.enter_context(tc.tile_pool(name="ring", bufs=2))
+        psum = ctx.enter_context(tc.psum_pool(name="psum", bufs=1))
+
+        def load_rows(src, dtype, name):
+            t = stage.tile([P, 2048], dtype, name=name, tag="rows")
+            nc.sync.dma_start(t[:], src)
+            return t
+
+        def load_k_first(src, name):
+            t = stage.tile([P, PACK, 512], F32, name=name, tag="rows")
+            nc.sync.dma_start(t[:], src.rearrange("(p j) c -> p j c", j=PACK))
+            return t
+
+        tab_s = keep.tile([P, T], U8, name="tab_s", align_bytes=64)
+        w2_s_raw = keep.tile([P, H], U8, name="w2_s_raw", align_bytes=64)
+        nc.vector.memset(tab_s[:].bitcast(I32), 0)
+        nc.vector.memset(w2_s_raw[:].bitcast(I32), 0)
+
+        idx = keep.tile([P, S // 16], U16, name="idx")
+        nc.sync.dma_start(idx[:], offs)
+        tab0 = load_rows(tab_words[0].rearrange("p t i -> p (t i)").bitcast(I32), I32, "tab0")
+        for a in range(2):
+            for q in range(4):
+                row = 32 * q + SCALE_ROW[a]
+                nc.sync.dma_start(
+                    tab_s[row : row + 4, :].bitcast(I32),
+                    tab_scales[a, 4 * q : 4 * q + 4, :].bitcast(I32),
+                )
+        w1_raw = [load_k_first(w1[:, 0:512], "w1_raw0")]
+        w2_raw = keep.tile([P, 2 * H], U8, name="w2_raw")
+        nc.sync.dma_start(w2_raw[:].bitcast(I32), w2_words[0].bitcast(I32))
+        for q in range(4):
+            nc.sync.dma_start(
+                w2_s_raw[32 * q : 32 * q + 4, :].bitcast(I32),
+                w2_scales[0, 4 * q : 4 * q + 4, :].bitcast(I32),
+            )
+        tab1 = keep.tile([P, T], I32, name="tab1", tag="tab1_then_page")
+        nc.sync.dma_start(tab1[:], tab_words[1].rearrange("p t i -> p (t i)").bitcast(I32))
+        tabs = [tab0, tab1]
+        wgs_sb = keep.tile([P, S], F32, name="wgs_sb")
+        nc.sync.dma_start(wgs_sb[:], wgs)
+        idx2 = keep.tile([P, S // 16], U16, name="idx2")
+        nc.sync.dma_start(idx2[:], offs2)
+
+        pages = [keep.tile([P, T2], F32, name="page%d" % i) for i in range(PAGES - 1)]
+        for page in pages:
+            nc.vector.memset(page[:], 0.0)
+
+        gain_rows = gain.rearrange("(b p j) m -> b j p m", b=2, j=PACK)
+        w1_raw.append(load_k_first(w1[:, 512:1024], "w1_raw1"))
+        gains = {}
+        w3_raw = []
+        for k, (b, t) in enumerate(SLICES):
+            gains[k] = load_rows(gain_rows[b, t], F32, "gain%d" % k)
+            if k in (1, 2):
+                w3_raw.append(load_k_first(w3[512 * (k - 1) : 512 * k, :], "w3_raw%d" % (k - 1)))
+        ambs = []
+        for c in range(CHUNKS):
+            a_sb = stage.tile([P, N_TILES, BANK], F32, name="amb%d" % c, tag="rows")
+            nc.sync.dma_start(a_sb[:], amb[:, c * BANK : (c + 1) * BANK].rearrange("(i p) m -> p i m", p=P))
+            ambs.append(a_sb)
+
+        def quantize(src_bf16, name):
+            codes = keep.tile([P, 512], U32, name=name + "_codes", align_bytes=64)
+            scales = keep.tile([P, 512], U8, name=name + "_scales", align_bytes=64)
+            nc.vector.quantize_mx(out=codes[:].bitcast(FP8X4), scales=scales[:], in_=src_bf16)
+            return codes, scales
+
+        def cast_w1(b, pool, tag):
+            g = pool.tile([P, 2048], BF16, name="w_bf16", tag=tag, align_bytes=64)
+            nc.scalar.copy(
+                g[:].rearrange("p (t m j) -> p m j t", t=PACK, j=PACK),
+                w1_raw[b][:].rearrange("p j (m t) -> p m j t", t=PACK),
+            )
+            return g
+
+        def cast_w3(b):
+            g = ring.tile([P, 2048], BF16, name="w_bf16", tag="w_bf16", align_bytes=64)
+            nc.scalar.copy(
+                g[:].rearrange("p (c i j) -> p c j i", i=4, j=PACK),
+                w3_raw[b][:].rearrange("p j (c i) -> p c j i", i=4),
+            )
+            return g
+
+        g_words = {}
+        g_scales = {}
+
+        def gather_words(a, jh, tag):
+            wd = keep.tile([P, BANK], U32, name="g_words", tag=tag, align_bytes=64)
+            nc.vector.tensor_copy(wd[:], tabs[a][:].bitcast(U32).indirect(idx[:, jh * 32 : (jh + 1) * 32]))
+            g_words[a, jh] = wd
+
+        def gather_scales(jh):
+            sc = keep.tile([P, BANK], U8, name="g_scales%d" % jh, align_bytes=64)
+            nc.vector.tensor_copy(sc[:], tab_s[:].indirect(idx[:, jh * 32 : (jh + 1) * 32]))
+            g_scales[jh] = sc
+
+        w1_bf0 = cast_w1(0, keep, "w1_then_words")
+        gather_words(0, 0, "words00")
+        gather_scales(0)
+        w2_p = keep.tile([P, 2 * H], U8, name="w2_p", align_bytes=64)
+        w2_s = keep.tile([P, H], U8, name="w2_s", align_bytes=64)
+        w1q = [quantize(w1_bf0[:], "w1q0")]
+        gather_words(1, 0, "words10")
+        nc.vector.tensor_copy(
+            w2_p[:].bitcast(U16).rearrange("p (b t m) -> p b t m", b=2, t=PACK),
+            w2_raw[:].bitcast(U16).rearrange("p (b m t) -> p b t m", b=2, t=PACK),
+        )
+        nc.vector.tensor_copy(
+            w2_s[:].rearrange("p (b t m) -> p b t m", b=2, t=PACK),
+            w2_s_raw[:].rearrange("p (b m t) -> p b t m", b=2, t=PACK),
+        )
+        gather_words(0, 1, "words01")
+        gather_scales(1)
+        gather_words(1, 1, "w1_then_words")
+        last_page = keep.tile([P, T2], F32, name="page_last", tag="tab1_then_page")
+        pages.append(last_page)
+
+        hs = {}
+
+        def stage1(k):
+            b, t = SLICES[k]
+            h = keep.tile([P, S], F32, name="h%d" % k)
+            col = b * 512 + t * P
+            for jh in range(HALVES):
+                acc = psum.tile([P, BANK], F32, name="e_acc", tag="bank%d" % ((2 * k + jh) % BANKS))
+                nc.tensor.matmul_mx(
+                    out=acc[:],
+                    lhsT=w1q[b][0][:, t * P : (t + 1) * P].bitcast(FP8X4),
+                    lhsT_scale=w1q[b][1][:, t * P : (t + 1) * P],
+                    rhs=g_words[0, jh][:].bitcast(FP8X4),
+                    rhs_scale=g_scales[jh][SCALE_ROW[0] : P, :],
+                    start=True,
+                    stop=False,
+                )
+                nc.tensor.matmul_mx(
+                    out=acc[:],
+                    lhsT=w2_p[:, 2 * col : 2 * (col + P)].bitcast(FP4X4),
+                    lhsT_scale=w2_s[:, col : col + P],
+                    rhs=g_words[1, jh][:].bitcast(FP8X4),
+                    rhs_scale=g_scales[jh][SCALE_ROW[1] : P, :],
+                    start=False,
+                    stop=True,
+                )
+                nc.scalar.activation(h[:, jh * BANK : (jh + 1) * BANK], acc[:], GELU)
+            hs[k] = h
+
+        def weigh(k):
+            nc.gpsimd.tensor_tensor(hs[k][:], hs[k][:], wgs_sb[:], MULT)
+
+        def scatter(k):
+            nc.vector.tensor_copy(pages[k % PAGES][:].indirect(idx2[:]), hs[k][:])
+
+        z_pairs = [ring.tile([P, 4 * T2], BF16, name="z_pairs%d" % b, tag="z_pairs") for b in range(2)]
+
+        def z_slot(k):
+            b, t = SLICES[k]
+            v = z_pairs[b][:].rearrange("p (c u m e) -> p c u m e", c=CHUNKS, u=2, e=2)
+            return v[:, :, t // 2, :, t % 2]
+
+        def times_gain(k):
+            nc.gpsimd.tensor_tensor(
+                z_slot(k),
+                pages[k % PAGES][:].rearrange("p (c m) -> p c m", c=CHUNKS),
+                gains[k][:].rearrange("p (c m) -> p c m", c=CHUNKS),
+                MULT,
+            )
+
+        zq = {}
+
+        def interleave_quantize(b, c):
+            zi = ring.tile([P, PACK * BANK], BF16, name="z_words", tag="z_words", bufs=3, align_bytes=64)
+            nc.scalar.copy(
+                zi[:].bitcast(F32).rearrange("p (m u) -> p m u", u=2),
+                z_pairs[b][:, c * 2048 : (c + 1) * 2048].bitcast(F32).rearrange("p (u m) -> p m u", u=2),
+            )
+            zq[b, c] = quantize(zi[:], "zq%d%d" % (b, c))
+
+        w3q = []
+        y_acc = {}
+
+        def stage2_pass(b, c, i):
+            if b == 0:
+                y_acc[c, i] = psum.tile([P, BANK], F32, name="y_acc", tag="bank%d" % ((N_TILES * c + i) % BANKS))
+            nc.tensor.matmul_mx(
+                out=y_acc[c, i][:],
+                lhsT=w3q[b][0][:, i * P : (i + 1) * P].bitcast(FP8X4),
+                lhsT_scale=w3q[b][1][:, i * P : (i + 1) * P],
+                rhs=zq[b, c][0][:].bitcast(FP8X4),
+                rhs_scale=zq[b, c][1][:],
+                start=(b == 0),
+                stop=(b == 1),
+            )
+
+        stage1(0)
+        h0 = hs[0]
+        nc.vector.tensor_tensor(h0[:, 0:BANK], h0[:, 0:BANK], wgs_sb[:, 0:BANK], MULT)
+        nc.vector.tensor_copy(pages[0][:].indirect(idx2[:, 0:32]), h0[:, 0:BANK])
+        nc.gpsimd.tensor_tensor(h0[:, BANK:S], h0[:, BANK:S], wgs_sb[:, BANK:S], MULT)
+        nc.vector.tensor_copy(pages[0][:].indirect(idx2[:, 32:64]), h0[:, BANK:S])
+        nc.gpsimd.memset(last_page[:], 0.0)
+        for k in range(1, 4):
+            stage1(k)
+        weigh(1)
+        w1q.append(quantize(cast_w1(1, ring, "w_bf16")[:], "w1q1"))
+        for k in range(4, 8):
+            stage1(k)
+        weigh(2)
+        for k in range(1, 8):
+            scatter(k)
+            times_gain(k - 1)
+            if k + 2 < 8:
+                weigh(k + 2)
+            if k in (2, 3):
+                w3q.append(quantize(cast_w3(k - 2)[:], "w3q%d" % (k - 2)))
+            if k == 4:
+                for c in range(CHUNKS):
+                    interleave_quantize(0, c)
+                for c in range(2):
+                    for i in range(N_TILES):
+                        stage2_pass(0, c, i)
+
+        last = len(SLICES) - 1
+        for c in range(CHUNKS):
+            cols = slice(c * BANK, (c + 1) * BANK)
+            nc.vector.tensor_tensor(z_slot(last)[:, c, :], pages[last % PAGES][:, cols], gains[last][:, cols], MULT)
+            interleave_quantize(1, c)
+            for i in range(N_TILES):
+                if c >= 2:
+                    stage2_pass(0, c, i)
+                stage2_pass(1, c, i)
+                res = ambs[c][:, i, :]
+                if i == 0:
+                    y_sb = ring.tile([P, BANK], F32, name="y_sb", tag="y_sb")
+                    nc.scalar.copy(y_sb[:], y_acc[c, i][:])
+                    nc.gpsimd.tensor_tensor(res, y_sb[:], res, ADD)
+                else:
+                    nc.vector.tensor_tensor(res, y_acc[c, i][:], res, ADD)
+                nc.sync.dma_start(out[i * P : (i + 1) * P, cols], res)

@@ -36,7 +36,7 @@ def tile_list_transformer_overload_board_kernel(
     nc = tc.nc
     with ExitStack() as ctx:
         keep = ctx.enter_context(tc.tile_pool(name="keep", bufs=1))
-        stage = ctx.enter_context(tc.tile_pool(name="stage", bufs=8))
+        stage = ctx.enter_context(tc.tile_pool(name="stage", bufs=7))
         ring = ctx.enter_context(tc.tile_pool(name="ring", bufs=2))
         psum = ctx.enter_context(tc.psum_pool(name="psum", bufs=1))
 
@@ -52,8 +52,8 @@ def tile_list_transformer_overload_board_kernel(
 
         tab_s = keep.tile([P, T], U8, name="tab_s", align_bytes=64)
         w2_s_raw = keep.tile([P, H], U8, name="w2_s_raw", align_bytes=64)
-        nc.vector.memset(tab_s[:].bitcast(I32), 0)
-        nc.vector.memset(w2_s_raw[:].bitcast(I32), 0)
+        nc.gpsimd.memset(tab_s[:].bitcast(I32), 0)
+        nc.gpsimd.memset(w2_s_raw[:].bitcast(I32), 0)
 
         idx = keep.tile([P, S // 16], U16, name="idx")
         nc.sync.dma_start(idx[:], offs)
@@ -73,53 +73,56 @@ def tile_list_transformer_overload_board_kernel(
                 w2_s_raw[32 * q : 32 * q + 4, :].bitcast(I32),
                 w2_scales[0, 4 * q : 4 * q + 4, :].bitcast(I32),
             )
-        tab1 = keep.tile([P, T], I32, name="tab1", tag="tab1_then_page")
-        nc.sync.dma_start(tab1[:], tab_words[1].rearrange("p t i -> p (t i)").bitcast(I32))
+        tab1 = load_rows(tab_words[1].rearrange("p t i -> p (t i)").bitcast(I32), I32, "tab1")
         tabs = [tab0, tab1]
         wgs_sb = keep.tile([P, S], F32, name="wgs_sb")
         nc.sync.dma_start(wgs_sb[:], wgs)
         idx2 = keep.tile([P, S // 16], U16, name="idx2")
         nc.sync.dma_start(idx2[:], offs2)
 
-        pages = [keep.tile([P, T2], F32, name="page%d" % i) for i in range(PAGES - 1)]
+        pages = [keep.tile([P, T2], F32, name="page%d" % i) for i in range(PAGES)]
         for page in pages:
-            nc.vector.memset(page[:], 0.0)
+            nc.gpsimd.memset(page[:], 0.0)
 
         gain_rows = gain.rearrange("(b p j) m -> b j p m", b=2, j=PACK)
         w1_raw.append(load_k_first(w1[:, 512:1024], "w1_raw1"))
         gains = {}
-        w3_raw = []
+        w3_raw = [load_k_first(w3[0:512, :], "w3_raw0")]
         for k, (b, t) in enumerate(SLICES):
-            gains[k] = load_rows(gain_rows[b, t], F32, "gain%d" % k)
-            if k in (1, 2):
-                w3_raw.append(load_k_first(w3[512 * (k - 1) : 512 * k, :], "w3_raw%d" % (k - 1)))
+            if k == 4:
+                gains[k] = keep.tile([P, T2], F32, name="gain_held", tag="gain%d_then_codes" % k, align_bytes=64)
+                nc.sync.dma_start(gains[k][:], gain_rows[b, t])
+            else:
+                gains[k] = load_rows(gain_rows[b, t], F32, "gain%d" % k)
+            if k == 1:
+                w3_raw.append(load_k_first(w3[512:1024, :], "w3_raw1"))
         ambs = []
         for c in range(CHUNKS):
             a_sb = stage.tile([P, N_TILES, BANK], F32, name="amb%d" % c, tag="rows")
             nc.sync.dma_start(a_sb[:], amb[:, c * BANK : (c + 1) * BANK].rearrange("(i p) m -> p i m", p=P))
             ambs.append(a_sb)
 
-        def quantize(src_bf16, name):
-            codes = keep.tile([P, 512], U32, name=name + "_codes", align_bytes=64)
-            scales = keep.tile([P, 512], U8, name=name + "_scales", align_bytes=64)
+        def quantize(src_bf16, name, tag=""):
+            width = src_bf16.shape[1] // PACK
+            codes = keep.tile([P, width], U32, name=name + "_codes", tag=tag, align_bytes=64)
+            scales = keep.tile([P, width], U8, name=name + "_scales", align_bytes=64)
             nc.vector.quantize_mx(out=codes[:].bitcast(FP8X4), scales=scales[:], in_=src_bf16)
             return codes, scales
 
-        def cast_w1(b, pool, tag):
-            g = pool.tile([P, 2048], BF16, name="w_bf16", tag=tag, align_bytes=64)
+        def cast_w1(b, dst):
             nc.scalar.copy(
-                g[:].rearrange("p (t m j) -> p m j t", t=PACK, j=PACK),
+                dst.rearrange("p (t m j) -> p m j t", t=PACK, j=PACK),
                 w1_raw[b][:].rearrange("p j (m t) -> p m j t", t=PACK),
             )
-            return g
 
-        def cast_w3(b):
-            g = ring.tile([P, 2048], BF16, name="w_bf16", tag="w_bf16", align_bytes=64)
+        def cast_w3(b, dst):
             nc.scalar.copy(
-                g[:].rearrange("p (c i j) -> p c j i", i=4, j=PACK),
+                dst.rearrange("p (c i j) -> p c j i", i=4, j=PACK),
                 w3_raw[b][:].rearrange("p j (c i) -> p c j i", i=4),
             )
-            return g
+
+        def halves(codes, scales):
+            return [(codes[:, c * BANK : (c + 1) * BANK], scales[:, c * BANK : (c + 1) * BANK]) for c in range(2)]
 
         g_words = {}
         g_scales = {}
@@ -134,7 +137,8 @@ def tile_list_transformer_overload_board_kernel(
             nc.vector.tensor_copy(sc[:], tab_s[:].indirect(idx[:, jh * 32 : (jh + 1) * 32]))
             g_scales[jh] = sc
 
-        w1_bf0 = cast_w1(0, keep, "w1_then_words")
+        w1_bf0 = keep.tile([P, 2048], BF16, name="w1_bf0", tag="w1_then_words", align_bytes=64)
+        cast_w1(0, w1_bf0[:])
         gather_words(0, 0, "words00")
         gather_scales(0)
         w2_p = keep.tile([P, 2 * H], U8, name="w2_p", align_bytes=64)
@@ -152,14 +156,12 @@ def tile_list_transformer_overload_board_kernel(
         gather_words(0, 1, "words01")
         gather_scales(1)
         gather_words(1, 1, "w1_then_words")
-        last_page = keep.tile([P, T2], F32, name="page_last", tag="tab1_then_page")
-        pages.append(last_page)
 
         hs = {}
 
         def stage1(k):
             b, t = SLICES[k]
-            h = keep.tile([P, S], F32, name="h%d" % k)
+            h = keep.tile([P, S], F32, name="h", tag="h%d" % k, align_bytes=64)
             col = b * 512 + t * P
             for jh in range(HALVES):
                 acc = psum.tile([P, BANK], F32, name="e_acc", tag="bank%d" % ((2 * k + jh) % BANKS))
@@ -207,15 +209,23 @@ def tile_list_transformer_overload_board_kernel(
 
         zq = {}
 
-        def interleave_quantize(b, c):
-            zi = ring.tile([P, PACK * BANK], BF16, name="z_words", tag="z_words", bufs=3, align_bytes=64)
+        def interleave(b, c0, n_chunks, dst):
             nc.scalar.copy(
-                zi[:].bitcast(F32).rearrange("p (m u) -> p m u", u=2),
-                z_pairs[b][:, c * 2048 : (c + 1) * 2048].bitcast(F32).rearrange("p (u m) -> p m u", u=2),
+                dst.bitcast(F32).rearrange("p (c m u) -> p c m u", c=n_chunks, u=2),
+                z_pairs[b][:, c0 * 2048 : (c0 + n_chunks) * 2048]
+                .bitcast(F32)
+                .rearrange("p (c u m) -> p c m u", c=n_chunks, u=2),
             )
-            zq[b, c] = quantize(zi[:], "zq%d%d" % (b, c))
 
-        w3q = []
+        def bf16_stage(width):
+            return ring.tile([P, width], BF16, name="bf16_stage", tag="bf16_stage", bufs=3, align_bytes=64)
+
+        def quantize_z0(c0, tag):
+            zi = bf16_stage(4096)
+            interleave(0, c0, 2, zi[:])
+            zq[0, c0], zq[0, c0 + 1] = halves(*quantize(zi[:], "zq0%d" % c0, tag))
+
+        w3q = {}
         y_acc = {}
 
         def stage2_pass(b, c, i):
@@ -225,8 +235,8 @@ def tile_list_transformer_overload_board_kernel(
                 out=y_acc[c, i][:],
                 lhsT=w3q[b][0][:, i * P : (i + 1) * P].bitcast(FP8X4),
                 lhsT_scale=w3q[b][1][:, i * P : (i + 1) * P],
-                rhs=zq[b, c][0][:].bitcast(FP8X4),
-                rhs_scale=zq[b, c][1][:],
+                rhs=zq[b, c][0].bitcast(FP8X4),
+                rhs_scale=zq[b, c][1],
                 start=(b == 0),
                 stop=(b == 1),
             )
@@ -237,42 +247,46 @@ def tile_list_transformer_overload_board_kernel(
         nc.vector.tensor_copy(pages[0][:].indirect(idx2[:, 0:32]), h0[:, 0:BANK])
         nc.gpsimd.tensor_tensor(h0[:, BANK:S], h0[:, BANK:S], wgs_sb[:, BANK:S], MULT)
         nc.vector.tensor_copy(pages[0][:].indirect(idx2[:, 32:64]), h0[:, BANK:S])
-        nc.gpsimd.memset(last_page[:], 0.0)
         for k in range(1, 4):
             stage1(k)
-        weigh(1)
-        w1q.append(quantize(cast_w1(1, ring, "w_bf16")[:], "w1q1"))
+            weigh(k)
+        w_pair = bf16_stage(4096)
+        cast_w1(1, w_pair[:, 0:2048])
+        cast_w3(0, w_pair[:, 2048:4096])
+        w1q1, w3q[0] = halves(*quantize(w_pair[:], "w1q1_w3q0"))
+        w1q.append(w1q1)
         for k in range(4, 8):
             stage1(k)
-        weigh(2)
-        for k in range(1, 8):
-            scatter(k)
-            times_gain(k - 1)
-            if k + 2 < 8:
-                weigh(k + 2)
-            if k in (2, 3):
-                w3q.append(quantize(cast_w3(k - 2)[:], "w3q%d" % (k - 2)))
-            if k == 4:
-                for c in range(CHUNKS):
-                    interleave_quantize(0, c)
-                for c in range(2):
-                    for i in range(N_TILES):
-                        stage2_pass(0, c, i)
-
+        w3_z = keep.tile([P, 4096], BF16, name="w3_z", align_bytes=64)
+        cast_w3(1, w3_z[:, 0:2048])
         last = len(SLICES) - 1
+        for k in range(1, 8):
+            times_gain(k - 1)
+            if 4 <= k + 2 <= last:
+                weigh(k + 2)
+            if k == last:
+                quantize_z0(0, "gain4_then_codes")
+            scatter(k)
+        for c in range(2):
+            for i in range(N_TILES):
+                stage2_pass(0, c, i)
+
         for c in range(CHUNKS):
             cols = slice(c * BANK, (c + 1) * BANK)
             nc.vector.tensor_tensor(z_slot(last)[:, c, :], pages[last % PAGES][:, cols], gains[last][:, cols], MULT)
-            interleave_quantize(1, c)
+            if c == 0:
+                quantize_z0(2, "h7")
+                interleave(1, 0, 1, w3_z[:, 2048:4096])
+                w3q[1], zq[1, 0] = halves(*quantize(w3_z[:], "w3q1_zq10"))
+            else:
+                zi = bf16_stage(2048)
+                interleave(1, c, 1, zi[:])
+                codes, scales = quantize(zi[:], "zq1%d" % c)
+                zq[1, c] = (codes[:], scales[:])
             for i in range(N_TILES):
                 if c >= 2:
                     stage2_pass(0, c, i)
                 stage2_pass(1, c, i)
                 res = ambs[c][:, i, :]
-                if i == 0:
-                    y_sb = ring.tile([P, BANK], F32, name="y_sb", tag="y_sb")
-                    nc.scalar.copy(y_sb[:], y_acc[c, i][:])
-                    nc.gpsimd.tensor_tensor(res, y_sb[:], res, ADD)
-                else:
-                    nc.vector.tensor_tensor(res, y_acc[c, i][:], res, ADD)
+                nc.vector.tensor_tensor(res, y_acc[c, i][:], res, ADD)
                 nc.sync.dma_start(out[i * P : (i + 1) * P, cols], res)

@@ -75,6 +75,7 @@ def tile_list_transformer_overload_board_kernel(
             )
         tab1 = load_rows(tab_words[1].rearrange("p t i -> p (t i)").bitcast(I32), I32, "tab1")
         tabs = [tab0, tab1]
+        w1_raw.append(load_k_first(w1[:, 512:1024], "w1_raw1"))
         wgs_sb = keep.tile([P, S], F32, name="wgs_sb")
         nc.sync.dma_start(wgs_sb[:], wgs)
         idx2 = keep.tile([P, S // 16], U16, name="idx2")
@@ -85,17 +86,16 @@ def tile_list_transformer_overload_board_kernel(
             nc.gpsimd.memset(page[:], 0.0)
 
         gain_rows = gain.rearrange("(b p j) m -> b j p m", b=2, j=PACK)
-        w1_raw.append(load_k_first(w1[:, 512:1024], "w1_raw1"))
         gains = {}
-        w3_raw = [load_k_first(w3[0:512, :], "w3_raw0")]
+        w3_raw = []
         for k, (b, t) in enumerate(SLICES):
             if k == 4:
                 gains[k] = keep.tile([P, T2], F32, name="gain_held", tag="gain%d_then_codes" % k, align_bytes=64)
                 nc.sync.dma_start(gains[k][:], gain_rows[b, t])
             else:
                 gains[k] = load_rows(gain_rows[b, t], F32, "gain%d" % k)
-            if k == 1:
-                w3_raw.append(load_k_first(w3[512:1024, :], "w3_raw1"))
+            if k in (0, 1):
+                w3_raw.append(load_k_first(w3[512 * k : 512 * (k + 1), :], "w3_raw%d" % k))
         ambs = []
         for c in range(CHUNKS):
             a_sb = stage.tile([P, N_TILES, BANK], F32, name="amb%d" % c, tag="rows")
@@ -109,8 +109,8 @@ def tile_list_transformer_overload_board_kernel(
             nc.vector.quantize_mx(out=codes[:].bitcast(FP8X4), scales=scales[:], in_=src_bf16)
             return codes, scales
 
-        def cast_w1(b, dst):
-            nc.scalar.copy(
+        def cast_w1(b, dst, copy):
+            copy(
                 dst.rearrange("p (t m j) -> p m j t", t=PACK, j=PACK),
                 w1_raw[b][:].rearrange("p j (m t) -> p m j t", t=PACK),
             )
@@ -138,7 +138,7 @@ def tile_list_transformer_overload_board_kernel(
             g_scales[jh] = sc
 
         w1_bf0 = keep.tile([P, 2048], BF16, name="w1_bf0", tag="w1_then_words", align_bytes=64)
-        cast_w1(0, w1_bf0[:])
+        cast_w1(0, w1_bf0[:], nc.scalar.copy)
         gather_words(0, 0, "words00")
         gather_scales(0)
         w2_p = keep.tile([P, 2 * H], U8, name="w2_p", align_bytes=64)
@@ -209,23 +209,16 @@ def tile_list_transformer_overload_board_kernel(
 
         zq = {}
 
-        def interleave(b, c0, n_chunks, dst):
+        def interleave(b, c, dst):
             nc.scalar.copy(
-                dst.bitcast(F32).rearrange("p (c m u) -> p c m u", c=n_chunks, u=2),
-                z_pairs[b][:, c0 * 2048 : (c0 + n_chunks) * 2048]
-                .bitcast(F32)
-                .rearrange("p (c u m) -> p c m u", c=n_chunks, u=2),
+                dst.bitcast(F32).rearrange("p (m u) -> p m u", u=2),
+                z_pairs[b][:, c * 2048 : (c + 1) * 2048].bitcast(F32).rearrange("p (u m) -> p m u", u=2),
             )
 
-        def bf16_stage(width):
-            return ring.tile([P, width], BF16, name="bf16_stage", tag="bf16_stage", bufs=3, align_bytes=64)
+        def bf16_stage(width, slot):
+            return keep.tile([P, width], BF16, name="bf16_stage", tag="bf16_stage%d" % slot, align_bytes=64)
 
-        def quantize_z0(c0, tag):
-            zi = bf16_stage(4096)
-            interleave(0, c0, 2, zi[:])
-            zq[0, c0], zq[0, c0 + 1] = halves(*quantize(zi[:], "zq0%d" % c0, tag))
-
-        w3q = {}
+        w3q = []
         y_acc = {}
 
         def stage2_pass(b, c, i):
@@ -241,51 +234,37 @@ def tile_list_transformer_overload_board_kernel(
                 stop=(b == 1),
             )
 
-        stage1(0)
-        h0 = hs[0]
-        nc.vector.tensor_tensor(h0[:, 0:BANK], h0[:, 0:BANK], wgs_sb[:, 0:BANK], MULT)
-        nc.vector.tensor_copy(pages[0][:].indirect(idx2[:, 0:32]), h0[:, 0:BANK])
-        nc.gpsimd.tensor_tensor(h0[:, BANK:S], h0[:, BANK:S], wgs_sb[:, BANK:S], MULT)
-        nc.vector.tensor_copy(pages[0][:].indirect(idx2[:, 32:64]), h0[:, BANK:S])
+        w1_bf1 = keep.tile([P, 2048], BF16, name="w1_bf1", tag="h1", align_bytes=64)
+        cast_w1(1, w1_bf1[:], nc.vector.tensor_copy)
+        w1q.append(quantize(w1_bf1[:], "w1q1"))
+        for k in range(8):
+            stage1(k)
+        nc.vector.tensor_tensor(hs[0][:], hs[0][:], wgs_sb[:], MULT)
+        scatter(0)
         for k in range(1, 4):
-            stage1(k)
             weigh(k)
-        w_pair = bf16_stage(4096)
-        cast_w1(1, w_pair[:, 0:2048])
-        cast_w3(0, w_pair[:, 2048:4096])
-        w1q1, w3q[0] = halves(*quantize(w_pair[:], "w1q1_w3q0"))
-        w1q.append(w1q1)
-        for k in range(4, 8):
-            stage1(k)
-        w3_z = keep.tile([P, 4096], BF16, name="w3_z", align_bytes=64)
-        cast_w3(1, w3_z[:, 0:2048])
+        w3_bf = bf16_stage(4096, 3)
+        for b in range(2):
+            cast_w3(b, w3_bf[:, b * 2048 : (b + 1) * 2048])
         last = len(SLICES) - 1
         for k in range(1, 8):
             times_gain(k - 1)
-            if 4 <= k + 2 <= last:
-                weigh(k + 2)
+            if k + 3 <= last:
+                weigh(k + 3)
             if k == last:
-                quantize_z0(0, "gain4_then_codes")
+                w3q.extend(halves(*quantize(w3_bf[:], "w3q", "gain4_then_codes")))
             scatter(k)
-        for c in range(2):
-            for i in range(N_TILES):
-                stage2_pass(0, c, i)
 
+        z_words = [bf16_stage(4096, c) for c in range(CHUNKS)]
+        for c in range(CHUNKS):
+            interleave(0, c, z_words[c][:, 0:2048])
         for c in range(CHUNKS):
             cols = slice(c * BANK, (c + 1) * BANK)
             nc.vector.tensor_tensor(z_slot(last)[:, c, :], pages[last % PAGES][:, cols], gains[last][:, cols], MULT)
-            if c == 0:
-                quantize_z0(2, "h7")
-                interleave(1, 0, 1, w3_z[:, 2048:4096])
-                w3q[1], zq[1, 0] = halves(*quantize(w3_z[:], "w3q1_zq10"))
-            else:
-                zi = bf16_stage(2048)
-                interleave(1, c, 1, zi[:])
-                codes, scales = quantize(zi[:], "zq1%d" % c)
-                zq[1, c] = (codes[:], scales[:])
+            interleave(1, c, z_words[c][:, 2048:4096])
+            zq[0, c], zq[1, c] = halves(*quantize(z_words[c][:], "zq%d" % c))
             for i in range(N_TILES):
-                if c >= 2:
-                    stage2_pass(0, c, i)
+                stage2_pass(0, c, i)
                 stage2_pass(1, c, i)
                 res = ambs[c][:, i, :]
                 nc.vector.tensor_tensor(res, y_acc[c, i][:], res, ADD)

@@ -36,7 +36,7 @@ def tile_list_transformer_overload_board_kernel(
     nc = tc.nc
     with ExitStack() as ctx:
         keep = ctx.enter_context(tc.tile_pool(name="keep", bufs=1))
-        stage = ctx.enter_context(tc.tile_pool(name="stage", bufs=7))
+        stage = ctx.enter_context(tc.tile_pool(name="stage", bufs=8))
         ring = ctx.enter_context(tc.tile_pool(name="ring", bufs=2))
         psum = ctx.enter_context(tc.psum_pool(name="psum", bufs=1))
 
@@ -89,11 +89,7 @@ def tile_list_transformer_overload_board_kernel(
         gains = {}
         w3_raw = []
         for k, (b, t) in enumerate(SLICES):
-            if k == 4:
-                gains[k] = keep.tile([P, T2], F32, name="gain_held", tag="gain%d_then_codes" % k, align_bytes=64)
-                nc.sync.dma_start(gains[k][:], gain_rows[b, t])
-            else:
-                gains[k] = load_rows(gain_rows[b, t], F32, "gain%d" % k)
+            gains[k] = load_rows(gain_rows[b, t], F32, "gain%d" % k)
             if k in (0, 1):
                 w3_raw.append(load_k_first(w3[512 * k : 512 * (k + 1), :], "w3_raw%d" % k))
         ambs = []
@@ -102,10 +98,10 @@ def tile_list_transformer_overload_board_kernel(
             nc.sync.dma_start(a_sb[:], amb[:, c * BANK : (c + 1) * BANK].rearrange("(i p) m -> p i m", p=P))
             ambs.append(a_sb)
 
-        def quantize(src_bf16, name, tag=""):
+        def quantize(src_bf16, name, tag="", pool=keep):
             width = src_bf16.shape[1] // PACK
-            codes = keep.tile([P, width], U32, name=name + "_codes", tag=tag, align_bytes=64)
-            scales = keep.tile([P, width], U8, name=name + "_scales", align_bytes=64)
+            codes = pool.tile([P, width], U32, name=name + "_codes", tag=tag, align_bytes=64)
+            scales = pool.tile([P, width], U8, name=name + "_scales", align_bytes=64)
             nc.vector.quantize_mx(out=codes[:].bitcast(FP8X4), scales=scales[:], in_=src_bf16)
             return codes, scales
 
@@ -164,7 +160,7 @@ def tile_list_transformer_overload_board_kernel(
             h = keep.tile([P, S], F32, name="h", tag="h%d" % k, align_bytes=64)
             col = b * 512 + t * P
             for jh in range(HALVES):
-                acc = psum.tile([P, BANK], F32, name="e_acc", tag="bank%d" % ((2 * k + jh) % BANKS))
+                acc = psum.tile([P, BANK], F32, name="e_acc", tag="bank%d" % (jh if k == 0 else 2 + (2 * k + jh) % 3))
                 nc.tensor.matmul_mx(
                     out=acc[:],
                     lhsT=w1q[b][0][:, t * P : (t + 1) * P].bitcast(FP8X4),
@@ -243,7 +239,7 @@ def tile_list_transformer_overload_board_kernel(
         scatter(0)
         for k in range(1, 4):
             weigh(k)
-        w3_bf = bf16_stage(4096, 3)
+        w3_bf = bf16_stage(4096, 4)
         for b in range(2):
             cast_w3(b, w3_bf[:, b * 2048 : (b + 1) * 2048])
         last = len(SLICES) - 1
@@ -251,8 +247,6 @@ def tile_list_transformer_overload_board_kernel(
             times_gain(k - 1)
             if k + 3 <= last:
                 weigh(k + 3)
-            if k == last:
-                w3q.extend(halves(*quantize(w3_bf[:], "w3q", "gain4_then_codes")))
             scatter(k)
 
         z_words = [bf16_stage(4096, c) for c in range(CHUNKS)]
@@ -261,8 +255,10 @@ def tile_list_transformer_overload_board_kernel(
         for c in range(CHUNKS):
             cols = slice(c * BANK, (c + 1) * BANK)
             nc.vector.tensor_tensor(z_slot(last)[:, c, :], pages[last % PAGES][:, cols], gains[last][:, cols], MULT)
+            if c == 0:
+                w3q.extend(halves(*quantize(w3_bf[:], "w3q", "h7")))
             interleave(1, c, z_words[c][:, 2048:4096])
-            zq[0, c], zq[1, c] = halves(*quantize(z_words[c][:], "zq%d" % c))
+            zq[0, c], zq[1, c] = halves(*quantize(z_words[c][:], "zq", pool=ring))
             for i in range(N_TILES):
                 stage2_pass(0, c, i)
                 stage2_pass(1, c, i)

@@ -25,9 +25,9 @@ BANKS = 8
 HALVES = S // BANK
 CHUNKS = T2 // BANK
 N_TILES = N // P
-PAGES = 3
+SLICES = 8
 SCALE_ROW = (4, 0)
-SLICES = [(0, 0), (0, 1), (0, 2), (0, 3), (1, 2), (1, 0), (1, 1), (1, 3)]
+PAGE_OF = (0, 1, 2, 0, 1, 2, 0, 2)
 
 
 def tile_list_transformer_overload_board_kernel(
@@ -36,8 +36,9 @@ def tile_list_transformer_overload_board_kernel(
     nc = tc.nc
     with ExitStack() as ctx:
         keep = ctx.enter_context(tc.tile_pool(name="keep", bufs=1))
-        stage = ctx.enter_context(tc.tile_pool(name="stage", bufs=8))
+        stage = ctx.enter_context(tc.tile_pool(name="stage", bufs=6))
         ring = ctx.enter_context(tc.tile_pool(name="ring", bufs=2))
+        arena = ctx.enter_context(tc.tile_pool(name="arena", bufs=1))
         psum = ctx.enter_context(tc.psum_pool(name="psum", bufs=1))
 
         def load_rows(src, dtype, name):
@@ -54,44 +55,54 @@ def tile_list_transformer_overload_board_kernel(
         w2_s_raw = keep.tile([P, H], U8, name="w2_s_raw", align_bytes=64)
         nc.gpsimd.memset(tab_s[:].bitcast(I32), 0)
         nc.gpsimd.memset(w2_s_raw[:].bitcast(I32), 0)
+        pages = [keep.tile([P, T2], F32, name="page%d" % i) for i in range(3)]
+        nc.vector.memset(pages[0][:], 0.0)
+        for page in pages[1:]:
+            nc.gpsimd.memset(page[:], 0.0)
 
-        idx = keep.tile([P, S // 16], U16, name="idx")
-        nc.sync.dma_start(idx[:], offs)
-        tab0 = load_rows(tab_words[0].rearrange("p t i -> p (t i)").bitcast(I32), I32, "tab0")
-        for a in range(2):
+        def load_tab_scales(a):
             for q in range(4):
                 row = 32 * q + SCALE_ROW[a]
                 nc.sync.dma_start(
                     tab_s[row : row + 4, :].bitcast(I32),
                     tab_scales[a, 4 * q : 4 * q + 4, :].bitcast(I32),
                 )
-        w1_raw = [load_k_first(w1[:, 0:512], "w1_raw0")]
-        w2_raw = keep.tile([P, 2 * H], U8, name="w2_raw")
-        nc.sync.dma_start(w2_raw[:].bitcast(I32), w2_words[0].bitcast(I32))
-        for q in range(4):
+
+        def load_w2_scales(q):
             nc.sync.dma_start(
                 w2_s_raw[32 * q : 32 * q + 4, :].bitcast(I32),
                 w2_scales[0, 4 * q : 4 * q + 4, :].bitcast(I32),
             )
+
+        idx = keep.tile([P, S // 16], U16, name="idx")
+        nc.sync.dma_start(idx[:], offs)
+        w2_raw = keep.tile([P, 2 * H], U8, name="w2_raw")
+        nc.sync.dma_start(w2_raw[:].bitcast(I32), w2_words[0].bitcast(I32))
+        load_tab_scales(0)
+        tab0 = load_rows(tab_words[0].rearrange("p t i -> p (t i)").bitcast(I32), I32, "tab0")
+        load_tab_scales(1)
+        load_w2_scales(0)
+        load_w2_scales(1)
+        w1_raw = [load_k_first(w1[:, 0:512], "w1_raw0")]
+        load_w2_scales(2)
+        load_w2_scales(3)
         tab1 = load_rows(tab_words[1].rearrange("p t i -> p (t i)").bitcast(I32), I32, "tab1")
         tabs = [tab0, tab1]
-        w1_raw.append(load_k_first(w1[:, 512:1024], "w1_raw1"))
         wgs_sb = keep.tile([P, S], F32, name="wgs_sb")
         nc.sync.dma_start(wgs_sb[:], wgs)
         idx2 = keep.tile([P, S // 16], U16, name="idx2")
         nc.sync.dma_start(idx2[:], offs2)
-
-        pages = [keep.tile([P, T2], F32, name="page%d" % i) for i in range(PAGES)]
-        for page in pages:
-            nc.gpsimd.memset(page[:], 0.0)
+        w1_raw1 = arena.tile([P, PACK, 512], F32, name="w1_raw1", align_bytes=64, offset=0)
+        nc.sync.dma_start(w1_raw1[:], w1[:, 512:1024].rearrange("(p j) c -> p j c", j=PACK))
+        w1_raw.append(w1_raw1)
 
         gain_rows = gain.rearrange("(b p j) m -> b j p m", b=2, j=PACK)
         gains = {}
         w3_raw = []
-        for k, (b, t) in enumerate(SLICES):
-            gains[k] = load_rows(gain_rows[b, t], F32, "gain%d" % k)
-            if k in (0, 1):
-                w3_raw.append(load_k_first(w3[512 * k : 512 * (k + 1), :], "w3_raw%d" % k))
+        for k in range(SLICES):
+            gains[k] = load_rows(gain_rows[k // PACK, k % PACK], F32, "gain%d" % k)
+            if k in (1, 2):
+                w3_raw.append(load_k_first(w3[512 * (k - 1) : 512 * k, :], "w3_raw%d" % k))
         ambs = []
         for c in range(CHUNKS):
             a_sb = stage.tile([P, N_TILES, BANK], F32, name="amb%d" % c, tag="rows")
@@ -105,10 +116,10 @@ def tile_list_transformer_overload_board_kernel(
             nc.vector.quantize_mx(out=codes[:].bitcast(FP8X4), scales=scales[:], in_=src_bf16)
             return codes, scales
 
-        def cast_w1(b, dst, copy):
-            copy(
-                dst.rearrange("p (t m j) -> p m j t", t=PACK, j=PACK),
-                w1_raw[b][:].rearrange("p j (m t) -> p m j t", t=PACK),
+        def cast_w1(b, dst, ms=slice(0, P)):
+            nc.scalar.copy(
+                dst.rearrange("p (t m j) -> p m j t", t=PACK, j=PACK)[:, ms],
+                w1_raw[b][:].rearrange("p j (m t) -> p m j t", t=PACK)[:, ms],
             )
 
         def cast_w3(b, dst):
@@ -120,53 +131,46 @@ def tile_list_transformer_overload_board_kernel(
         def halves(codes, scales):
             return [(codes[:, c * BANK : (c + 1) * BANK], scales[:, c * BANK : (c + 1) * BANK]) for c in range(2)]
 
-        g_words = {}
-        g_scales = {}
-
-        def gather_words(a, jh, tag):
-            wd = keep.tile([P, BANK], U32, name="g_words", tag=tag, align_bytes=64)
-            nc.vector.tensor_copy(wd[:], tabs[a][:].bitcast(U32).indirect(idx[:, jh * 32 : (jh + 1) * 32]))
-            g_words[a, jh] = wd
-
-        def gather_scales(jh):
-            sc = keep.tile([P, BANK], U8, name="g_scales%d" % jh, align_bytes=64)
-            nc.vector.tensor_copy(sc[:], tab_s[:].indirect(idx[:, jh * 32 : (jh + 1) * 32]))
-            g_scales[jh] = sc
-
-        w1_bf0 = keep.tile([P, 2048], BF16, name="w1_bf0", tag="w1_then_words", align_bytes=64)
-        cast_w1(0, w1_bf0[:], nc.scalar.copy)
-        gather_words(0, 0, "words00")
-        gather_scales(0)
+        words0 = keep.tile([P, S], U32, name="words0", align_bytes=64)
+        g_scales = keep.tile([P, S], U8, name="g_scales", align_bytes=64)
+        words1 = [keep.tile([P, BANK], U32, name="words1%d" % jh, align_bytes=64) for jh in range(HALVES)]
         w2_p = keep.tile([P, 2 * H], U8, name="w2_p", align_bytes=64)
         w2_s = keep.tile([P, H], U8, name="w2_s", align_bytes=64)
-        w1q = [quantize(w1_bf0[:], "w1q0")]
-        gather_words(1, 0, "words10")
+
+        w1_bf0 = keep.tile([P, 2048], BF16, name="w1_bf0", tag="h7", align_bytes=64)
+        cast_w1(0, w1_bf0[:])
         nc.vector.tensor_copy(
             w2_p[:].bitcast(U16).rearrange("p (b t m) -> p b t m", b=2, t=PACK),
             w2_raw[:].bitcast(U16).rearrange("p (b m t) -> p b t m", b=2, t=PACK),
         )
+        nc.vector.tensor_copy(words0[:], tabs[0][:].bitcast(U32).indirect(idx[:]))
+        nc.vector.tensor_copy(g_scales[:], tab_s[:].indirect(idx[:]))
         nc.vector.tensor_copy(
             w2_s[:].rearrange("p (b t m) -> p b t m", b=2, t=PACK),
             w2_s_raw[:].rearrange("p (b m t) -> p b t m", b=2, t=PACK),
         )
-        gather_words(0, 1, "words01")
-        gather_scales(1)
-        gather_words(1, 1, "w1_then_words")
+        w1q = [quantize(w1_bf0[:], "w1q0")]
+        for jh in range(HALVES):
+            nc.vector.tensor_copy(words1[jh][:], tabs[1][:].bitcast(U32).indirect(idx[:, jh * 32 : (jh + 1) * 32]))
 
         hs = {}
+        raw = {}
 
-        def stage1(k):
-            b, t = SLICES[k]
-            h = keep.tile([P, S], F32, name="h", tag="h%d" % k, align_bytes=64)
+        def stage1(k, jhs=(0, 1)):
+            b, t = divmod(k, PACK)
+            if k not in hs:
+                hs[k] = keep.tile([P, S], F32, name="h", tag="h%d" % k, align_bytes=64)
+            h = hs[k]
             col = b * 512 + t * P
-            for jh in range(HALVES):
-                acc = psum.tile([P, BANK], F32, name="e_acc", tag="bank%d" % (jh if k == 0 else 2 + (2 * k + jh) % 3))
+            for jh in jhs:
+                js = slice(jh * BANK, (jh + 1) * BANK)
+                acc = psum.tile([P, BANK], F32, name="e_acc", tag="bank%d" % ((2 * k + jh) % BANKS))
                 nc.tensor.matmul_mx(
                     out=acc[:],
                     lhsT=w1q[b][0][:, t * P : (t + 1) * P].bitcast(FP8X4),
                     lhsT_scale=w1q[b][1][:, t * P : (t + 1) * P],
-                    rhs=g_words[0, jh][:].bitcast(FP8X4),
-                    rhs_scale=g_scales[jh][SCALE_ROW[0] : P, :],
+                    rhs=words0[:, js].bitcast(FP8X4),
+                    rhs_scale=g_scales[SCALE_ROW[0] : P, js],
                     start=True,
                     stop=False,
                 )
@@ -174,46 +178,31 @@ def tile_list_transformer_overload_board_kernel(
                     out=acc[:],
                     lhsT=w2_p[:, 2 * col : 2 * (col + P)].bitcast(FP4X4),
                     lhsT_scale=w2_s[:, col : col + P],
-                    rhs=g_words[1, jh][:].bitcast(FP8X4),
-                    rhs_scale=g_scales[jh][SCALE_ROW[1] : P, :],
+                    rhs=words1[jh][:].bitcast(FP8X4),
+                    rhs_scale=g_scales[SCALE_ROW[1] : P, js],
                     start=False,
                     stop=True,
                 )
-                nc.scalar.activation(h[:, jh * BANK : (jh + 1) * BANK], acc[:], GELU)
-            hs[k] = h
+                raw.setdefault((k, jh), h[:, js])
+                nc.scalar.activation(raw[k, jh], acc[:], GELU)
 
         def weigh(k):
             nc.gpsimd.tensor_tensor(hs[k][:], hs[k][:], wgs_sb[:], MULT)
 
-        def scatter(k):
-            nc.vector.tensor_copy(pages[k % PAGES][:].indirect(idx2[:]), hs[k][:])
+        def weigh_half(k, jh):
+            js = slice(jh * BANK, (jh + 1) * BANK)
+            nc.gpsimd.tensor_tensor(hs[k][:, js], raw[k, jh], wgs_sb[:, js], MULT)
 
-        z_pairs = [ring.tile([P, 4 * T2], BF16, name="z_pairs%d" % b, tag="z_pairs") for b in range(2)]
+        def scatter(k, js=slice(0, S)):
+            offsets = idx2[:, js.start // 16 : js.stop // 16]
+            nc.vector.tensor_copy(pages[PAGE_OF[k]][:].indirect(offsets), hs[k][:, js])
 
-        def z_slot(k):
-            b, t = SLICES[k]
-            v = z_pairs[b][:].rearrange("p (c u m e) -> p c u m e", c=CHUNKS, u=2, e=2)
-            return v[:, :, t // 2, :, t % 2]
+        z_plane = {}
 
-        def times_gain(k):
-            nc.gpsimd.tensor_tensor(
-                z_slot(k),
-                pages[k % PAGES][:].rearrange("p (c m) -> p c m", c=CHUNKS),
-                gains[k][:].rearrange("p (c m) -> p c m", c=CHUNKS),
-                MULT,
-            )
+        def times_gain(k, cols=slice(0, T2)):
+            nc.gpsimd.tensor_tensor(z_plane[k][:, cols], pages[PAGE_OF[k]][:, cols], gains[k][:, cols], MULT)
 
         zq = {}
-
-        def interleave(b, c, dst):
-            nc.scalar.copy(
-                dst.bitcast(F32).rearrange("p (m u) -> p m u", u=2),
-                z_pairs[b][:, c * 2048 : (c + 1) * 2048].bitcast(F32).rearrange("p (u m) -> p m u", u=2),
-            )
-
-        def bf16_stage(width, slot):
-            return keep.tile([P, width], BF16, name="bf16_stage", tag="bf16_stage%d" % slot, align_bytes=64)
-
         w3q = []
         y_acc = {}
 
@@ -230,37 +219,93 @@ def tile_list_transformer_overload_board_kernel(
                 stop=(b == 1),
             )
 
-        w1_bf1 = keep.tile([P, 2048], BF16, name="w1_bf1", tag="h1", align_bytes=64)
-        cast_w1(1, w1_bf1[:], nc.vector.tensor_copy)
+        stage1(0)
+        stage1(1, (0,))
+        stage1(2, (0,))
+        w1_bf1 = arena.tile([P, 2048], BF16, name="w1_bf1", align_bytes=64, offset=8192)
+        cast_w1(1, w1_bf1[:])
+        late = arena.tile([P, 2, BANK], F32, name="late", align_bytes=64, offset=4096)
+        for k in (1, 2):
+            raw[k, 1] = late[:, k - 1, :]
+            stage1(k, (1,))
+        stage1(3)
+        for jh in range(HALVES):
+            weigh_half(0, jh)
+            scatter(0, slice(jh * BANK, (jh + 1) * BANK))
         w1q.append(quantize(w1_bf1[:], "w1q1"))
-        for k in range(8):
+        for k in range(4, SLICES):
             stage1(k)
-        nc.vector.tensor_tensor(hs[0][:], hs[0][:], wgs_sb[:], MULT)
-        scatter(0)
-        for k in range(1, 4):
-            weigh(k)
-        w3_bf = bf16_stage(4096, 4)
+        w3_bf = keep.tile([P, 4096], BF16, name="w3_bf", tag="w3_bf", align_bytes=64)
         for b in range(2):
             cast_w3(b, w3_bf[:, b * 2048 : (b + 1) * 2048])
-        last = len(SLICES) - 1
-        for k in range(1, 8):
-            times_gain(k - 1)
-            if k + 3 <= last:
-                weigh(k + 3)
-            scatter(k)
 
-        z_words = [bf16_stage(4096, c) for c in range(CHUNKS)]
-        for c in range(CHUNKS):
-            interleave(0, c, z_words[c][:, 0:2048])
+        planes = [arena.tile([P, 2, T2], BF16, name="planes0", align_bytes=64, offset=4096)]
+        planes.extend(keep.tile([P, 2, T2], BF16, name="planes", tag="planes%d" % u, align_bytes=64) for u in (1, 2))
+        for k in range(6):
+            z_plane[k] = planes[k // 2][:, k % 2, :]
+
+        def weave_pair(dst_words, u, pair, cols):
+            nc.scalar.copy(
+                dst_words.rearrange("p (m t) -> p m t", t=PACK)[:, :, 2 * u : 2 * u + 2],
+                pair[:, :, cols].rearrange("p t m -> p m t"),
+            )
+
+        weigh_half(1, 0)
+        weigh_half(2, 0)
+        weigh_half(1, 1)
+        weigh_half(2, 1)
+        weigh_half(3, 0)
+        weigh_half(3, 1)
+        z0_words = [keep.tile([P, 4096], BF16, name="z0_words", tag="z0_words%d" % u, align_bytes=64) for u in range(2)]
+        board_halves = [slice(half * 1024, (half + 1) * 1024) for half in range(2)]
+        for k in range(1, 4):
+            scatter(k)
+            times_gain(k - 1)
+            weigh(k + 3)
+        for half in range(2):
+            weave_pair(z0_words[half][:], 0, planes[0], board_halves[half])
+        scatter(4)
+        for half in range(2):
+            times_gain(3, board_halves[half])
+            weave_pair(z0_words[half][:], 1, planes[1], board_halves[half])
+        scatter(5)
+        times_gain(4)
+        h7_weighed = keep.tile([P, S], F32, name="h7_weighed", tag="planes1", align_bytes=64)
+        nc.gpsimd.tensor_tensor(h7_weighed[:], hs[7][:], wgs_sb[:], MULT)
+        hs[7] = h7_weighed
+        scatter(6)
+        times_gain(5)
+        w3q.extend(halves(*quantize(w3_bf[:], "w3q", "h6")))
+        z0_codes = keep.tile([P, T2], U32, name="z0_codes", tag="w3_bf", align_bytes=64)
+        z0_scales = keep.tile([P, T2], U8, name="z0_scales", align_bytes=64)
+        for u in range(2):
+            cols = slice(u * 1024, (u + 1) * 1024)
+            nc.vector.quantize_mx(out=z0_codes[:, cols].bitcast(FP8X4), scales=z0_scales[:, cols], in_=z0_words[u][:])
         for c in range(CHUNKS):
             cols = slice(c * BANK, (c + 1) * BANK)
-            nc.vector.tensor_tensor(z_slot(last)[:, c, :], pages[last % PAGES][:, cols], gains[last][:, cols], MULT)
-            if c == 0:
-                w3q.extend(halves(*quantize(w3_bf[:], "w3q", "h7")))
-            interleave(1, c, z_words[c][:, 2048:4096])
-            zq[0, c], zq[1, c] = halves(*quantize(z_words[c][:], "zq", pool=ring))
+            zq[0, c] = (z0_codes[:, cols], z0_scales[:, cols])
+        scatter(7)
+        planes1b = keep.tile([P, 2, T2], BF16, name="planes1b", tag="z0_words1", align_bytes=64)
+        z_plane[6] = planes1b[:, 0, :]
+        times_gain(6)
+        for c in range(2):
             for i in range(N_TILES):
                 stage2_pass(0, c, i)
+
+        z1_words = [keep.tile([P, 2048], BF16, name="z1_words", tag="h%d" % c, align_bytes=64) for c in range(CHUNKS)]
+        for c in range(CHUNKS):
+            weave_pair(z1_words[c][:], 0, planes[2], slice(c * BANK, (c + 1) * BANK))
+        for c in range(CHUNKS):
+            cols = slice(c * BANK, (c + 1) * BANK)
+            nc.vector.tensor_tensor(planes1b[:, 1, cols], pages[PAGE_OF[7]][:, cols], gains[7][:, cols], MULT)
+            weave_pair(z1_words[c][:], 1, planes1b, cols)
+        for c in range(CHUNKS):
+            cols = slice(c * BANK, (c + 1) * BANK)
+            codes, scales = quantize(z1_words[c][:], "z1q", pool=ring)
+            zq[1, c] = (codes[:], scales[:])
+            for i in range(N_TILES):
+                if c >= 2:
+                    stage2_pass(0, c, i)
                 stage2_pass(1, c, i)
                 res = ambs[c][:, i, :]
                 nc.vector.tensor_tensor(res, y_acc[c, i][:], res, ADD)

@@ -26,8 +26,10 @@ HALVES = S // BANK
 CHUNKS = T2 // BANK
 N_TILES = N // P
 SLICES = 8
+GPSIMD_CHUNKS = 2
 SCALE_ROW = (4, 0)
-PAGE_OF = (0, 1, 2, 0, 1, 2, 0, 2)
+SLICE_ROWS = [(0, 0), (0, 1), (0, 2), (0, 3), (1, 2), (1, 0), (1, 1), (1, 3)]
+PAGE_OF = (0, 1, 2, 0, 1, 2, 0, 1)
 
 
 def tile_list_transformer_overload_board_kernel(
@@ -60,13 +62,13 @@ def tile_list_transformer_overload_board_kernel(
         for page in pages[1:]:
             nc.gpsimd.memset(page[:], 0.0)
 
-        def load_tab_scales(a):
-            for q in range(4):
-                row = 32 * q + SCALE_ROW[a]
-                nc.sync.dma_start(
-                    tab_s[row : row + 4, :].bitcast(I32),
-                    tab_scales[a, 4 * q : 4 * q + 4, :].bitcast(I32),
-                )
+        def load_tab_scales(run):
+            a, q = divmod(run, 4)
+            row = 32 * q + SCALE_ROW[a]
+            nc.sync.dma_start(
+                tab_s[row : row + 4, :].bitcast(I32),
+                tab_scales[a, 4 * q : 4 * q + 4, :].bitcast(I32),
+            )
 
         def load_w2_scales(q):
             nc.sync.dma_start(
@@ -78,14 +80,14 @@ def tile_list_transformer_overload_board_kernel(
         nc.sync.dma_start(idx[:], offs)
         w2_raw = keep.tile([P, 2 * H], U8, name="w2_raw")
         nc.sync.dma_start(w2_raw[:].bitcast(I32), w2_words[0].bitcast(I32))
-        load_tab_scales(0)
+        for run in range(2):
+            load_tab_scales(run)
         tab0 = load_rows(tab_words[0].rearrange("p t i -> p (t i)").bitcast(I32), I32, "tab0")
-        load_tab_scales(1)
-        load_w2_scales(0)
-        load_w2_scales(1)
+        for run in range(2, 8):
+            load_tab_scales(run)
         w1_raw = [load_k_first(w1[:, 0:512], "w1_raw0")]
-        load_w2_scales(2)
-        load_w2_scales(3)
+        for q in range(4):
+            load_w2_scales(q)
         tab1 = load_rows(tab_words[1].rearrange("p t i -> p (t i)").bitcast(I32), I32, "tab1")
         tabs = [tab0, tab1]
         wgs_sb = keep.tile([P, S], F32, name="wgs_sb")
@@ -100,9 +102,9 @@ def tile_list_transformer_overload_board_kernel(
         gains = {}
         w3_raw = []
         for k in range(SLICES):
-            gains[k] = load_rows(gain_rows[k // PACK, k % PACK], F32, "gain%d" % k)
-            if k in (1, 2):
-                w3_raw.append(load_k_first(w3[512 * (k - 1) : 512 * k, :], "w3_raw%d" % k))
+            gains[k] = load_rows(gain_rows[SLICE_ROWS[k][0], SLICE_ROWS[k][1]], F32, "gain%d" % k)
+            if k == 5:
+                w3_raw.extend(load_k_first(w3[512 * b : 512 * (b + 1), :], "w3_raw%d" % b) for b in range(2))
         ambs = []
         for c in range(CHUNKS):
             a_sb = stage.tile([P, N_TILES, BANK], F32, name="amb%d" % c, tag="rows")
@@ -116,10 +118,10 @@ def tile_list_transformer_overload_board_kernel(
             nc.vector.quantize_mx(out=codes[:].bitcast(FP8X4), scales=scales[:], in_=src_bf16)
             return codes, scales
 
-        def cast_w1(b, dst, ms=slice(0, P)):
+        def cast_w1(b, dst, ts):
             nc.scalar.copy(
-                dst.rearrange("p (t m j) -> p m j t", t=PACK, j=PACK)[:, ms],
-                w1_raw[b][:].rearrange("p j (m t) -> p m j t", t=PACK)[:, ms],
+                dst.rearrange("p (t m j) -> p m j t", m=P, j=PACK),
+                w1_raw[b][:].rearrange("p j (m t) -> p m j t", t=PACK)[:, :, :, ts],
             )
 
         def cast_w3(b, dst):
@@ -133,12 +135,12 @@ def tile_list_transformer_overload_board_kernel(
 
         words0 = keep.tile([P, S], U32, name="words0", align_bytes=64)
         g_scales = keep.tile([P, S], U8, name="g_scales", align_bytes=64)
-        words1 = [keep.tile([P, BANK], U32, name="words1%d" % jh, align_bytes=64) for jh in range(HALVES)]
         w2_p = keep.tile([P, 2 * H], U8, name="w2_p", align_bytes=64)
         w2_s = keep.tile([P, H], U8, name="w2_s", align_bytes=64)
 
-        w1_bf0 = keep.tile([P, 2048], BF16, name="w1_bf0", tag="h7", align_bytes=64)
-        cast_w1(0, w1_bf0[:])
+        w1_bf0 = [keep.tile([P, 1024], BF16, name="w1_bf0", tag="w1_then_words%d" % u, align_bytes=64) for u in range(2)]
+        for u in range(2):
+            cast_w1(0, w1_bf0[u][:], slice(2 * u, 2 * u + 2))
         nc.vector.tensor_copy(
             w2_p[:].bitcast(U16).rearrange("p (b t m) -> p b t m", b=2, t=PACK),
             w2_raw[:].bitcast(U16).rearrange("p (b m t) -> p b t m", b=2, t=PACK),
@@ -149,15 +151,24 @@ def tile_list_transformer_overload_board_kernel(
             w2_s[:].rearrange("p (b t m) -> p b t m", b=2, t=PACK),
             w2_s_raw[:].rearrange("p (b m t) -> p b t m", b=2, t=PACK),
         )
-        w1q = [quantize(w1_bf0[:], "w1q0")]
+        w1_codes = keep.tile([P, H], U32, name="w1_codes", align_bytes=64)
+        w1_scales = keep.tile([P, H], U8, name="w1_scales", align_bytes=64)
+
+        def quantize_w1(src, col):
+            cols = slice(col, col + src.shape[1] // PACK)
+            nc.vector.quantize_mx(out=w1_codes[:, cols].bitcast(FP8X4), scales=w1_scales[:, cols], in_=src)
+
+        words1 = []
         for jh in range(HALVES):
+            quantize_w1(w1_bf0[jh][:], 256 * jh)
+            words1.append(keep.tile([P, BANK], U32, name="words1", tag="w1_then_words%d" % jh, align_bytes=64))
             nc.vector.tensor_copy(words1[jh][:], tabs[1][:].bitcast(U32).indirect(idx[:, jh * 32 : (jh + 1) * 32]))
 
         hs = {}
         raw = {}
 
         def stage1(k, jhs=(0, 1)):
-            b, t = divmod(k, PACK)
+            b, t = SLICE_ROWS[k]
             if k not in hs:
                 hs[k] = keep.tile([P, S], F32, name="h", tag="h%d" % k, align_bytes=64)
             h = hs[k]
@@ -167,8 +178,8 @@ def tile_list_transformer_overload_board_kernel(
                 acc = psum.tile([P, BANK], F32, name="e_acc", tag="bank%d" % ((2 * k + jh) % BANKS))
                 nc.tensor.matmul_mx(
                     out=acc[:],
-                    lhsT=w1q[b][0][:, t * P : (t + 1) * P].bitcast(FP8X4),
-                    lhsT_scale=w1q[b][1][:, t * P : (t + 1) * P],
+                    lhsT=w1_codes[:, col : col + P].bitcast(FP8X4),
+                    lhsT_scale=w1_scales[:, col : col + P],
                     rhs=words0[:, js].bitcast(FP8X4),
                     rhs_scale=g_scales[SCALE_ROW[0] : P, js],
                     start=True,
@@ -189,18 +200,23 @@ def tile_list_transformer_overload_board_kernel(
         def weigh(k):
             nc.gpsimd.tensor_tensor(hs[k][:], hs[k][:], wgs_sb[:], MULT)
 
-        def weigh_half(k, jh):
+        def weigh_half(k, jh, engine):
             js = slice(jh * BANK, (jh + 1) * BANK)
-            nc.gpsimd.tensor_tensor(hs[k][:, js], raw[k, jh], wgs_sb[:, js], MULT)
+            engine.tensor_tensor(hs[k][:, js], raw[k, jh], wgs_sb[:, js], MULT)
 
         def scatter(k, js=slice(0, S)):
             offsets = idx2[:, js.start // 16 : js.stop // 16]
             nc.vector.tensor_copy(pages[PAGE_OF[k]][:].indirect(offsets), hs[k][:, js])
 
-        z_plane = {}
+        z_slot = {}
 
-        def times_gain(k, cols=slice(0, T2)):
-            nc.gpsimd.tensor_tensor(z_plane[k][:, cols], pages[PAGE_OF[k]][:, cols], gains[k][:, cols], MULT)
+        def times_gain(k):
+            nc.gpsimd.tensor_tensor(
+                z_slot[k],
+                pages[PAGE_OF[k]][:].rearrange("p (c m) -> p c m", c=CHUNKS),
+                gains[k][:].rearrange("p (c m) -> p c m", c=CHUNKS),
+                MULT,
+            )
 
         zq = {}
         w3q = []
@@ -220,93 +236,100 @@ def tile_list_transformer_overload_board_kernel(
             )
 
         stage1(0)
-        stage1(1, (0,))
-        stage1(2, (0,))
+        for k in (1, 2, 3):
+            stage1(k, (0,))
         w1_bf1 = arena.tile([P, 2048], BF16, name="w1_bf1", align_bytes=64, offset=8192)
-        cast_w1(1, w1_bf1[:])
-        late = arena.tile([P, 2, BANK], F32, name="late", align_bytes=64, offset=4096)
-        for k in (1, 2):
+        cast_w1(1, w1_bf1[:], slice(0, PACK))
+        late = arena.tile([P, 3, BANK], F32, name="late", align_bytes=64, offset=2048)
+        for k in (1, 2, 3):
             raw[k, 1] = late[:, k - 1, :]
             stage1(k, (1,))
-        stage1(3)
-        for jh in range(HALVES):
-            weigh_half(0, jh)
-            scatter(0, slice(jh * BANK, (jh + 1) * BANK))
-        w1q.append(quantize(w1_bf1[:], "w1q1"))
+        weigh_half(0, 0, nc.vector)
+        scatter(0, slice(0, BANK))
+        weigh_half(0, 1, nc.gpsimd)
+        scatter(0, slice(BANK, S))
+        for k in (1, 2, 3):
+            weigh_half(k, 0, nc.gpsimd)
+        quantize_w1(w1_bf1[:], 512)
+        for k in (1, 2, 3):
+            weigh_half(k, 1, nc.vector)
         for k in range(4, SLICES):
             stage1(k)
         w3_bf = keep.tile([P, 4096], BF16, name="w3_bf", tag="w3_bf", align_bytes=64)
         for b in range(2):
             cast_w3(b, w3_bf[:, b * 2048 : (b + 1) * 2048])
 
-        planes = [arena.tile([P, 2, T2], BF16, name="planes0", align_bytes=64, offset=4096)]
-        planes.extend(keep.tile([P, 2, T2], BF16, name="planes", tag="planes%d" % u, align_bytes=64) for u in (1, 2))
-        for k in range(6):
-            z_plane[k] = planes[k // 2][:, k % 2, :]
+        z_pairs = [
+            arena.tile([P, 4 * T2], BF16, name="z_pairs0", align_bytes=64, offset=4096),
+            keep.tile([P, 4 * T2], BF16, name="z_pairs1", align_bytes=64),
+        ]
+        for k, (b, t) in enumerate(SLICE_ROWS):
+            z_slot[k] = z_pairs[b][:].rearrange("p (c u m e) -> p c u m e", c=CHUNKS, u=2, e=2)[:, :, t // 2, :, t % 2]
+        z_words = [keep.tile([P, 2, 2048], BF16, name="z_words", tag="z_words%d" % c, align_bytes=64) for c in range(CHUNKS)]
 
-        def weave_pair(dst_words, u, pair, cols):
+        def weave(b, c):
             nc.scalar.copy(
-                dst_words.rearrange("p (m t) -> p m t", t=PACK)[:, :, 2 * u : 2 * u + 2],
-                pair[:, :, cols].rearrange("p t m -> p m t"),
+                z_words[c][:, b, :].bitcast(F32).rearrange("p (m u) -> p m u", u=2),
+                z_pairs[b][:, c * 2048 : (c + 1) * 2048].bitcast(F32).rearrange("p (u m) -> p m u", u=2),
             )
 
-        weigh_half(1, 0)
-        weigh_half(2, 0)
-        weigh_half(1, 1)
-        weigh_half(2, 1)
-        weigh_half(3, 0)
-        weigh_half(3, 1)
-        z0_words = [keep.tile([P, 4096], BF16, name="z0_words", tag="z0_words%d" % u, align_bytes=64) for u in range(2)]
-        board_halves = [slice(half * 1024, (half + 1) * 1024) for half in range(2)]
-        for k in range(1, 4):
+        for k in range(1, SLICES):
             scatter(k)
             times_gain(k - 1)
-            weigh(k + 3)
-        for half in range(2):
-            weave_pair(z0_words[half][:], 0, planes[0], board_halves[half])
-        scatter(4)
-        for half in range(2):
-            times_gain(3, board_halves[half])
-            weave_pair(z0_words[half][:], 1, planes[1], board_halves[half])
-        scatter(5)
-        times_gain(4)
-        h7_weighed = keep.tile([P, S], F32, name="h7_weighed", tag="planes1", align_bytes=64)
-        nc.gpsimd.tensor_tensor(h7_weighed[:], hs[7][:], wgs_sb[:], MULT)
-        hs[7] = h7_weighed
-        scatter(6)
-        times_gain(5)
-        w3q.extend(halves(*quantize(w3_bf[:], "w3q", "h6")))
-        z0_codes = keep.tile([P, T2], U32, name="z0_codes", tag="w3_bf", align_bytes=64)
-        z0_scales = keep.tile([P, T2], U8, name="z0_scales", align_bytes=64)
-        for u in range(2):
-            cols = slice(u * 1024, (u + 1) * 1024)
-            nc.vector.quantize_mx(out=z0_codes[:, cols].bitcast(FP8X4), scales=z0_scales[:, cols], in_=z0_words[u][:])
-        for c in range(CHUNKS):
+            if k + 3 < SLICES:
+                weigh(k + 3)
+            if k == 4:
+                for c in range(CHUNKS):
+                    weave(0, c)
+
+        def last_gain(c):
             cols = slice(c * BANK, (c + 1) * BANK)
-            zq[0, c] = (z0_codes[:, cols], z0_scales[:, cols])
-        scatter(7)
-        planes1b = keep.tile([P, 2, T2], BF16, name="planes1b", tag="z0_words1", align_bytes=64)
-        z_plane[6] = planes1b[:, 0, :]
-        times_gain(6)
-        for c in range(2):
+            nc.vector.tensor_tensor(z_slot[7][:, c, :], pages[PAGE_OF[7]][:, cols], gains[7][:, cols], MULT)
+            weave(1, c)
+
+        def add_and_store(c, i, engine, src, res):
+            engine.tensor_tensor(res, src, ambs[c][:, i, :], ADD)
+            nc.sync.dma_start(out[i * P : (i + 1) * P, c * BANK : (c + 1) * BANK], res)
+
+        def add_on_vector(c, i):
+            add_and_store(c, i, nc.vector, y_acc[c, i][:], ambs[c][:, i, :])
+
+        def products(c):
+            zq[0, c], zq[1, c] = halves(*quantize(z_words[c][:].rearrange("p b w -> p (b w)"), "zq", pool=ring))
             for i in range(N_TILES):
                 stage2_pass(0, c, i)
-
-        z1_words = [keep.tile([P, 2048], BF16, name="z1_words", tag="h%d" % c, align_bytes=64) for c in range(CHUNKS)]
-        for c in range(CHUNKS):
-            weave_pair(z1_words[c][:], 0, planes[2], slice(c * BANK, (c + 1) * BANK))
-        for c in range(CHUNKS):
-            cols = slice(c * BANK, (c + 1) * BANK)
-            nc.vector.tensor_tensor(planes1b[:, 1, cols], pages[PAGE_OF[7]][:, cols], gains[7][:, cols], MULT)
-            weave_pair(z1_words[c][:], 1, planes1b, cols)
-        for c in range(CHUNKS):
-            cols = slice(c * BANK, (c + 1) * BANK)
-            codes, scales = quantize(z1_words[c][:], "z1q", pool=ring)
-            zq[1, c] = (codes[:], scales[:])
-            for i in range(N_TILES):
-                if c >= 2:
-                    stage2_pass(0, c, i)
                 stage2_pass(1, c, i)
-                res = ambs[c][:, i, :]
-                nc.vector.tensor_tensor(res, y_acc[c, i][:], res, ADD)
-                nc.sync.dma_start(out[i * P : (i + 1) * P, cols], res)
+
+        def first_products(b):
+            codes, scales = quantize(z_words[0][:, b, :], "zq_first%d" % b, ("w3_bf", "h5")[b])
+            zq[b, 0] = (codes[:], scales[:])
+            for i in range(N_TILES):
+                stage2_pass(b, 0, i)
+
+        def add_on_gpsimd(c, tag):
+            y_sb = keep.tile([P, BANK], F32, name="y_sb", tag="h%d" % c, align_bytes=64)
+            nc.scalar.copy(y_sb[:], y_acc[c, N_TILES - 1][:])
+            res = keep.tile([P, BANK], F32, name="res", tag=tag, align_bytes=64)
+            add_and_store(c, N_TILES - 1, nc.gpsimd, y_sb[:], res[:])
+
+        last_gain(0)
+        w3q.extend(halves(*quantize(w3_bf[:], "w3q", "h7")))
+        first_products(0)
+        last_gain(1)
+        first_products(1)
+        last_gain(2)
+        held_back = None
+        for c in range(CHUNKS):
+            banks = list(range(N_TILES - 1 if c < GPSIMD_CHUNKS else N_TILES))
+            if 0 < c < CHUNKS - 1:
+                held_back = banks.pop()
+            for i in banks:
+                add_on_vector(c, i)
+            if c + 1 < CHUNKS:
+                products(c + 1)
+            if c == 0:
+                last_gain(3)
+            elif c + 1 < CHUNKS:
+                add_on_vector(c, held_back)
+            if c < GPSIMD_CHUNKS:
+                add_on_gpsimd(c, "z_words%d" % (c + 1))

@@ -58,8 +58,7 @@ def tile_list_transformer_overload_board_kernel(
         nc.gpsimd.memset(tab_s[:].bitcast(I32), 0)
         nc.gpsimd.memset(w2_s_raw[:].bitcast(I32), 0)
         pages = [keep.tile([P, T2], F32, name="page%d" % i) for i in range(3)]
-        nc.vector.memset(pages[0][:], 0.0)
-        for page in pages[1:]:
+        for page in pages:
             nc.gpsimd.memset(page[:], 0.0)
 
         def load_tab_scales(run):
@@ -78,14 +77,12 @@ def tile_list_transformer_overload_board_kernel(
 
         idx = keep.tile([P, S // 16], U16, name="idx")
         nc.sync.dma_start(idx[:], offs)
-        w2_raw = keep.tile([P, 2 * H], U8, name="w2_raw")
-        nc.sync.dma_start(w2_raw[:].bitcast(I32), w2_words[0].bitcast(I32))
-        for run in range(2):
-            load_tab_scales(run)
         tab0 = load_rows(tab_words[0].rearrange("p t i -> p (t i)").bitcast(I32), I32, "tab0")
-        for run in range(2, 8):
+        for run in range(8):
             load_tab_scales(run)
         w1_raw = [load_k_first(w1[:, 0:512], "w1_raw0")]
+        w2_raw = keep.tile([P, 2 * H], U8, name="w2_raw")
+        nc.sync.dma_start(w2_raw[:].bitcast(I32), w2_words[0].bitcast(I32))
         for q in range(4):
             load_w2_scales(q)
         tab1 = load_rows(tab_words[1].rearrange("p t i -> p (t i)").bitcast(I32), I32, "tab1")
@@ -141,12 +138,12 @@ def tile_list_transformer_overload_board_kernel(
         w1_bf0 = [keep.tile([P, 1024], BF16, name="w1_bf0", tag="w1_then_words%d" % u, align_bytes=64) for u in range(2)]
         for u in range(2):
             cast_w1(0, w1_bf0[u][:], slice(2 * u, 2 * u + 2))
+        nc.vector.tensor_copy(words0[:], tabs[0][:].bitcast(U32).indirect(idx[:]))
+        nc.vector.tensor_copy(g_scales[:], tab_s[:].indirect(idx[:]))
         nc.vector.tensor_copy(
             w2_p[:].bitcast(U16).rearrange("p (b t m) -> p b t m", b=2, t=PACK),
             w2_raw[:].bitcast(U16).rearrange("p (b m t) -> p b t m", b=2, t=PACK),
         )
-        nc.vector.tensor_copy(words0[:], tabs[0][:].bitcast(U32).indirect(idx[:]))
-        nc.vector.tensor_copy(g_scales[:], tab_s[:].indirect(idx[:]))
         nc.vector.tensor_copy(
             w2_s[:].rearrange("p (b t m) -> p b t m", b=2, t=PACK),
             w2_s_raw[:].rearrange("p (b m t) -> p b t m", b=2, t=PACK),

@@ -249,7 +249,7 @@ def tile_list_transformer_overload_board_kernel(
             weigh_half(k, 0, nc.gpsimd)
         quantize_w1(w1_bf1[:], 512)
         for k in (1, 2, 3):
-            weigh_half(k, 1, nc.vector)
+            weigh_half(k, 1, nc.gpsimd)
         for k in range(4, SLICES):
             stage1(k)
         w3_bf = keep.tile([P, 4096], BF16, name="w3_bf", tag="w3_bf", align_bytes=64)

@@ -26,7 +26,6 @@ HALVES = S // BANK
 CHUNKS = T2 // BANK
 N_TILES = N // P
 SLICES = 8
-GPSIMD_CHUNKS = 2
 SCALE_ROW = (4, 0)
 SLICE_ROWS = [(0, 0), (0, 1), (0, 2), (0, 3), (1, 2), (1, 0), (1, 1), (1, 3)]
 PAGE_OF = (0, 1, 2, 0, 1, 2, 0, 1)
@@ -39,7 +38,6 @@ def tile_list_transformer_overload_board_kernel(
     with ExitStack() as ctx:
         keep = ctx.enter_context(tc.tile_pool(name="keep", bufs=1))
         stage = ctx.enter_context(tc.tile_pool(name="stage", bufs=6))
-        ring = ctx.enter_context(tc.tile_pool(name="ring", bufs=2))
         arena = ctx.enter_context(tc.tile_pool(name="arena", bufs=1))
         psum = ctx.enter_context(tc.psum_pool(name="psum", bufs=1))
 
@@ -262,11 +260,15 @@ def tile_list_transformer_overload_board_kernel(
         ]
         for k, (b, t) in enumerate(SLICE_ROWS):
             z_slot[k] = z_pairs[b][:].rearrange("p (c u m e) -> p c u m e", c=CHUNKS, u=2, e=2)[:, :, t // 2, :, t % 2]
-        z_words = [keep.tile([P, 2, 2048], BF16, name="z_words", tag="z_words%d" % c, align_bytes=64) for c in range(CHUNKS)]
+        z_words = {
+            (b, c): keep.tile([P, 2048], BF16, name="z_words", tag="z_words%d%d" % (b, c), align_bytes=64)
+            for b in range(2)
+            for c in range(CHUNKS)
+        }
 
         def weave(b, c):
             nc.scalar.copy(
-                z_words[c][:, b, :].bitcast(F32).rearrange("p (m u) -> p m u", u=2),
+                z_words[b, c][:].bitcast(F32).rearrange("p (m u) -> p m u", u=2),
                 z_pairs[b][:, c * 2048 : (c + 1) * 2048].bitcast(F32).rearrange("p (u m) -> p m u", u=2),
             )
 
@@ -284,49 +286,33 @@ def tile_list_transformer_overload_board_kernel(
             nc.vector.tensor_tensor(z_slot[7][:, c, :], pages[PAGE_OF[7]][:, cols], gains[7][:, cols], MULT)
             weave(1, c)
 
-        def add_and_store(c, i, engine, src, res):
-            engine.tensor_tensor(res, src, ambs[c][:, i, :], ADD)
+        def add_and_store(c, i):
+            res = ambs[c][:, i, :]
+            nc.vector.tensor_tensor(res, y_acc[c, i][:], res, ADD)
             nc.sync.dma_start(out[i * P : (i + 1) * P, c * BANK : (c + 1) * BANK], res)
 
-        def add_on_vector(c, i):
-            add_and_store(c, i, nc.vector, y_acc[c, i][:], ambs[c][:, i, :])
-
-        def products(c):
-            zq[0, c], zq[1, c] = halves(*quantize(z_words[c][:].rearrange("p b w -> p (b w)"), "zq", pool=ring))
+        def products(b, c):
+            tag = "h%d" % c if b == 1 else ("w3_bf" if c == 0 else "z_words0%d" % (c - 1))
+            codes, scales = quantize(z_words[b, c][:], "zq%d%d" % (b, c), tag)
+            zq[b, c] = (codes[:], scales[:])
             for i in range(N_TILES):
-                stage2_pass(0, c, i)
-                stage2_pass(1, c, i)
-
-        def first_products(b):
-            codes, scales = quantize(z_words[0][:, b, :], "zq_first%d" % b, ("w3_bf", "h5")[b])
-            zq[b, 0] = (codes[:], scales[:])
-            for i in range(N_TILES):
-                stage2_pass(b, 0, i)
-
-        def add_on_gpsimd(c, tag):
-            y_sb = keep.tile([P, BANK], F32, name="y_sb", tag="h%d" % c, align_bytes=64)
-            nc.scalar.copy(y_sb[:], y_acc[c, N_TILES - 1][:])
-            res = keep.tile([P, BANK], F32, name="res", tag=tag, align_bytes=64)
-            add_and_store(c, N_TILES - 1, nc.gpsimd, y_sb[:], res[:])
+                stage2_pass(b, c, i)
 
         last_gain(0)
         w3q.extend(halves(*quantize(w3_bf[:], "w3q", "h7")))
-        first_products(0)
+        products(0, 0)
         last_gain(1)
-        first_products(1)
+        products(1, 0)
+        products(0, 1)
         last_gain(2)
-        held_back = None
         for c in range(CHUNKS):
-            banks = list(range(N_TILES - 1 if c < GPSIMD_CHUNKS else N_TILES))
-            if 0 < c < CHUNKS - 1:
-                held_back = banks.pop()
-            for i in banks:
-                add_on_vector(c, i)
+            add_and_store(c, 0)
+            add_and_store(c, 1)
             if c + 1 < CHUNKS:
-                products(c + 1)
+                products(1, c + 1)
+            add_and_store(c, 2)
+            add_and_store(c, 3)
+            if c + 2 < CHUNKS:
+                products(0, c + 2)
             if c == 0:
                 last_gain(3)
-            elif c + 1 < CHUNKS:
-                add_on_vector(c, held_back)
-            if c < GPSIMD_CHUNKS:
-                add_on_gpsimd(c, "z_words%d" % (c + 1))

@@ -26,6 +26,7 @@ HALVES = S // BANK
 CHUNKS = T2 // BANK
 N_TILES = N // P
 SLICES = 8
+FIRST = 256
 SCALE_ROW = (4, 0)
 SLICE_ROWS = [(0, 0), (0, 1), (0, 2), (0, 3), (1, 2), (1, 0), (1, 1), (1, 3)]
 PAGE_OF = (0, 1, 2, 0, 1, 2, 0, 1)
@@ -60,17 +61,16 @@ def tile_list_transformer_overload_board_kernel(
             nc.gpsimd.memset(page[:], 0.0)
 
         def load_tab_scales(run):
-            a, q = divmod(run, 4)
-            row = 32 * q + SCALE_ROW[a]
+            r, a = divmod(run, 2)
             nc.sync.dma_start(
-                tab_s[row : row + 4, :].bitcast(I32),
-                tab_scales[a, 4 * q : 4 * q + 4, :].bitcast(I32),
+                tab_s[SCALE_ROW[a] + r : P : 32, :].bitcast(I32),
+                tab_scales[a, r:16:4, :].bitcast(I32),
             )
 
         def load_w2_scales(q):
             nc.sync.dma_start(
-                w2_s_raw[32 * q : 32 * q + 4, :].bitcast(I32),
-                w2_scales[0, 4 * q : 4 * q + 4, :].bitcast(I32),
+                w2_s_raw[q:P:32, :].bitcast(I32),
+                w2_scales[0, q:16:4, :].bitcast(I32),
             )
 
         idx = keep.tile([P, S // 16], U16, name="idx")
@@ -157,47 +157,58 @@ def tile_list_transformer_overload_board_kernel(
         for jh in range(HALVES):
             quantize_w1(w1_bf0[jh][:], 256 * jh)
             words1.append(keep.tile([P, BANK], U32, name="words1", tag="w1_then_words%d" % jh, align_bytes=64))
-            nc.vector.tensor_copy(words1[jh][:], tabs[1][:].bitcast(U32).indirect(idx[:, jh * 32 : (jh + 1) * 32]))
+            for lo in range(0, BANK, FIRST if jh == 0 else BANK):
+                js = slice(jh * BANK + lo, jh * BANK + lo + (FIRST if jh == 0 else BANK))
+                nc.vector.tensor_copy(
+                    words1[jh][:, lo : lo + js.stop - js.start],
+                    tabs[1][:].bitcast(U32).indirect(idx[:, js.start // 16 : js.stop // 16]),
+                )
 
         hs = {}
         raw = {}
 
-        def stage1(k, jhs=(0, 1)):
+        def heat(k, js, bank, dst):
             b, t = SLICE_ROWS[k]
-            if k not in hs:
-                hs[k] = keep.tile([P, S], F32, name="h", tag="h%d" % k, align_bytes=64)
-            h = hs[k]
             col = b * 512 + t * P
-            for jh in jhs:
-                js = slice(jh * BANK, (jh + 1) * BANK)
-                acc = psum.tile([P, BANK], F32, name="e_acc", tag="bank%d" % ((2 * k + jh) % BANKS))
+            width = js.stop - js.start
+            jh, lo = divmod(js.start, BANK)
+            acc = psum.tile([P, BANK], F32, name="e_acc", tag="bank%d" % bank)
+            nc.tensor.matmul_mx(
+                out=acc[:, 0:width],
+                lhsT=w1_codes[:, col : col + P].bitcast(FP8X4),
+                lhsT_scale=w1_scales[:, col : col + P],
+                rhs=words0[:, js].bitcast(FP8X4),
+                rhs_scale=g_scales[SCALE_ROW[0] : P, js],
+                start=True,
+                stop=False,
+            )
+            step = BANK if width == BANK else P
+            for n0 in range(0, width, step):
                 nc.tensor.matmul_mx(
-                    out=acc[:],
-                    lhsT=w1_codes[:, col : col + P].bitcast(FP8X4),
-                    lhsT_scale=w1_scales[:, col : col + P],
-                    rhs=words0[:, js].bitcast(FP8X4),
-                    rhs_scale=g_scales[SCALE_ROW[0] : P, js],
-                    start=True,
-                    stop=False,
-                )
-                nc.tensor.matmul_mx(
-                    out=acc[:],
+                    out=acc[:, n0 : n0 + step],
                     lhsT=w2_p[:, 2 * col : 2 * (col + P)].bitcast(FP4X4),
                     lhsT_scale=w2_s[:, col : col + P],
-                    rhs=words1[jh][:].bitcast(FP8X4),
-                    rhs_scale=g_scales[SCALE_ROW[1] : P, js],
+                    rhs=words1[jh][:, lo + n0 : lo + n0 + step].bitcast(FP8X4),
+                    rhs_scale=g_scales[SCALE_ROW[1] : P, js.start + n0 : js.start + n0 + step],
                     start=False,
-                    stop=True,
+                    stop=(n0 + step == width),
                 )
-                raw.setdefault((k, jh), h[:, js])
-                nc.scalar.activation(raw[k, jh], acc[:], GELU)
+            nc.scalar.activation(dst, acc[:, 0:width], GELU)
+
+        def stage1(k, jhs=(0, 1)):
+            if k not in hs:
+                hs[k] = keep.tile([P, S], F32, name="h", tag="h%d" % k, align_bytes=64)
+            for jh in jhs:
+                js = slice(jh * BANK, (jh + 1) * BANK)
+                raw.setdefault((k, jh), hs[k][:, js])
+                heat(k, js, (2 * k + 1 + jh) % BANKS, raw[k, jh])
 
         def weigh(k):
             nc.gpsimd.tensor_tensor(hs[k][:], hs[k][:], wgs_sb[:], MULT)
 
-        def weigh_half(k, jh, engine):
+        def weigh_half(k, jh):
             js = slice(jh * BANK, (jh + 1) * BANK)
-            engine.tensor_tensor(hs[k][:, js], raw[k, jh], wgs_sb[:, js], MULT)
+            nc.gpsimd.tensor_tensor(hs[k][:, js], raw[k, jh], wgs_sb[:, js], MULT)
 
         def scatter(k, js=slice(0, S)):
             offsets = idx2[:, js.start // 16 : js.stop // 16]
@@ -230,7 +241,10 @@ def tile_list_transformer_overload_board_kernel(
                 stop=(b == 1),
             )
 
-        stage1(0)
+        hs[0] = keep.tile([P, S], F32, name="h", tag="h0", align_bytes=64)
+        first_pieces = [slice(0, FIRST), slice(FIRST, BANK), slice(BANK, S)]
+        for bank, js in enumerate(first_pieces):
+            heat(0, js, bank, hs[0][:, js])
         for k in (1, 2, 3):
             stage1(k, (0,))
         w1_bf1 = arena.tile([P, 2048], BF16, name="w1_bf1", align_bytes=64, offset=8192)
@@ -239,15 +253,14 @@ def tile_list_transformer_overload_board_kernel(
         for k in (1, 2, 3):
             raw[k, 1] = late[:, k - 1, :]
             stage1(k, (1,))
-        weigh_half(0, 0, nc.vector)
-        scatter(0, slice(0, BANK))
-        weigh_half(0, 1, nc.gpsimd)
-        scatter(0, slice(BANK, S))
+        for js in first_pieces:
+            nc.gpsimd.tensor_tensor(hs[0][:, js], hs[0][:, js], wgs_sb[:, js], MULT)
+            scatter(0, js)
         for k in (1, 2, 3):
-            weigh_half(k, 0, nc.gpsimd)
+            weigh_half(k, 0)
         quantize_w1(w1_bf1[:], 512)
         for k in (1, 2, 3):
-            weigh_half(k, 1, nc.gpsimd)
+            weigh_half(k, 1)
         for k in range(4, SLICES):
             stage1(k)
         w3_bf = keep.tile([P, 4096], BF16, name="w3_bf", tag="w3_bf", align_bytes=64)

@@ -28,7 +28,6 @@ N_TILES = N // P
 SLICES = 8
 FIRST = 256
 SCALE_ROW = (4, 0)
-SLICE_ROWS = [(0, 0), (0, 1), (0, 2), (0, 3), (1, 2), (1, 0), (1, 1), (1, 3)]
 PAGE_OF = (0, 1, 2, 0, 1, 2, 0, 1)
 
 
@@ -61,16 +60,17 @@ def tile_list_transformer_overload_board_kernel(
             nc.gpsimd.memset(page[:], 0.0)
 
         def load_tab_scales(run):
-            r, a = divmod(run, 2)
+            a, q = divmod(run, 4)
+            row = 32 * q + SCALE_ROW[a]
             nc.sync.dma_start(
-                tab_s[SCALE_ROW[a] + r : P : 32, :].bitcast(I32),
-                tab_scales[a, r:16:4, :].bitcast(I32),
+                tab_s[row : row + 4, :].bitcast(I32),
+                tab_scales[a, 4 * q : 4 * q + 4, :].bitcast(I32),
             )
 
         def load_w2_scales(q):
             nc.sync.dma_start(
-                w2_s_raw[q:P:32, :].bitcast(I32),
-                w2_scales[0, q:16:4, :].bitcast(I32),
+                w2_s_raw[32 * q : 32 * q + 4, :].bitcast(I32),
+                w2_scales[0, 4 * q : 4 * q + 4, :].bitcast(I32),
             )
 
         idx = keep.tile([P, S // 16], U16, name="idx")
@@ -97,7 +97,7 @@ def tile_list_transformer_overload_board_kernel(
         gains = {}
         w3_raw = []
         for k in range(SLICES):
-            gains[k] = load_rows(gain_rows[SLICE_ROWS[k][0], SLICE_ROWS[k][1]], F32, "gain%d" % k)
+            gains[k] = load_rows(gain_rows[k // PACK, k % PACK], F32, "gain%d" % k)
             if k == 5:
                 w3_raw.extend(load_k_first(w3[512 * b : 512 * (b + 1), :], "w3_raw%d" % b) for b in range(2))
         ambs = []
@@ -168,7 +168,7 @@ def tile_list_transformer_overload_board_kernel(
         raw = {}
 
         def heat(k, js, bank, dst):
-            b, t = SLICE_ROWS[k]
+            b, t = divmod(k, PACK)
             col = b * 512 + t * P
             width = js.stop - js.start
             jh, lo = divmod(js.start, BANK)
@@ -253,8 +253,9 @@ def tile_list_transformer_overload_board_kernel(
         for k in (1, 2, 3):
             raw[k, 1] = late[:, k - 1, :]
             stage1(k, (1,))
-        for js in first_pieces:
-            nc.gpsimd.tensor_tensor(hs[0][:, js], hs[0][:, js], wgs_sb[:, js], MULT)
+        for jh, engine in enumerate((nc.vector, nc.gpsimd)):
+            js = slice(jh * BANK, (jh + 1) * BANK)
+            engine.tensor_tensor(hs[0][:, js], hs[0][:, js], wgs_sb[:, js], MULT)
             scatter(0, js)
         for k in (1, 2, 3):
             weigh_half(k, 0)
@@ -267,22 +268,36 @@ def tile_list_transformer_overload_board_kernel(
         for b in range(2):
             cast_w3(b, w3_bf[:, b * 2048 : (b + 1) * 2048])
 
-        z_pairs = [
-            arena.tile([P, 4 * T2], BF16, name="z_pairs0", align_bytes=64, offset=4096),
-            keep.tile([P, 4 * T2], BF16, name="z_pairs1", align_bytes=64),
-        ]
-        for k, (b, t) in enumerate(SLICE_ROWS):
-            z_slot[k] = z_pairs[b][:].rearrange("p (c u m e) -> p c u m e", c=CHUNKS, u=2, e=2)[:, :, t // 2, :, t % 2]
+        z_pairs = arena.tile([P, 4 * T2], BF16, name="z_pairs", align_bytes=64, offset=4096)
+        z_pair_low = keep.tile([P, 2 * T2], BF16, name="z_pair_low", align_bytes=64)
+        z_planes = keep.tile([P, 2, T2], BF16, name="z_planes", align_bytes=64)
+        for t in range(PACK):
+            z_slot[t] = z_pairs[:].rearrange("p (c u m e) -> p c u m e", c=CHUNKS, u=2, e=2)[:, :, t // 2, :, t % 2]
+        for t in range(2):
+            z_slot[4 + t] = z_pair_low[:].rearrange("p (c m e) -> p c m e", c=CHUNKS, e=2)[:, :, :, t]
+            z_slot[6 + t] = z_planes[:, t, :].rearrange("p (c m) -> p c m", c=CHUNKS)
         z_words = {
             (b, c): keep.tile([P, 2048], BF16, name="z_words", tag="z_words%d%d" % (b, c), align_bytes=64)
             for b in range(2)
             for c in range(CHUNKS)
         }
 
-        def weave(b, c):
+        def weave_pass0(c):
             nc.scalar.copy(
-                z_words[b, c][:].bitcast(F32).rearrange("p (m u) -> p m u", u=2),
-                z_pairs[b][:, c * 2048 : (c + 1) * 2048].bitcast(F32).rearrange("p (u m) -> p m u", u=2),
+                z_words[0, c][:].bitcast(F32).rearrange("p (m u) -> p m u", u=2),
+                z_pairs[:, c * 2048 : (c + 1) * 2048].bitcast(F32).rearrange("p (u m) -> p m u", u=2),
+            )
+
+        def weave_low(c):
+            nc.scalar.copy(
+                z_words[1, c][:].bitcast(F32).rearrange("p (m u) -> p m u", u=2)[:, :, 0],
+                z_pair_low[:, c * 1024 : (c + 1) * 1024].bitcast(F32),
+            )
+
+        def weave_high(c):
+            nc.scalar.copy(
+                z_words[1, c][:].rearrange("p (m t) -> p m t", t=PACK)[:, :, 2:4],
+                z_planes[:, :, c * BANK : (c + 1) * BANK].rearrange("p t m -> p m t"),
             )
 
         for k in range(1, SLICES):
@@ -292,12 +307,15 @@ def tile_list_transformer_overload_board_kernel(
                 weigh(k + 3)
             if k == 4:
                 for c in range(CHUNKS):
-                    weave(0, c)
+                    weave_pass0(c)
+            if k == 6:
+                for c in range(CHUNKS):
+                    weave_low(c)
 
         def last_gain(c):
             cols = slice(c * BANK, (c + 1) * BANK)
             nc.vector.tensor_tensor(z_slot[7][:, c, :], pages[PAGE_OF[7]][:, cols], gains[7][:, cols], MULT)
-            weave(1, c)
+            weave_high(c)
 
         def add_and_store(c, i):
             res = ambs[c][:, i, :]

@@ -27,6 +27,8 @@ CHUNKS = T2 // BANK
 N_TILES = N // P
 SLICES = 8
 FIRST = 256
+RING = 5
+BLOCK = 3 * BANK + 2048
 SCALE_ROW = (4, 0)
 PAGE_OF = (0, 1, 2, 0, 1, 2, 0, 1)
 
@@ -97,7 +99,14 @@ def tile_list_transformer_overload_board_kernel(
         gains = {}
         w3_raw = []
         for k in range(SLICES):
-            gains[k] = load_rows(gain_rows[k // PACK, k % PACK], F32, "gain%d" % k)
+            rows = gain_rows[k // PACK, k % PACK]
+            if k < SLICES - 1:
+                gains[k] = load_rows(rows, F32, "gain%d" % k)
+            else:
+                gain_first = keep.tile([P, BANK], F32, name="gain_first", tag="gain_first", align_bytes=64)
+                nc.sync.dma_start(gain_first[:], rows[:, 0:BANK])
+                gain_rest = stage.tile([P, T2 - BANK], F32, name="gain_rest", tag="rows")
+                nc.sync.dma_start(gain_rest[:], rows[:, BANK:T2])
             if k == 5:
                 w3_raw.extend(load_k_first(w3[512 * b : 512 * (b + 1), :], "w3_raw%d" % b) for b in range(2))
         ambs = []
@@ -124,9 +133,6 @@ def tile_list_transformer_overload_board_kernel(
                 dst.rearrange("p (c i j) -> p c j i", i=4, j=PACK),
                 w3_raw[b][:].rearrange("p j (c i) -> p c j i", i=4),
             )
-
-        def halves(codes, scales):
-            return [(codes[:, c * BANK : (c + 1) * BANK], scales[:, c * BANK : (c + 1) * BANK]) for c in range(2)]
 
         words0 = keep.tile([P, S], U32, name="words0", align_bytes=64)
         g_scales = keep.tile([P, S], U8, name="g_scales", align_bytes=64)
@@ -230,7 +236,7 @@ def tile_list_transformer_overload_board_kernel(
 
         def stage2_pass(b, c, i):
             if b == 0:
-                y_acc[c, i] = psum.tile([P, BANK], F32, name="y_acc", tag="bank%d" % ((N_TILES * c + i) % BANKS))
+                y_acc[c, i] = psum.tile([P, BANK], F32, name="y_acc", tag="bank%d" % ((N_TILES * c + i) % RING))
             nc.tensor.matmul_mx(
                 out=y_acc[c, i][:],
                 lhsT=w3q[b][0][:, i * P : (i + 1) * P].bitcast(FP8X4),
@@ -264,40 +270,35 @@ def tile_list_transformer_overload_board_kernel(
             weigh_half(k, 1)
         for k in range(4, SLICES):
             stage1(k)
-        w3_bf = keep.tile([P, 4096], BF16, name="w3_bf", tag="w3_bf", align_bytes=64)
+        zone = keep.tile([P, CHUNKS, BLOCK], BF16, name="zone", align_bytes=64)
+        w3_bf0 = keep.tile([P, 2048], BF16, name="w3_bf0", tag="w3_bf0", align_bytes=64)
+        w3_bf = [w3_bf0[:], zone[:, 1, 3 * BANK : BLOCK]]
         for b in range(2):
-            cast_w3(b, w3_bf[:, b * 2048 : (b + 1) * 2048])
+            cast_w3(b, w3_bf[b])
 
         z_pairs = arena.tile([P, 4 * T2], BF16, name="z_pairs", align_bytes=64, offset=4096)
-        z_pair_low = keep.tile([P, 2 * T2], BF16, name="z_pair_low", align_bytes=64)
-        z_planes = keep.tile([P, 2, T2], BF16, name="z_planes", align_bytes=64)
         for t in range(PACK):
             z_slot[t] = z_pairs[:].rearrange("p (c u m e) -> p c u m e", c=CHUNKS, u=2, e=2)[:, :, t // 2, :, t % 2]
-        for t in range(2):
-            z_slot[4 + t] = z_pair_low[:].rearrange("p (c m e) -> p c m e", c=CHUNKS, e=2)[:, :, :, t]
-            z_slot[6 + t] = z_planes[:, t, :].rearrange("p (c m) -> p c m", c=CHUNKS)
+            z_slot[PACK + t] = zone[:, :, t * BANK : (t + 1) * BANK]
         z_words = {
-            (b, c): keep.tile([P, 2048], BF16, name="z_words", tag="z_words%d%d" % (b, c), align_bytes=64)
+            (b, c): keep.tile([P, 2048], BF16, name="z_words", tag="z_words%d%d" % (b, c), align_bytes=64)[:]
             for b in range(2)
             for c in range(CHUNKS)
+            if (b, c) not in ((0, 1), (0, 2))
         }
+        for c in (1, 2):
+            z_words[0, c] = zone[:, c + 1, 3 * BANK : BLOCK]
 
         def weave_pass0(c):
             nc.scalar.copy(
-                z_words[0, c][:].bitcast(F32).rearrange("p (m u) -> p m u", u=2),
+                z_words[0, c].bitcast(F32).rearrange("p (m u) -> p m u", u=2),
                 z_pairs[:, c * 2048 : (c + 1) * 2048].bitcast(F32).rearrange("p (u m) -> p m u", u=2),
             )
 
-        def weave_low(c):
+        def weave_pass1(c, ts):
             nc.scalar.copy(
-                z_words[1, c][:].bitcast(F32).rearrange("p (m u) -> p m u", u=2)[:, :, 0],
-                z_pair_low[:, c * 1024 : (c + 1) * 1024].bitcast(F32),
-            )
-
-        def weave_high(c):
-            nc.scalar.copy(
-                z_words[1, c][:].rearrange("p (m t) -> p m t", t=PACK)[:, :, 2:4],
-                z_planes[:, :, c * BANK : (c + 1) * BANK].rearrange("p t m -> p m t"),
+                z_words[1, c].rearrange("p (m i t) -> p m t i", i=4, t=PACK)[:, :, ts, :],
+                zone[:, c, 0 : PACK * BANK].rearrange("p (t m i) -> p m t i", t=PACK, i=4)[:, :, ts, :],
             )
 
         for k in range(1, SLICES):
@@ -309,41 +310,41 @@ def tile_list_transformer_overload_board_kernel(
                 for c in range(CHUNKS):
                     weave_pass0(c)
             if k == 6:
-                for c in range(CHUNKS):
-                    weave_low(c)
+                weave_pass1(0, slice(0, 2))
 
-        def last_gain(c):
+        def last_gain(c, engine):
             cols = slice(c * BANK, (c + 1) * BANK)
-            nc.vector.tensor_tensor(z_slot[7][:, c, :], pages[PAGE_OF[7]][:, cols], gains[7][:, cols], MULT)
-            weave_high(c)
+            gain_c = gain_first[:] if c == 0 else gain_rest[:, (c - 1) * BANK : c * BANK]
+            engine.tensor_tensor(z_slot[7][:, c, :], pages[PAGE_OF[7]][:, cols], gain_c, MULT)
+            weave_pass1(c, slice(2, PACK) if c == 0 else slice(0, PACK))
 
         def add_and_store(c, i):
             res = ambs[c][:, i, :]
             nc.vector.tensor_tensor(res, y_acc[c, i][:], res, ADD)
             nc.sync.dma_start(out[i * P : (i + 1) * P, c * BANK : (c + 1) * BANK], res)
 
-        def products(b, c):
-            tag = "h%d" % c if b == 1 else ("w3_bf" if c == 0 else "z_words0%d" % (c - 1))
-            codes, scales = quantize(z_words[b, c][:], "zq%d%d" % (b, c), tag)
+        def products(b, c, tag):
+            codes, scales = quantize(z_words[b, c], "zq%d%d" % (b, c), tag)
             zq[b, c] = (codes[:], scales[:])
             for i in range(N_TILES):
                 stage2_pass(b, c, i)
 
-        last_gain(0)
-        w3q.extend(halves(*quantize(w3_bf[:], "w3q", "h7")))
-        products(0, 0)
-        last_gain(1)
-        products(1, 0)
-        products(0, 1)
-        last_gain(2)
+        def quantize_w3(b, tag):
+            codes, scales = quantize(w3_bf[b], "w3q%d" % b, tag)
+            w3q.append((codes[:], scales[:]))
+
+        last_gain(0, nc.vector)
+        quantize_w3(0, "gain_first")
+        products(0, 0, "w3_bf0")
+        quantize_w3(1, "z_words00")
+        last_gain(1, nc.vector)
         for c in range(CHUNKS):
-            add_and_store(c, 0)
-            add_and_store(c, 1)
-            if c + 1 < CHUNKS:
-                products(1, c + 1)
-            add_and_store(c, 2)
-            add_and_store(c, 3)
+            if c < CHUNKS - 1:
+                products(1, c, "h%d" % c)
+                products(0, c + 1, "z_words1%d" % c)
             if c + 2 < CHUNKS:
-                products(0, c + 2)
-            if c == 0:
-                last_gain(3)
+                last_gain(c + 2, nc.gpsimd)
+            for i in range(N_TILES):
+                if (c, i) == (CHUNKS - 2, N_TILES - 1):
+                    products(1, CHUNKS - 1, "h3")
+                add_and_store(c, i)

@@ -27,7 +27,6 @@ CHUNKS = T2 // BANK
 N_TILES = N // P
 SLICES = 8
 FIRST = 256
-RING = 5
 BLOCK = 3 * BANK + 2048
 SCALE_ROW = (4, 0)
 PAGE_OF = (0, 1, 2, 0, 1, 2, 0, 1)
@@ -103,10 +102,14 @@ def tile_list_transformer_overload_board_kernel(
             if k < SLICES - 1:
                 gains[k] = load_rows(rows, F32, "gain%d" % k)
             else:
-                gain_first = keep.tile([P, BANK], F32, name="gain_first", tag="gain_first", align_bytes=64)
-                nc.sync.dma_start(gain_first[:], rows[:, 0:BANK])
-                gain_rest = stage.tile([P, T2 - BANK], F32, name="gain_rest", tag="rows")
-                nc.sync.dma_start(gain_rest[:], rows[:, BANK:T2])
+                last_gains = []
+                for c in range(2):
+                    g_sb = keep.tile([P, BANK], F32, name="last_gain", tag="last_gain%d" % c, align_bytes=64)
+                    nc.sync.dma_start(g_sb[:], rows[:, c * BANK : (c + 1) * BANK])
+                    last_gains.append(g_sb[:])
+                gain_rest = stage.tile([P, 2, BANK], F32, name="gain_rest", tag="rows")
+                nc.sync.dma_start(gain_rest[:], rows[:, 2 * BANK : T2].rearrange("p (c m) -> p c m", c=2))
+                last_gains.extend(gain_rest[:, c, :] for c in range(2))
             if k == 5:
                 w3_raw.extend(load_k_first(w3[512 * b : 512 * (b + 1), :], "w3_raw%d" % b) for b in range(2))
         ambs = []
@@ -236,7 +239,7 @@ def tile_list_transformer_overload_board_kernel(
 
         def stage2_pass(b, c, i):
             if b == 0:
-                y_acc[c, i] = psum.tile([P, BANK], F32, name="y_acc", tag="bank%d" % ((N_TILES * c + i) % RING))
+                y_acc[c, i] = psum.tile([P, BANK], F32, name="y_acc", tag="bank%d" % ((N_TILES * c + i) % BANKS))
             nc.tensor.matmul_mx(
                 out=y_acc[c, i][:],
                 lhsT=w3q[b][0][:, i * P : (i + 1) * P].bitcast(FP8X4),
@@ -271,8 +274,7 @@ def tile_list_transformer_overload_board_kernel(
         for k in range(4, SLICES):
             stage1(k)
         zone = keep.tile([P, CHUNKS, BLOCK], BF16, name="zone", align_bytes=64)
-        w3_bf0 = keep.tile([P, 2048], BF16, name="w3_bf0", tag="w3_bf0", align_bytes=64)
-        w3_bf = [w3_bf0[:], zone[:, 1, 3 * BANK : BLOCK]]
+        w3_bf = [keep.tile([P, 2048], BF16, name="w3_bf", tag="w3_bf%d" % b, align_bytes=64)[:] for b in range(2)]
         for b in range(2):
             cast_w3(b, w3_bf[b])
 
@@ -284,10 +286,10 @@ def tile_list_transformer_overload_board_kernel(
             (b, c): keep.tile([P, 2048], BF16, name="z_words", tag="z_words%d%d" % (b, c), align_bytes=64)[:]
             for b in range(2)
             for c in range(CHUNKS)
-            if (b, c) not in ((0, 1), (0, 2))
+            if (b, c) not in ((1, 0), (1, 1))
         }
-        for c in (1, 2):
-            z_words[0, c] = zone[:, c + 1, 3 * BANK : BLOCK]
+        for c in range(2):
+            z_words[1, c] = zone[:, c + 2, 3 * BANK : BLOCK]
 
         def weave_pass0(c):
             nc.scalar.copy(
@@ -314,8 +316,7 @@ def tile_list_transformer_overload_board_kernel(
 
         def last_gain(c, engine):
             cols = slice(c * BANK, (c + 1) * BANK)
-            gain_c = gain_first[:] if c == 0 else gain_rest[:, (c - 1) * BANK : c * BANK]
-            engine.tensor_tensor(z_slot[7][:, c, :], pages[PAGE_OF[7]][:, cols], gain_c, MULT)
+            engine.tensor_tensor(z_slot[7][:, c, :], pages[PAGE_OF[7]][:, cols], last_gains[c], MULT)
             weave_pass1(c, slice(2, PACK) if c == 0 else slice(0, PACK))
 
         def add_and_store(c, i):
@@ -334,17 +335,21 @@ def tile_list_transformer_overload_board_kernel(
             w3q.append((codes[:], scales[:]))
 
         last_gain(0, nc.vector)
-        quantize_w3(0, "gain_first")
-        products(0, 0, "w3_bf0")
-        quantize_w3(1, "z_words00")
         last_gain(1, nc.vector)
+        quantize_w3(0, "last_gain0")
+        products(0, 0, "last_gain1")
+        quantize_w3(1, "w3_bf0")
+        products(1, 0, "h0")
+        products(0, 1, "w3_bf1")
+        last_gain(2, nc.vector)
+        products(0, 2, "z_words01")
         for c in range(CHUNKS):
-            if c < CHUNKS - 1:
-                products(1, c, "h%d" % c)
-                products(0, c + 1, "z_words1%d" % c)
-            if c + 2 < CHUNKS:
-                last_gain(c + 2, nc.gpsimd)
-            for i in range(N_TILES):
-                if (c, i) == (CHUNKS - 2, N_TILES - 1):
-                    products(1, CHUNKS - 1, "h3")
+            add_and_store(c, 0)
+            if c == 0:
+                products(0, 3, "z_words02")
+            if c + 1 < CHUNKS:
+                products(1, c + 1, "h%d" % (c + 1))
+            if c == 0:
+                last_gain(3, nc.gpsimd)
+            for i in range(1, N_TILES):
                 add_and_store(c, i)

@@ -40,6 +40,7 @@ def tile_list_transformer_overload_board_kernel(
         keep = ctx.enter_context(tc.tile_pool(name="keep", bufs=1))
         stage = ctx.enter_context(tc.tile_pool(name="stage", bufs=6))
         arena = ctx.enter_context(tc.tile_pool(name="arena", bufs=1))
+        head = ctx.enter_context(tc.tile_pool(name="head", bufs=1))
         psum = ctx.enter_context(tc.psum_pool(name="psum", bufs=1))
 
         def load_rows(src, dtype, name):
@@ -53,44 +54,40 @@ def tile_list_transformer_overload_board_kernel(
             return t
 
         tab_s = keep.tile([P, T], U8, name="tab_s", align_bytes=64)
-        w2_s_raw = keep.tile([P, H], U8, name="w2_s_raw", align_bytes=64)
+        w2_s_raw = head.tile([P, H], U8, name="w2_s_raw", align_bytes=64, offset=0)
         nc.gpsimd.memset(tab_s[:].bitcast(I32), 0)
         nc.gpsimd.memset(w2_s_raw[:].bitcast(I32), 0)
         pages = [keep.tile([P, T2], F32, name="page%d" % i) for i in range(3)]
         for page in pages:
             nc.gpsimd.memset(page[:], 0.0)
 
-        def load_tab_scales(run):
-            a, q = divmod(run, 4)
-            row = 32 * q + SCALE_ROW[a]
-            nc.sync.dma_start(
-                tab_s[row : row + 4, :].bitcast(I32),
-                tab_scales[a, 4 * q : 4 * q + 4, :].bitcast(I32),
-            )
+        def load_tab_scales(a, r):
+            row = SCALE_ROW[a] + r
+            nc.sync.dma_start(tab_s[row:P:32, :].bitcast(I32), tab_scales[a, r:16:4, :].bitcast(I32))
 
-        def load_w2_scales(q):
-            nc.sync.dma_start(
-                w2_s_raw[32 * q : 32 * q + 4, :].bitcast(I32),
-                w2_scales[0, 4 * q : 4 * q + 4, :].bitcast(I32),
-            )
+        def load_w2_scales(r):
+            nc.sync.dma_start(w2_s_raw[r:P:32, :].bitcast(I32), w2_scales[0, r:16:4, :].bitcast(I32))
 
         idx = keep.tile([P, S // 16], U16, name="idx")
         nc.sync.dma_start(idx[:], offs)
         tab0 = load_rows(tab_words[0].rearrange("p t i -> p (t i)").bitcast(I32), I32, "tab0")
-        for run in range(8):
-            load_tab_scales(run)
+        runs = [(a, r) for r in range(4) for a in range(2)]
+        for a, r in runs[:5]:
+            load_tab_scales(a, r)
         w1_raw = [load_k_first(w1[:, 0:512], "w1_raw0")]
-        w2_raw = keep.tile([P, 2 * H], U8, name="w2_raw")
-        nc.sync.dma_start(w2_raw[:].bitcast(I32), w2_words[0].bitcast(I32))
-        for q in range(4):
-            load_w2_scales(q)
+        for a, r in runs[5:]:
+            load_tab_scales(a, r)
         tab1 = load_rows(tab_words[1].rearrange("p t i -> p (t i)").bitcast(I32), I32, "tab1")
         tabs = [tab0, tab1]
+        w2_raw = head.tile([P, 2 * H], U8, name="w2_raw", align_bytes=64, offset=H)
+        nc.sync.dma_start(w2_raw[:].bitcast(I32), w2_words[0].bitcast(I32))
+        for r in range(4):
+            load_w2_scales(r)
         wgs_sb = keep.tile([P, S], F32, name="wgs_sb")
         nc.sync.dma_start(wgs_sb[:], wgs)
         idx2 = keep.tile([P, S // 16], U16, name="idx2")
         nc.sync.dma_start(idx2[:], offs2)
-        w1_raw1 = arena.tile([P, PACK, 512], F32, name="w1_raw1", align_bytes=64, offset=0)
+        w1_raw1 = arena.tile([P, PACK, 512], F32, name="w1_raw1", align_bytes=64, offset=4096)
         nc.sync.dma_start(w1_raw1[:], w1[:, 512:1024].rearrange("(p j) c -> p j c", j=PACK))
         w1_raw.append(w1_raw1)
 
@@ -138,23 +135,8 @@ def tile_list_transformer_overload_board_kernel(
             )
 
         words0 = keep.tile([P, S], U32, name="words0", align_bytes=64)
-        g_scales = keep.tile([P, S], U8, name="g_scales", align_bytes=64)
         w2_p = keep.tile([P, 2 * H], U8, name="w2_p", align_bytes=64)
         w2_s = keep.tile([P, H], U8, name="w2_s", align_bytes=64)
-
-        w1_bf0 = [keep.tile([P, 1024], BF16, name="w1_bf0", tag="w1_then_words%d" % u, align_bytes=64) for u in range(2)]
-        for u in range(2):
-            cast_w1(0, w1_bf0[u][:], slice(2 * u, 2 * u + 2))
-        nc.vector.tensor_copy(words0[:], tabs[0][:].bitcast(U32).indirect(idx[:]))
-        nc.vector.tensor_copy(g_scales[:], tab_s[:].indirect(idx[:]))
-        nc.vector.tensor_copy(
-            w2_p[:].bitcast(U16).rearrange("p (b t m) -> p b t m", b=2, t=PACK),
-            w2_raw[:].bitcast(U16).rearrange("p (b m t) -> p b t m", b=2, t=PACK),
-        )
-        nc.vector.tensor_copy(
-            w2_s[:].rearrange("p (b t m) -> p b t m", b=2, t=PACK),
-            w2_s_raw[:].rearrange("p (b m t) -> p b t m", b=2, t=PACK),
-        )
         w1_codes = keep.tile([P, H], U32, name="w1_codes", align_bytes=64)
         w1_scales = keep.tile([P, H], U8, name="w1_scales", align_bytes=64)
 
@@ -162,16 +144,36 @@ def tile_list_transformer_overload_board_kernel(
             cols = slice(col, col + src.shape[1] // PACK)
             nc.vector.quantize_mx(out=w1_codes[:, cols].bitcast(FP8X4), scales=w1_scales[:, cols], in_=src)
 
-        words1 = []
-        for jh in range(HALVES):
-            quantize_w1(w1_bf0[jh][:], 256 * jh)
-            words1.append(keep.tile([P, BANK], U32, name="words1", tag="w1_then_words%d" % jh, align_bytes=64))
-            for lo in range(0, BANK, FIRST if jh == 0 else BANK):
-                js = slice(jh * BANK + lo, jh * BANK + lo + (FIRST if jh == 0 else BANK))
-                nc.vector.tensor_copy(
-                    words1[jh][:, lo : lo + js.stop - js.start],
-                    tabs[1][:].bitcast(U32).indirect(idx[:, js.start // 16 : js.stop // 16]),
-                )
+        def deal_w2(b):
+            cols = slice(b * 512, (b + 1) * 512)
+            nc.vector.tensor_copy(
+                w2_p[:].bitcast(U16)[:, cols].rearrange("p (t u m) -> p u t m", t=PACK, u=2),
+                w2_raw[:].bitcast(U16)[:, cols].rearrange("p (u m t) -> p u t m", t=PACK, u=2),
+            )
+            nc.vector.tensor_copy(
+                w2_s[:, cols].rearrange("p (t u m) -> p u t m", t=PACK, u=2),
+                w2_s_raw[:, cols].rearrange("p (u m t) -> p u t m", t=PACK, u=2),
+            )
+
+        def gather(dst, window, jh):
+            nc.vector.tensor_copy(dst[:], window.indirect(idx[:, jh * BANK // 16 : (jh + 1) * BANK // 16]))
+
+        w1_bf0 = [keep.tile([P, 1024], BF16, name="w1_bf0", tag="w1_then_words%d" % u, align_bytes=64) for u in range(2)]
+        for u in range(2):
+            cast_w1(0, w1_bf0[u][:], slice(2 * u, 2 * u + 2))
+        nc.vector.tensor_copy(words0[:], tabs[0][:].bitcast(U32).indirect(idx[:]))
+        g_scales = [keep.tile([P, BANK], U8, name="g_scales0", align_bytes=64)]
+        gather(g_scales[0], tab_s[:], 0)
+        quantize_w1(w1_bf0[0][:], 0)
+        words1 = [keep.tile([P, BANK], U32, name="words1_low", align_bytes=64)]
+        gather(words1[0], tabs[1][:].bitcast(U32), 0)
+        deal_w2(0)
+        quantize_w1(w1_bf0[1][:], 256)
+        deal_w2(1)
+        g_scales.append(head.tile([P, BANK], U8, name="g_scales1", align_bytes=64, offset=0))
+        gather(g_scales[1], tab_s[:], 1)
+        words1.append(head.tile([P, BANK], U32, name="words1_high", align_bytes=64, offset=BANK))
+        gather(words1[1], tabs[1][:].bitcast(U32), 1)
 
         hs = {}
         raw = {}
@@ -187,7 +189,7 @@ def tile_list_transformer_overload_board_kernel(
                 lhsT=w1_codes[:, col : col + P].bitcast(FP8X4),
                 lhsT_scale=w1_scales[:, col : col + P],
                 rhs=words0[:, js].bitcast(FP8X4),
-                rhs_scale=g_scales[SCALE_ROW[0] : P, js],
+                rhs_scale=g_scales[jh][SCALE_ROW[0] : P, lo : lo + width],
                 start=True,
                 stop=False,
             )
@@ -198,7 +200,7 @@ def tile_list_transformer_overload_board_kernel(
                     lhsT=w2_p[:, 2 * col : 2 * (col + P)].bitcast(FP4X4),
                     lhsT_scale=w2_s[:, col : col + P],
                     rhs=words1[jh][:, lo + n0 : lo + n0 + step].bitcast(FP8X4),
-                    rhs_scale=g_scales[SCALE_ROW[1] : P, js.start + n0 : js.start + n0 + step],
+                    rhs_scale=g_scales[jh][SCALE_ROW[1] : P, lo + n0 : lo + n0 + step],
                     start=False,
                     stop=(n0 + step == width),
                 )
@@ -215,9 +217,8 @@ def tile_list_transformer_overload_board_kernel(
         def weigh(k):
             nc.gpsimd.tensor_tensor(hs[k][:], hs[k][:], wgs_sb[:], MULT)
 
-        def weigh_half(k, jh):
-            js = slice(jh * BANK, (jh + 1) * BANK)
-            nc.gpsimd.tensor_tensor(hs[k][:, js], raw[k, jh], wgs_sb[:, js], MULT)
+        def weigh_part(k, js, src):
+            nc.gpsimd.tensor_tensor(hs[k][:, js], src, wgs_sb[:, js], MULT)
 
         def scatter(k, js=slice(0, S)):
             offsets = idx2[:, js.start // 16 : js.stop // 16]
@@ -250,27 +251,33 @@ def tile_list_transformer_overload_board_kernel(
                 stop=(b == 1),
             )
 
+        low, high = slice(0, BANK), slice(BANK, S)
         hs[0] = keep.tile([P, S], F32, name="h", tag="h0", align_bytes=64)
-        first_pieces = [slice(0, FIRST), slice(FIRST, BANK), slice(BANK, S)]
+        first_pieces = [slice(0, FIRST), slice(FIRST, BANK)]
         for bank, js in enumerate(first_pieces):
             heat(0, js, bank, hs[0][:, js])
-        for k in (1, 2, 3):
-            stage1(k, (0,))
-        w1_bf1 = arena.tile([P, 2048], BF16, name="w1_bf1", align_bytes=64, offset=8192)
-        cast_w1(1, w1_bf1[:], slice(0, PACK))
-        late = arena.tile([P, 3, BANK], F32, name="late", align_bytes=64, offset=2048)
-        for k in (1, 2, 3):
-            raw[k, 1] = late[:, k - 1, :]
-            stage1(k, (1,))
-        for jh, engine in enumerate((nc.vector, nc.gpsimd)):
-            js = slice(jh * BANK, (jh + 1) * BANK)
-            engine.tensor_tensor(hs[0][:, js], hs[0][:, js], wgs_sb[:, js], MULT)
+            weigh_part(0, js, hs[0][:, js])
             scatter(0, js)
-        for k in (1, 2, 3):
-            weigh_half(k, 0)
+        for k in (1, 2):
+            stage1(k, (0,))
+            weigh_part(k, low, raw[k, 0])
+        w1_bf1 = arena.tile([P, 2048], BF16, name="w1_bf1", align_bytes=64, offset=0)
+        cast_w1(1, w1_bf1[:, 0:1024], slice(0, 2))
+        heat(0, high, 2, hs[0][:, high])
+        weigh_part(0, high, hs[0][:, high])
+        scatter(0, high)
+        stage1(3, (0,))
+        weigh_part(3, low, raw[3, 0])
+        cast_w1(1, w1_bf1[:, 1024:2048], slice(2, PACK))
+        for k in (1, 2):
+            late = arena.tile([P, BANK], F32, name="late%d" % k, align_bytes=64, offset=2048 * (k + 1))
+            raw[k, 1] = late[:]
+            stage1(k, (1,))
+            weigh_part(k, high, raw[k, 1])
         quantize_w1(w1_bf1[:], 512)
-        for k in (1, 2, 3):
-            weigh_half(k, 1)
+        late3 = arena.tile([P, BANK], F32, name="late3", align_bytes=64, offset=0)
+        raw[3, 1] = late3[:]
+        stage1(3, (1,))
         for k in range(4, SLICES):
             stage1(k)
         zone = keep.tile([P, CHUNKS, BLOCK], BF16, name="zone", align_bytes=64)
@@ -278,7 +285,7 @@ def tile_list_transformer_overload_board_kernel(
         for b in range(2):
             cast_w3(b, w3_bf[b])
 
-        z_pairs = arena.tile([P, 4 * T2], BF16, name="z_pairs", align_bytes=64, offset=4096)
+        z_pairs = arena.tile([P, 4 * T2], BF16, name="z_pairs", align_bytes=64, offset=2048)
         for t in range(PACK):
             z_slot[t] = z_pairs[:].rearrange("p (c u m e) -> p c u m e", c=CHUNKS, u=2, e=2)[:, :, t // 2, :, t % 2]
             z_slot[PACK + t] = zone[:, :, t * BANK : (t + 1) * BANK]
@@ -306,6 +313,8 @@ def tile_list_transformer_overload_board_kernel(
         for k in range(1, SLICES):
             scatter(k)
             times_gain(k - 1)
+            if k == 1:
+                weigh_part(3, high, raw[3, 1])
             if k + 3 < SLICES:
                 weigh(k + 3)
             if k == 4:
@@ -348,7 +357,7 @@ def tile_list_transformer_overload_board_kernel(
             if c == 0:
                 products(0, 3, "z_words02")
             if c + 1 < CHUNKS:
-                products(1, c + 1, "h%d" % (c + 1))
+                products(1, c + 1, "h%d" % (c + 3))
             if c == 0:
                 last_gain(3, nc.gpsimd)
             for i in range(1, N_TILES):

@@ -61,17 +61,19 @@ def tile_list_transformer_overload_board_kernel(
         for page in pages:
             nc.gpsimd.memset(page[:], 0.0)
 
-        def load_tab_scales(a, r):
-            row = SCALE_ROW[a] + r
-            nc.sync.dma_start(tab_s[row:P:32, :].bitcast(I32), tab_scales[a, r:16:4, :].bitcast(I32))
+        def load_tab_scales(a, q):
+            row = 32 * q + SCALE_ROW[a]
+            nc.sync.dma_start(tab_s[row : row + 4, :].bitcast(I32), tab_scales[a, 4 * q : 4 * q + 4, :].bitcast(I32))
 
-        def load_w2_scales(r):
-            nc.sync.dma_start(w2_s_raw[r:P:32, :].bitcast(I32), w2_scales[0, r:16:4, :].bitcast(I32))
+        def load_w2_scales(q):
+            nc.sync.dma_start(
+                w2_s_raw[32 * q : 32 * q + 4, :].bitcast(I32), w2_scales[0, 4 * q : 4 * q + 4, :].bitcast(I32)
+            )
 
         idx = keep.tile([P, S // 16], U16, name="idx")
         nc.sync.dma_start(idx[:], offs)
         tab0 = load_rows(tab_words[0].rearrange("p t i -> p (t i)").bitcast(I32), I32, "tab0")
-        runs = [(a, r) for r in range(4) for a in range(2)]
+        runs = [(a, q + half) for q in range(2) for a in range(2) for half in (0, 2)]
         for a, r in runs[:5]:
             load_tab_scales(a, r)
         w1_raw = [load_k_first(w1[:, 0:512], "w1_raw0")]
@@ -81,8 +83,8 @@ def tile_list_transformer_overload_board_kernel(
         tabs = [tab0, tab1]
         w2_raw = head.tile([P, 2 * H], U8, name="w2_raw", align_bytes=64, offset=H)
         nc.sync.dma_start(w2_raw[:].bitcast(I32), w2_words[0].bitcast(I32))
-        for r in range(4):
-            load_w2_scales(r)
+        for q in (0, 2, 1, 3):
+            load_w2_scales(q)
         wgs_sb = keep.tile([P, S], F32, name="wgs_sb")
         nc.sync.dma_start(wgs_sb[:], wgs)
         idx2 = keep.tile([P, S // 16], U16, name="idx2")

@@ -27,7 +27,6 @@ CHUNKS = T2 // BANK
 N_TILES = N // P
 SLICES = 8
 FIRST = 256
-BLOCK = 3 * BANK + 2048
 SCALE_ROW = (4, 0)
 PAGE_OF = (0, 1, 2, 0, 1, 2, 0, 1)
 
@@ -229,10 +228,11 @@ def tile_list_transformer_overload_board_kernel(
         z_slot = {}
 
         def times_gain(k):
+            chunks = slice(0, CHUNKS - 1 if k == SLICES - 2 else CHUNKS)
             nc.gpsimd.tensor_tensor(
-                z_slot[k],
-                pages[PAGE_OF[k]][:].rearrange("p (c m) -> p c m", c=CHUNKS),
-                gains[k][:].rearrange("p (c m) -> p c m", c=CHUNKS),
+                z_slot[k][:, chunks, :],
+                pages[PAGE_OF[k]][:].rearrange("p (c m) -> p c m", c=CHUNKS)[:, chunks, :],
+                gains[k][:].rearrange("p (c m) -> p c m", c=CHUNKS)[:, chunks, :],
                 MULT,
             )
 
@@ -282,7 +282,7 @@ def tile_list_transformer_overload_board_kernel(
         stage1(3, (1,))
         for k in range(4, SLICES):
             stage1(k)
-        zone = keep.tile([P, CHUNKS, BLOCK], BF16, name="zone", align_bytes=64)
+        planes = keep.tile([P, PACK * T2 + 2 * BANK], BF16, name="planes", align_bytes=64)
         w3_bf = [keep.tile([P, 2048], BF16, name="w3_bf", tag="w3_bf%d" % b, align_bytes=64)[:] for b in range(2)]
         for b in range(2):
             cast_w3(b, w3_bf[b])
@@ -290,15 +290,14 @@ def tile_list_transformer_overload_board_kernel(
         z_pairs = arena.tile([P, 4 * T2], BF16, name="z_pairs", align_bytes=64, offset=2048)
         for t in range(PACK):
             z_slot[t] = z_pairs[:].rearrange("p (c u m e) -> p c u m e", c=CHUNKS, u=2, e=2)[:, :, t // 2, :, t % 2]
-            z_slot[PACK + t] = zone[:, :, t * BANK : (t + 1) * BANK]
+            z_slot[PACK + t] = planes[:, t * T2 : (t + 1) * T2].rearrange("p (c m) -> p c m", c=CHUNKS)
         z_words = {
             (b, c): keep.tile([P, 2048], BF16, name="z_words", tag="z_words%d%d" % (b, c), align_bytes=64)[:]
             for b in range(2)
             for c in range(CHUNKS)
-            if (b, c) not in ((1, 0), (1, 1))
+            if (b, c) not in ((1, 0), (1, 3))
         }
-        for c in range(2):
-            z_words[1, c] = zone[:, c + 2, 3 * BANK : BLOCK]
+        z_words[1, 0] = planes[:, 3 * T2 + 2 * BANK : PACK * T2 + 2 * BANK]
 
         def weave_pass0(c):
             nc.scalar.copy(
@@ -309,7 +308,7 @@ def tile_list_transformer_overload_board_kernel(
         def weave_pass1(c, ts):
             nc.scalar.copy(
                 z_words[1, c].rearrange("p (m i t) -> p m t i", i=4, t=PACK)[:, :, ts, :],
-                zone[:, c, 0 : PACK * BANK].rearrange("p (t m i) -> p m t i", t=PACK, i=4)[:, :, ts, :],
+                planes[:, 0 : PACK * T2].rearrange("p (t c m i) -> p c m t i", t=PACK, c=CHUNKS, i=4)[:, c, :, ts, :],
             )
 
         for k in range(1, SLICES):
@@ -323,12 +322,13 @@ def tile_list_transformer_overload_board_kernel(
                 for c in range(CHUNKS):
                     weave_pass0(c)
             if k == 6:
-                weave_pass1(0, slice(0, 2))
+                for c in range(CHUNKS - 1):
+                    weave_pass1(c, slice(0, 2))
 
         def last_gain(c, engine):
             cols = slice(c * BANK, (c + 1) * BANK)
             engine.tensor_tensor(z_slot[7][:, c, :], pages[PAGE_OF[7]][:, cols], last_gains[c], MULT)
-            weave_pass1(c, slice(2, PACK) if c == 0 else slice(0, PACK))
+            weave_pass1(c, slice(2, PACK))
 
         def add_and_store(c, i):
             res = ambs[c][:, i, :]
@@ -354,13 +354,21 @@ def tile_list_transformer_overload_board_kernel(
         products(0, 1, "w3_bf1")
         last_gain(2, nc.vector)
         products(0, 2, "z_words01")
-        for c in range(CHUNKS):
-            add_and_store(c, 0)
-            if c == 0:
-                products(0, 3, "z_words02")
-            if c + 1 < CHUNKS:
-                products(1, c + 1, "h%d" % (c + 3))
-            if c == 0:
-                last_gain(3, nc.gpsimd)
-            for i in range(1, N_TILES):
-                add_and_store(c, i)
+        add_and_store(0, 0)
+        products(0, 3, "z_words02")
+        products(1, 1, "h4")
+        add_and_store(0, 1)
+        add_and_store(0, 2)
+        products(1, 2, "h5")
+        last = CHUNKS - 1
+        cols = slice(last * BANK, T2)
+        z_last = keep.tile([P, 2048], BF16, name="z_words", tag="z_words12", align_bytes=64)
+        z_words[1, last] = z_last[:]
+        for k, gain_k in ((6, gains[6][:, cols]), (7, last_gains[last])):
+            dst = z_last[:].rearrange("p (m t) -> p m t", t=PACK)[:, :, k - PACK]
+            nc.gpsimd.tensor_tensor(dst, pages[PAGE_OF[k]][:, cols], gain_k, MULT)
+        weave_pass1(last, slice(0, 2))
+        for c, i in [(0, 3)] + [(c, i) for c in range(1, CHUNKS) for i in range(N_TILES)]:
+            if (c, i) == (2, 2):
+                products(1, last, "h6")
+            add_and_store(c, i)

@@ -39,7 +39,6 @@ def tile_list_transformer_overload_board_kernel(
         keep = ctx.enter_context(tc.tile_pool(name="keep", bufs=1))
         stage = ctx.enter_context(tc.tile_pool(name="stage", bufs=6))
         arena = ctx.enter_context(tc.tile_pool(name="arena", bufs=1))
-        head = ctx.enter_context(tc.tile_pool(name="head", bufs=1))
         psum = ctx.enter_context(tc.psum_pool(name="psum", bufs=1))
 
         def load_rows(src, dtype, name):
@@ -53,42 +52,44 @@ def tile_list_transformer_overload_board_kernel(
             return t
 
         tab_s = keep.tile([P, T], U8, name="tab_s", align_bytes=64)
-        w2_s_raw = head.tile([P, H], U8, name="w2_s_raw", align_bytes=64, offset=0)
+        w2_s_raw = keep.tile([P, H], U8, name="w2_s_raw", align_bytes=64)
         nc.gpsimd.memset(tab_s[:].bitcast(I32), 0)
         nc.gpsimd.memset(w2_s_raw[:].bitcast(I32), 0)
         pages = [keep.tile([P, T2], F32, name="page%d" % i) for i in range(3)]
         for page in pages:
             nc.gpsimd.memset(page[:], 0.0)
 
-        def load_tab_scales(a, q):
+        def load_tab_scales(run):
+            a, q = divmod(run, 4)
             row = 32 * q + SCALE_ROW[a]
-            nc.sync.dma_start(tab_s[row : row + 4, :].bitcast(I32), tab_scales[a, 4 * q : 4 * q + 4, :].bitcast(I32))
+            nc.sync.dma_start(
+                tab_s[row : row + 4, :].bitcast(I32),
+                tab_scales[a, 4 * q : 4 * q + 4, :].bitcast(I32),
+            )
 
         def load_w2_scales(q):
             nc.sync.dma_start(
-                w2_s_raw[32 * q : 32 * q + 4, :].bitcast(I32), w2_scales[0, 4 * q : 4 * q + 4, :].bitcast(I32)
+                w2_s_raw[32 * q : 32 * q + 4, :].bitcast(I32),
+                w2_scales[0, 4 * q : 4 * q + 4, :].bitcast(I32),
             )
 
         idx = keep.tile([P, S // 16], U16, name="idx")
         nc.sync.dma_start(idx[:], offs)
         tab0 = load_rows(tab_words[0].rearrange("p t i -> p (t i)").bitcast(I32), I32, "tab0")
-        runs = [(a, q + half) for q in range(2) for a in range(2) for half in (0, 2)]
-        for a, r in runs[:5]:
-            load_tab_scales(a, r)
+        for run in range(8):
+            load_tab_scales(run)
         w1_raw = [load_k_first(w1[:, 0:512], "w1_raw0")]
-        for a, r in runs[5:]:
-            load_tab_scales(a, r)
+        w2_raw = keep.tile([P, 2 * H], U8, name="w2_raw")
+        nc.sync.dma_start(w2_raw[:].bitcast(I32), w2_words[0].bitcast(I32))
+        for q in range(4):
+            load_w2_scales(q)
         tab1 = load_rows(tab_words[1].rearrange("p t i -> p (t i)").bitcast(I32), I32, "tab1")
         tabs = [tab0, tab1]
-        w2_raw = head.tile([P, 2 * H], U8, name="w2_raw", align_bytes=64, offset=H)
-        nc.sync.dma_start(w2_raw[:].bitcast(I32), w2_words[0].bitcast(I32))
-        for q in (0, 2, 1, 3):
-            load_w2_scales(q)
         wgs_sb = keep.tile([P, S], F32, name="wgs_sb")
         nc.sync.dma_start(wgs_sb[:], wgs)
         idx2 = keep.tile([P, S // 16], U16, name="idx2")
         nc.sync.dma_start(idx2[:], offs2)
-        w1_raw1 = arena.tile([P, PACK, 512], F32, name="w1_raw1", align_bytes=64, offset=4096)
+        w1_raw1 = arena.tile([P, PACK, 512], F32, name="w1_raw1", align_bytes=64, offset=0)
         nc.sync.dma_start(w1_raw1[:], w1[:, 512:1024].rearrange("(p j) c -> p j c", j=PACK))
         w1_raw.append(w1_raw1)
 
@@ -136,8 +137,23 @@ def tile_list_transformer_overload_board_kernel(
             )
 
         words0 = keep.tile([P, S], U32, name="words0", align_bytes=64)
+        g_scales = keep.tile([P, S], U8, name="g_scales", align_bytes=64)
         w2_p = keep.tile([P, 2 * H], U8, name="w2_p", align_bytes=64)
         w2_s = keep.tile([P, H], U8, name="w2_s", align_bytes=64)
+
+        w1_bf0 = [keep.tile([P, 1024], BF16, name="w1_bf0", tag="w1_then_words%d" % u, align_bytes=64) for u in range(2)]
+        for u in range(2):
+            cast_w1(0, w1_bf0[u][:], slice(2 * u, 2 * u + 2))
+        nc.vector.tensor_copy(words0[:], tabs[0][:].bitcast(U32).indirect(idx[:]))
+        nc.vector.tensor_copy(g_scales[:], tab_s[:].indirect(idx[:]))
+        nc.vector.tensor_copy(
+            w2_p[:].bitcast(U16).rearrange("p (b t m) -> p b t m", b=2, t=PACK),
+            w2_raw[:].bitcast(U16).rearrange("p (b m t) -> p b t m", b=2, t=PACK),
+        )
+        nc.vector.tensor_copy(
+            w2_s[:].rearrange("p (b t m) -> p b t m", b=2, t=PACK),
+            w2_s_raw[:].rearrange("p (b m t) -> p b t m", b=2, t=PACK),
+        )
         w1_codes = keep.tile([P, H], U32, name="w1_codes", align_bytes=64)
         w1_scales = keep.tile([P, H], U8, name="w1_scales", align_bytes=64)
 
@@ -145,36 +161,16 @@ def tile_list_transformer_overload_board_kernel(
             cols = slice(col, col + src.shape[1] // PACK)
             nc.vector.quantize_mx(out=w1_codes[:, cols].bitcast(FP8X4), scales=w1_scales[:, cols], in_=src)
 
-        def deal_w2(b):
-            cols = slice(b * 512, (b + 1) * 512)
-            nc.vector.tensor_copy(
-                w2_p[:].bitcast(U16)[:, cols].rearrange("p (t u m) -> p u t m", t=PACK, u=2),
-                w2_raw[:].bitcast(U16)[:, cols].rearrange("p (u m t) -> p u t m", t=PACK, u=2),
-            )
-            nc.vector.tensor_copy(
-                w2_s[:, cols].rearrange("p (t u m) -> p u t m", t=PACK, u=2),
-                w2_s_raw[:, cols].rearrange("p (u m t) -> p u t m", t=PACK, u=2),
-            )
-
-        def gather(dst, window, jh):
-            nc.vector.tensor_copy(dst[:], window.indirect(idx[:, jh * BANK // 16 : (jh + 1) * BANK // 16]))
-
-        w1_bf0 = [keep.tile([P, 1024], BF16, name="w1_bf0", tag="w1_then_words%d" % u, align_bytes=64) for u in range(2)]
-        for u in range(2):
-            cast_w1(0, w1_bf0[u][:], slice(2 * u, 2 * u + 2))
-        nc.vector.tensor_copy(words0[:], tabs[0][:].bitcast(U32).indirect(idx[:]))
-        g_scales = [keep.tile([P, BANK], U8, name="g_scales0", align_bytes=64)]
-        gather(g_scales[0], tab_s[:], 0)
-        quantize_w1(w1_bf0[0][:], 0)
-        words1 = [keep.tile([P, BANK], U32, name="words1_low", align_bytes=64)]
-        gather(words1[0], tabs[1][:].bitcast(U32), 0)
-        deal_w2(0)
-        quantize_w1(w1_bf0[1][:], 256)
-        deal_w2(1)
-        g_scales.append(head.tile([P, BANK], U8, name="g_scales1", align_bytes=64, offset=0))
-        gather(g_scales[1], tab_s[:], 1)
-        words1.append(head.tile([P, BANK], U32, name="words1_high", align_bytes=64, offset=BANK))
-        gather(words1[1], tabs[1][:].bitcast(U32), 1)
+        words1 = []
+        for jh in range(HALVES):
+            quantize_w1(w1_bf0[jh][:], 256 * jh)
+            words1.append(keep.tile([P, BANK], U32, name="words1", tag="w1_then_words%d" % jh, align_bytes=64))
+            for lo in range(0, BANK, FIRST if jh == 0 else BANK):
+                js = slice(jh * BANK + lo, jh * BANK + lo + (FIRST if jh == 0 else BANK))
+                nc.vector.tensor_copy(
+                    words1[jh][:, lo : lo + js.stop - js.start],
+                    tabs[1][:].bitcast(U32).indirect(idx[:, js.start // 16 : js.stop // 16]),
+                )
 
         hs = {}
         raw = {}
@@ -190,7 +186,7 @@ def tile_list_transformer_overload_board_kernel(
                 lhsT=w1_codes[:, col : col + P].bitcast(FP8X4),
                 lhsT_scale=w1_scales[:, col : col + P],
                 rhs=words0[:, js].bitcast(FP8X4),
-                rhs_scale=g_scales[jh][SCALE_ROW[0] : P, lo : lo + width],
+                rhs_scale=g_scales[SCALE_ROW[0] : P, js],
                 start=True,
                 stop=False,
             )
@@ -201,7 +197,7 @@ def tile_list_transformer_overload_board_kernel(
                     lhsT=w2_p[:, 2 * col : 2 * (col + P)].bitcast(FP4X4),
                     lhsT_scale=w2_s[:, col : col + P],
                     rhs=words1[jh][:, lo + n0 : lo + n0 + step].bitcast(FP8X4),
-                    rhs_scale=g_scales[jh][SCALE_ROW[1] : P, lo + n0 : lo + n0 + step],
+                    rhs_scale=g_scales[SCALE_ROW[1] : P, js.start + n0 : js.start + n0 + step],
                     start=False,
                     stop=(n0 + step == width),
                 )
@@ -218,8 +214,9 @@ def tile_list_transformer_overload_board_kernel(
         def weigh(k):
             nc.gpsimd.tensor_tensor(hs[k][:], hs[k][:], wgs_sb[:], MULT)
 
-        def weigh_part(k, js, src):
-            nc.gpsimd.tensor_tensor(hs[k][:, js], src, wgs_sb[:, js], MULT)
+        def weigh_half(k, jh):
+            js = slice(jh * BANK, (jh + 1) * BANK)
+            nc.gpsimd.tensor_tensor(hs[k][:, js], raw[k, jh], wgs_sb[:, js], MULT)
 
         def scatter(k, js=slice(0, S)):
             offsets = idx2[:, js.start // 16 : js.stop // 16]
@@ -253,33 +250,27 @@ def tile_list_transformer_overload_board_kernel(
                 stop=(b == 1),
             )
 
-        low, high = slice(0, BANK), slice(BANK, S)
         hs[0] = keep.tile([P, S], F32, name="h", tag="h0", align_bytes=64)
-        first_pieces = [slice(0, FIRST), slice(FIRST, BANK)]
+        first_pieces = [slice(0, FIRST), slice(FIRST, BANK), slice(BANK, S)]
         for bank, js in enumerate(first_pieces):
             heat(0, js, bank, hs[0][:, js])
-            weigh_part(0, js, hs[0][:, js])
-            scatter(0, js)
-        for k in (1, 2):
+        for k in (1, 2, 3):
             stage1(k, (0,))
-            weigh_part(k, low, raw[k, 0])
-        w1_bf1 = arena.tile([P, 2048], BF16, name="w1_bf1", align_bytes=64, offset=0)
-        cast_w1(1, w1_bf1[:, 0:1024], slice(0, 2))
-        heat(0, high, 2, hs[0][:, high])
-        weigh_part(0, high, hs[0][:, high])
-        scatter(0, high)
-        stage1(3, (0,))
-        weigh_part(3, low, raw[3, 0])
-        cast_w1(1, w1_bf1[:, 1024:2048], slice(2, PACK))
-        for k in (1, 2):
-            late = arena.tile([P, BANK], F32, name="late%d" % k, align_bytes=64, offset=2048 * (k + 1))
-            raw[k, 1] = late[:]
+        w1_bf1 = arena.tile([P, 2048], BF16, name="w1_bf1", align_bytes=64, offset=8192)
+        cast_w1(1, w1_bf1[:], slice(0, PACK))
+        late = arena.tile([P, 3, BANK], F32, name="late", align_bytes=64, offset=2048)
+        for k in (1, 2, 3):
+            raw[k, 1] = late[:, k - 1, :]
             stage1(k, (1,))
-            weigh_part(k, high, raw[k, 1])
+        for jh, engine in enumerate((nc.vector, nc.gpsimd)):
+            js = slice(jh * BANK, (jh + 1) * BANK)
+            engine.tensor_tensor(hs[0][:, js], hs[0][:, js], wgs_sb[:, js], MULT)
+            scatter(0, js)
+        for k in (1, 2, 3):
+            weigh_half(k, 0)
         quantize_w1(w1_bf1[:], 512)
-        late3 = arena.tile([P, BANK], F32, name="late3", align_bytes=64, offset=0)
-        raw[3, 1] = late3[:]
-        stage1(3, (1,))
+        for k in (1, 2, 3):
+            weigh_half(k, 1)
         for k in range(4, SLICES):
             stage1(k)
         planes = keep.tile([P, PACK * T2 + 2 * BANK], BF16, name="planes", align_bytes=64)
@@ -287,7 +278,7 @@ def tile_list_transformer_overload_board_kernel(
         for b in range(2):
             cast_w3(b, w3_bf[b])
 
-        z_pairs = arena.tile([P, 4 * T2], BF16, name="z_pairs", align_bytes=64, offset=2048)
+        z_pairs = arena.tile([P, 4 * T2], BF16, name="z_pairs", align_bytes=64, offset=4096)
         for t in range(PACK):
             z_slot[t] = z_pairs[:].rearrange("p (c u m e) -> p c u m e", c=CHUNKS, u=2, e=2)[:, :, t // 2, :, t % 2]
             z_slot[PACK + t] = planes[:, t * T2 : (t + 1) * T2].rearrange("p (c m) -> p c m", c=CHUNKS)
@@ -314,8 +305,6 @@ def tile_list_transformer_overload_board_kernel(
         for k in range(1, SLICES):
             scatter(k)
             times_gain(k - 1)
-            if k == 1:
-                weigh_part(3, high, raw[3, 1])
             if k + 3 < SLICES:
                 weigh(k + 3)
             if k == 4:

@@ -273,22 +273,25 @@ def tile_list_transformer_overload_board_kernel(
             weigh_half(k, 1)
         for k in range(4, SLICES):
             stage1(k)
-        planes = keep.tile([P, PACK * T2 + 2 * BANK], BF16, name="planes", align_bytes=64)
-        w3_bf = [keep.tile([P, 2048], BF16, name="w3_bf", tag="w3_bf%d" % b, align_bytes=64)[:] for b in range(2)]
+        z_low = keep.tile([P, 2, T2], BF16, name="z_low", align_bytes=64)
+        z_high = keep.tile([P, 5 * BANK + 2048], BF16, name="z_high", align_bytes=64)
+        w3_bf1 = keep.tile([P, 2048], BF16, name="w3_bf1", tag="w3_bf1", align_bytes=64)
+        w3_bf = [z_high[:, 5 * BANK : 5 * BANK + 2048], w3_bf1[:]]
         for b in range(2):
             cast_w3(b, w3_bf[b])
 
         z_pairs = arena.tile([P, 4 * T2], BF16, name="z_pairs", align_bytes=64, offset=4096)
         for t in range(PACK):
             z_slot[t] = z_pairs[:].rearrange("p (c u m e) -> p c u m e", c=CHUNKS, u=2, e=2)[:, :, t // 2, :, t % 2]
-            z_slot[PACK + t] = planes[:, t * T2 : (t + 1) * T2].rearrange("p (c m) -> p c m", c=CHUNKS)
+        for t in range(2):
+            z_slot[4 + t] = z_low[:, t, :].rearrange("p (c m) -> p c m", c=CHUNKS)
+            z_slot[6 + t] = z_high[:, 0 : 6 * BANK].rearrange("p (c t m) -> p c t m", t=2, m=BANK)[:, :, t, :]
         z_words = {
             (b, c): keep.tile([P, 2048], BF16, name="z_words", tag="z_words%d%d" % (b, c), align_bytes=64)[:]
             for b in range(2)
             for c in range(CHUNKS)
-            if (b, c) not in ((1, 0), (1, 3))
+            if (b, c) != (1, CHUNKS - 1)
         }
-        z_words[1, 0] = planes[:, 3 * T2 + 2 * BANK : PACK * T2 + 2 * BANK]
 
         def weave_pass0(c):
             nc.scalar.copy(
@@ -296,11 +299,17 @@ def tile_list_transformer_overload_board_kernel(
                 z_pairs[:, c * 2048 : (c + 1) * 2048].bitcast(F32).rearrange("p (u m) -> p m u", u=2),
             )
 
-        def weave_pass1(c, ts):
+        def place_pair(c, u, rows):
             nc.scalar.copy(
-                z_words[1, c].rearrange("p (m i t) -> p m t i", i=4, t=PACK)[:, :, ts, :],
-                planes[:, 0 : PACK * T2].rearrange("p (t c m i) -> p c m t i", t=PACK, c=CHUNKS, i=4)[:, c, :, ts, :],
+                z_words[1, c].rearrange("p (m i t) -> p m t i", i=4, t=PACK)[:, :, 2 * u : 2 * u + 2, :],
+                rows.rearrange("p t (m i) -> p m t i", i=4),
             )
+
+        def place_low(c):
+            place_pair(c, 0, z_low[:, :, c * BANK : (c + 1) * BANK])
+
+        def place_high(c):
+            place_pair(c, 1, z_high[:, 2 * c * BANK : 2 * (c + 1) * BANK].rearrange("p (t m) -> p t m", t=2))
 
         for k in range(1, SLICES):
             scatter(k)
@@ -312,12 +321,12 @@ def tile_list_transformer_overload_board_kernel(
                     weave_pass0(c)
             if k == 6:
                 for c in range(CHUNKS - 1):
-                    weave_pass1(c, slice(0, 2))
+                    place_low(c)
 
         def last_gain(c, engine):
             cols = slice(c * BANK, (c + 1) * BANK)
             engine.tensor_tensor(z_slot[7][:, c, :], pages[PAGE_OF[7]][:, cols], last_gains[c], MULT)
-            weave_pass1(c, slice(2, PACK))
+            place_high(c)
 
         def add_and_store(c, i):
             res = ambs[c][:, i, :]
@@ -338,26 +347,24 @@ def tile_list_transformer_overload_board_kernel(
         last_gain(1, nc.vector)
         quantize_w3(0, "last_gain0")
         products(0, 0, "last_gain1")
-        quantize_w3(1, "w3_bf0")
+        last_gain(2, nc.vector)
+        quantize_w3(1, "z_words00")
         products(1, 0, "h0")
         products(0, 1, "w3_bf1")
-        last_gain(2, nc.vector)
-        products(0, 2, "z_words01")
+        products(0, 2, "z_words10")
+        products(0, 3, "z_words01")
         add_and_store(0, 0)
-        products(0, 3, "z_words02")
         products(1, 1, "h4")
-        add_and_store(0, 1)
-        add_and_store(0, 2)
         products(1, 2, "h5")
         last = CHUNKS - 1
         cols = slice(last * BANK, T2)
-        z_last = keep.tile([P, 2048], BF16, name="z_words", tag="z_words12", align_bytes=64)
-        z_words[1, last] = z_last[:]
-        for k, gain_k in ((6, gains[6][:, cols]), (7, last_gains[last])):
-            dst = z_last[:].rearrange("p (m t) -> p m t", t=PACK)[:, :, k - PACK]
-            nc.gpsimd.tensor_tensor(dst, pages[PAGE_OF[k]][:, cols], gain_k, MULT)
-        weave_pass1(last, slice(0, 2))
-        for c, i in [(0, 3)] + [(c, i) for c in range(1, CHUNKS) for i in range(N_TILES)]:
+        z_last = keep.tile([P, 2, BANK], BF16, name="z_last", tag="z_words12", align_bytes=64)
+        for t, gain_k in enumerate((gains[SLICES - 2][:, cols], last_gains[last])):
+            nc.gpsimd.tensor_tensor(z_last[:, t, :], pages[PAGE_OF[SLICES - 2 + t]][:, cols], gain_k, MULT)
+        z_words[1, last] = keep.tile([P, 2048], BF16, name="z_words", tag="z_words02", align_bytes=64)[:]
+        place_low(last)
+        place_pair(last, 1, z_last[:])
+        for c, i in [(c, i) for c in range(CHUNKS) for i in range(N_TILES)][1:]:
             if (c, i) == (2, 2):
                 products(1, last, "h6")
             add_and_store(c, i)

@@ -331,7 +331,12 @@ def tile_list_transformer_overload_board_kernel(
         def add_and_store(c, i):
             res = ambs[c][:, i, :]
             nc.vector.tensor_tensor(res, y_acc[c, i][:], res, ADD)
-            nc.sync.dma_start(out[i * P : (i + 1) * P, c * BANK : (c + 1) * BANK], res)
+            cols = slice(c * BANK, (c + 1) * BANK)
+            if c == CHUNKS - 1 and i >= 2:
+                nc.sync.dma_start(out[i * P : (i + 1) * P, cols], res)
+            elif i % 2 == 1:
+                rows = out[(i - 1) * P : (i + 1) * P, cols].rearrange("(i p) m -> p i m", p=P)
+                nc.sync.dma_start(rows, ambs[c][:, i - 1 : i + 1, :])
 
         def products(b, c, tag):
             codes, scales = quantize(z_words[b, c], "zq%d%d" % (b, c), tag)

@@ -251,10 +251,15 @@ def tile_list_transformer_overload_board_kernel(
             )
 
         hs[0] = keep.tile([P, S], F32, name="h", tag="h0", align_bytes=64)
-        first_pieces = [slice(0, FIRST), slice(FIRST, BANK), slice(BANK, S)]
-        for bank, js in enumerate(first_pieces):
-            heat(0, js, bank, hs[0][:, js])
-        for k in (1, 2, 3):
+        low, high = slice(0, BANK), slice(BANK, S)
+        raw0 = keep.tile([P, BANK], F32, name="raw0", tag="h1", align_bytes=64)
+        for bank, js in enumerate((slice(0, FIRST), slice(FIRST, BANK))):
+            heat(0, js, bank, raw0[:, js])
+        raw1 = keep.tile([P, BANK], F32, name="raw1", align_bytes=64)
+        raw[1, 0] = raw1[:]
+        stage1(1, (0,))
+        heat(0, high, 2, hs[0][:, high])
+        for k in (2, 3):
             stage1(k, (0,))
         w1_bf1 = arena.tile([P, 2048], BF16, name="w1_bf1", align_bytes=64, offset=8192)
         cast_w1(1, w1_bf1[:], slice(0, PACK))
@@ -262,11 +267,14 @@ def tile_list_transformer_overload_board_kernel(
         for k in (1, 2, 3):
             raw[k, 1] = late[:, k - 1, :]
             stage1(k, (1,))
-        for jh, engine in enumerate((nc.vector, nc.gpsimd)):
-            js = slice(jh * BANK, (jh + 1) * BANK)
-            engine.tensor_tensor(hs[0][:, js], hs[0][:, js], wgs_sb[:, js], MULT)
-            scatter(0, js)
-        for k in (1, 2, 3):
+        nc.vector.tensor_tensor(hs[0][:, low], raw0[:], wgs_sb[:, low], MULT)
+        scatter(0, low)
+        weigh_half(1, 0)
+        scatter(1, low)
+        raw[0, 1] = hs[0][:, high]
+        weigh_half(0, 1)
+        scatter(0, high)
+        for k in (2, 3):
             weigh_half(k, 0)
         quantize_w1(w1_bf1[:], 512)
         for k in (1, 2, 3):
@@ -312,7 +320,7 @@ def tile_list_transformer_overload_board_kernel(
             place_pair(c, 1, z_high[:, 2 * c * BANK : 2 * (c + 1) * BANK].rearrange("p (t m) -> p t m", t=2))
 
         for k in range(1, SLICES):
-            scatter(k)
+            scatter(k, high if k == 1 else slice(0, S))
             times_gain(k - 1)
             if k + 3 < SLICES:
                 weigh(k + 3)
@@ -332,9 +340,7 @@ def tile_list_transformer_overload_board_kernel(
             res = ambs[c][:, i, :]
             nc.vector.tensor_tensor(res, y_acc[c, i][:], res, ADD)
             cols = slice(c * BANK, (c + 1) * BANK)
-            if c == CHUNKS - 1 and i >= 2:
-                nc.sync.dma_start(out[i * P : (i + 1) * P, cols], res)
-            elif i % 2 == 1:
+            if i % 2 == 1:
                 rows = out[(i - 1) * P : (i + 1) * P, cols].rearrange("(i p) m -> p i m", p=P)
                 nc.sync.dma_start(rows, ambs[c][:, i - 1 : i + 1, :])
 

@@ -76,14 +76,19 @@ def tile_list_transformer_overload_board_kernel(
         idx = keep.tile([P, S // 16], U16, name="idx")
         nc.sync.dma_start(idx[:], offs)
         tab0 = load_rows(tab_words[0].rearrange("p t i -> p (t i)").bitcast(I32), I32, "tab0")
-        for run in range(8):
+        tab1 = stage.tile([P, T], I32, name="tab1", tag="rows")
+        tab1_src = tab_words[1].rearrange("p t i -> p (t i)").bitcast(I32)
+        for run in range(5):
+            load_tab_scales(run)
+        nc.sync.dma_start(tab1[:, 0 : T // 2], tab1_src[:, 0 : T // 2])
+        for run in range(5, 8):
             load_tab_scales(run)
         w1_raw = [load_k_first(w1[:, 0:512], "w1_raw0")]
         w2_raw = keep.tile([P, 2 * H], U8, name="w2_raw")
         nc.sync.dma_start(w2_raw[:].bitcast(I32), w2_words[0].bitcast(I32))
         for q in range(4):
             load_w2_scales(q)
-        tab1 = load_rows(tab_words[1].rearrange("p t i -> p (t i)").bitcast(I32), I32, "tab1")
+        nc.sync.dma_start(tab1[:, T // 2 : T], tab1_src[:, T // 2 : T])
         tabs = [tab0, tab1]
         wgs_sb = keep.tile([P, S], F32, name="wgs_sb")
         nc.sync.dma_start(wgs_sb[:], wgs)
@@ -106,7 +111,7 @@ def tile_list_transformer_overload_board_kernel(
                     g_sb = keep.tile([P, BANK], F32, name="last_gain", tag="last_gain%d" % c, align_bytes=64)
                     nc.sync.dma_start(g_sb[:], rows[:, c * BANK : (c + 1) * BANK])
                     last_gains.append(g_sb[:])
-                gain_rest = stage.tile([P, 2, BANK], F32, name="gain_rest", tag="rows")
+                gain_rest = keep.tile([P, 2, BANK], F32, name="gain_rest", tag="gain_rest", align_bytes=64)
                 nc.sync.dma_start(gain_rest[:], rows[:, 2 * BANK : T2].rearrange("p (c m) -> p c m", c=2))
                 last_gains.extend(gain_rest[:, c, :] for c in range(2))
             if k == 5:
@@ -363,9 +368,8 @@ def tile_list_transformer_overload_board_kernel(
         products(1, 0, "h0")
         products(0, 1, "w3_bf1")
         products(0, 2, "z_words10")
-        products(0, 3, "z_words01")
-        add_and_store(0, 0)
         products(1, 1, "h4")
+        add_and_store(0, 0)
         products(1, 2, "h5")
         last = CHUNKS - 1
         cols = slice(last * BANK, T2)
@@ -376,6 +380,8 @@ def tile_list_transformer_overload_board_kernel(
         place_low(last)
         place_pair(last, 1, z_last[:])
         for c, i in [(c, i) for c in range(CHUNKS) for i in range(N_TILES)][1:]:
+            if (c, i) == (1, 3):
+                products(0, last, "gain_rest")
             if (c, i) == (2, 2):
                 products(1, last, "h6")
             add_and_store(c, i)

@@ -272,8 +272,10 @@ def tile_list_transformer_overload_board_kernel(
         for k in (1, 2, 3):
             raw[k, 1] = late[:, k - 1, :]
             stage1(k, (1,))
-        nc.vector.tensor_tensor(hs[0][:, low], raw0[:], wgs_sb[:, low], MULT)
-        scatter(0, low)
+        for js in (slice(0, FIRST), slice(FIRST, BANK)):
+            nc.vector.tensor_tensor(hs[0][:, js], raw0[:, js], wgs_sb[:, js], MULT)
+        for js in (slice(0, FIRST), slice(FIRST, BANK)):
+            scatter(0, js)
         weigh_half(1, 0)
         scatter(1, low)
         raw[0, 1] = hs[0][:, high]

@@ -1,6 +1,7 @@
 from contextlib import ExitStack
 
 import concourse.mybir as mybir
+from concourse.masks import make_identity
 
 K1, H, N, T, S, T2 = 512, 1024, 512, 2048, 1024, 2048
 FLOPS = 2 * (2 * K1) * H * S + 2 * H * N * T2
@@ -19,7 +20,6 @@ GELU = mybir.ActivationFunctionType.Gelu_apprx_tanh
 
 P = 128
 PACK = 4
-K_PASS = P * PACK
 BANK = 512
 BANKS = 8
 HALVES = S // BANK
@@ -29,6 +29,8 @@ SLICES = 8
 FIRST = 256
 SCALE_ROW = (4, 0)
 PAGE_OF = (0, 1, 2, 0, 1, 2, 0, 1)
+TURNED = 2 * P
+LAST = CHUNKS - 1
 
 
 def tile_list_transformer_overload_board_kernel(
@@ -52,7 +54,7 @@ def tile_list_transformer_overload_board_kernel(
             return t
 
         tab_s = keep.tile([P, T], U8, name="tab_s", align_bytes=64)
-        w2_s_raw = keep.tile([P, H], U8, name="w2_s_raw", align_bytes=64)
+        w2_s_raw = keep.tile([P, H], U8, name="w2_s_raw", tag="w2_s_raw", align_bytes=64)
         nc.gpsimd.memset(tab_s[:].bitcast(I32), 0)
         nc.gpsimd.memset(w2_s_raw[:].bitcast(I32), 0)
         pages = [keep.tile([P, T2], F32, name="page%d" % i) for i in range(3)]
@@ -101,6 +103,13 @@ def tile_list_transformer_overload_board_kernel(
         gain_rows = gain.rearrange("(b p j) m -> b j p m", b=2, j=PACK)
         gains = {}
         w3_raw = []
+        ambs = {}
+
+        def load_amb(c):
+            cols = slice(max(c * BANK, TURNED), (c + 1) * BANK)
+            ambs[c] = stage.tile([P, N_TILES, cols.stop - cols.start], F32, name="amb%d" % c, tag="rows")
+            nc.sync.dma_start(ambs[c][:], amb[:, cols].rearrange("(i p) m -> p i m", p=P))
+
         for k in range(SLICES):
             rows = gain_rows[k // PACK, k % PACK]
             if k < SLICES - 1:
@@ -111,23 +120,23 @@ def tile_list_transformer_overload_board_kernel(
                     g_sb = keep.tile([P, BANK], F32, name="last_gain", tag="last_gain%d" % c, align_bytes=64)
                     nc.sync.dma_start(g_sb[:], rows[:, c * BANK : (c + 1) * BANK])
                     last_gains.append(g_sb[:])
-                gain_rest = keep.tile([P, 2, BANK], F32, name="gain_rest", tag="gain_rest", align_bytes=64)
+                gain_rest = arena.tile([P, 2, BANK], F32, name="gain_rest", align_bytes=64, offset=20480)
                 nc.sync.dma_start(gain_rest[:], rows[:, 2 * BANK : T2].rearrange("p (c m) -> p c m", c=2))
                 last_gains.extend(gain_rest[:, c, :] for c in range(2))
             if k == 5:
                 w3_raw.extend(load_k_first(w3[512 * b : 512 * (b + 1), :], "w3_raw%d" % b) for b in range(2))
-        ambs = []
+                amb_first = keep.tile([P, N_TILES, TURNED], F32, name="amb_first", align_bytes=64)
+                nc.sync.dma_start(amb_first[:], amb[:, 0:TURNED].rearrange("(i p) m -> p i m", p=P))
         for c in range(CHUNKS):
-            a_sb = stage.tile([P, N_TILES, BANK], F32, name="amb%d" % c, tag="rows")
-            nc.sync.dma_start(a_sb[:], amb[:, c * BANK : (c + 1) * BANK].rearrange("(i p) m -> p i m", p=P))
-            ambs.append(a_sb)
+            load_amb(c)
 
-        def quantize(src_bf16, name, tag="", pool=keep):
-            width = src_bf16.shape[1] // PACK
-            codes = pool.tile([P, width], U32, name=name + "_codes", tag=tag, align_bytes=64)
-            scales = pool.tile([P, width], U8, name=name + "_scales", align_bytes=64)
+        def quantize(src_bf16, name, codes):
+            scales = keep.tile([P, BANK], U8, name=name + "_scales", align_bytes=64)
             nc.vector.quantize_mx(out=codes[:].bitcast(FP8X4), scales=scales[:], in_=src_bf16)
-            return codes, scales
+            return codes[:], scales[:]
+
+        def codes_on(tag):
+            return keep.tile([P, BANK], U32, name="codes", tag=tag, align_bytes=64)
 
         def cast_w1(b, dst, ts):
             nc.scalar.copy(
@@ -159,6 +168,8 @@ def tile_list_transformer_overload_board_kernel(
             w2_s[:].rearrange("p (b t m) -> p b t m", b=2, t=PACK),
             w2_s_raw[:].rearrange("p (b m t) -> p b t m", b=2, t=PACK),
         )
+        ident = keep.tile([P, P], F32, name="ident", tag="w2_s_raw", align_bytes=64)
+        make_identity(nc, ident[:])
         w1_codes = keep.tile([P, H], U32, name="w1_codes", align_bytes=64)
         w1_scales = keep.tile([P, H], U8, name="w1_scales", align_bytes=64)
 
@@ -180,12 +191,15 @@ def tile_list_transformer_overload_board_kernel(
         hs = {}
         raw = {}
 
+        def bank_tile(bank, name, shape=(P, BANK)):
+            return psum.tile(list(shape), F32, name=name, tag="bank%d" % bank)
+
         def heat(k, js, bank, dst):
             b, t = divmod(k, PACK)
             col = b * 512 + t * P
             width = js.stop - js.start
             jh, lo = divmod(js.start, BANK)
-            acc = psum.tile([P, BANK], F32, name="e_acc", tag="bank%d" % bank)
+            acc = bank_tile(bank, "e_acc")
             nc.tensor.matmul_mx(
                 out=acc[:, 0:width],
                 lhsT=w1_codes[:, col : col + P].bitcast(FP8X4),
@@ -195,17 +209,15 @@ def tile_list_transformer_overload_board_kernel(
                 start=True,
                 stop=False,
             )
-            step = BANK if width == BANK else P
-            for n0 in range(0, width, step):
-                nc.tensor.matmul_mx(
-                    out=acc[:, n0 : n0 + step],
-                    lhsT=w2_p[:, 2 * col : 2 * (col + P)].bitcast(FP4X4),
-                    lhsT_scale=w2_s[:, col : col + P],
-                    rhs=words1[jh][:, lo + n0 : lo + n0 + step].bitcast(FP8X4),
-                    rhs_scale=g_scales[SCALE_ROW[1] : P, js.start + n0 : js.start + n0 + step],
-                    start=False,
-                    stop=(n0 + step == width),
-                )
+            nc.tensor.matmul_mx(
+                out=acc[:, 0:width],
+                lhsT=w2_p[:, 2 * col : 2 * (col + P)].bitcast(FP4X4),
+                lhsT_scale=w2_s[:, col : col + P],
+                rhs=words1[jh][:, lo : lo + width].bitcast(FP8X4),
+                rhs_scale=g_scales[SCALE_ROW[1] : P, js],
+                start=False,
+                stop=True,
+            )
             nc.scalar.activation(dst, acc[:, 0:width], GELU)
 
         def stage1(k, jhs=(0, 1)):
@@ -229,30 +241,12 @@ def tile_list_transformer_overload_board_kernel(
 
         z_slot = {}
 
-        def times_gain(k):
-            chunks = slice(0, CHUNKS - 1 if k == SLICES - 2 else CHUNKS)
+        def times_gain(k, chunks):
             nc.gpsimd.tensor_tensor(
                 z_slot[k][:, chunks, :],
                 pages[PAGE_OF[k]][:].rearrange("p (c m) -> p c m", c=CHUNKS)[:, chunks, :],
                 gains[k][:].rearrange("p (c m) -> p c m", c=CHUNKS)[:, chunks, :],
                 MULT,
-            )
-
-        zq = {}
-        w3q = []
-        y_acc = {}
-
-        def stage2_pass(b, c, i):
-            if b == 0:
-                y_acc[c, i] = psum.tile([P, BANK], F32, name="y_acc", tag="bank%d" % ((N_TILES * c + i) % BANKS))
-            nc.tensor.matmul_mx(
-                out=y_acc[c, i][:],
-                lhsT=w3q[b][0][:, i * P : (i + 1) * P].bitcast(FP8X4),
-                lhsT_scale=w3q[b][1][:, i * P : (i + 1) * P],
-                rhs=zq[b, c][0].bitcast(FP8X4),
-                rhs_scale=zq[b, c][1],
-                start=(b == 0),
-                stop=(b == 1),
             )
 
         hs[0] = keep.tile([P, S], F32, name="h", tag="h0", align_bytes=64)
@@ -305,7 +299,6 @@ def tile_list_transformer_overload_board_kernel(
             (b, c): keep.tile([P, 2048], BF16, name="z_words", tag="z_words%d%d" % (b, c), align_bytes=64)[:]
             for b in range(2)
             for c in range(CHUNKS)
-            if (b, c) != (1, CHUNKS - 1)
         }
 
         def weave_pass0(c):
@@ -326,21 +319,89 @@ def tile_list_transformer_overload_board_kernel(
         def place_high(c):
             place_pair(c, 1, z_high[:, 2 * c * BANK : 2 * (c + 1) * BANK].rearrange("p (t m) -> p t m", t=2))
 
+        sums = {}
+
+        def turn_into_sums(src, first):
+            for mj in range(2):
+                for i in range(N_TILES):
+                    pair, ii = divmod(i, 2)
+                    if first and (mj, ii) == (0, 0):
+                        sums[pair] = bank_tile(6 + pair, "sum_acc", (P, 2, TURNED))
+                    nc.tensor.matmul(
+                        sums[pair][:, ii, mj * P : (mj + 1) * P],
+                        lhsT=src[:, mj, i * P : (i + 1) * P],
+                        rhs=ident[:],
+                        start=first and (mj, ii) == (0, 0),
+                        stop=not first and (mj, ii) == (1, 1),
+                        is_transpose=True,
+                    )
+
+        def turn_amb():
+            amb_t = keep.tile([P, 2, N], F32, name="amb_t", tag="h1", align_bytes=64)
+            for mj in range(2):
+                acc = bank_tile(4 + mj, "amb_acc")
+                for i in range(N_TILES):
+                    nc.tensor.transpose(acc[:, i * P : (i + 1) * P], amb_first[:, i, mj * P : (mj + 1) * P], ident[:])
+                nc.scalar.copy(amb_t[:, mj, :], acc[:])
+            turn_into_sums(amb_t, True)
+
         for k in range(1, SLICES):
             scatter(k, high if k == 1 else slice(0, S))
-            times_gain(k - 1)
+            if k - 1 == 5:
+                times_gain(5, slice(0, 2))
+                times_gain(5, slice(2, CHUNKS))
+            else:
+                times_gain(k - 1, slice(0, LAST if k - 1 == 6 else CHUNKS))
             if k + 3 < SLICES:
                 weigh(k + 3)
             if k == 4:
                 for c in range(CHUNKS):
                     weave_pass0(c)
+            if k == 5:
+                turn_amb()
             if k == 6:
-                for c in range(CHUNKS - 1):
+                for c in range(CHUNKS):
                     place_low(c)
 
-        def last_gain(c, engine):
+        zq = {}
+        w3q = []
+        y_acc = {}
+        banks_of = {1: (2, 3, 4, 5), 2: (0, 1, 6, 7), 3: (2, 3, 4, 5)}
+
+        def mx_pass(acc, lhs, lhs_cols, rhs, rhs_cols, start, stop):
+            nc.tensor.matmul_mx(
+                out=acc,
+                lhsT=lhs[0][:, lhs_cols].bitcast(FP8X4),
+                lhsT_scale=lhs[1][:, lhs_cols],
+                rhs=rhs[0][:, rhs_cols].bitcast(FP8X4),
+                rhs_scale=rhs[1][:, rhs_cols],
+                start=start,
+                stop=stop,
+            )
+
+        def passes(b, c, tiles=range(N_TILES)):
+            for i in tiles:
+                if b == 0:
+                    y_acc[c, i] = bank_tile(banks_of[c][i], "y_acc")
+                mx_pass(y_acc[c, i][:], w3q[b], slice(i * P, (i + 1) * P), zq[b, c], slice(0, BANK), b == 0, b == 1)
+
+        def first_passes(b):
+            for mj in range(2):
+                if b == 0:
+                    y_acc["turned", mj] = bank_tile(4 + mj, "yt_acc")
+                mx_pass(y_acc["turned", mj][:], zq[b, 0], slice(mj * P, (mj + 1) * P), w3q[b], slice(0, N), b == 0, b == 1)
+            for i in range(N_TILES):
+                pair, ii = divmod(i, 2)
+                if (b, ii) == (0, 0):
+                    y_acc[0, pair] = bank_tile(pair, "y_acc", (P, 2, BANK - TURNED))
+                mx_pass(
+                    y_acc[0, pair][:, ii, :], w3q[b], slice(i * P, (i + 1) * P), zq[b, 0], slice(TURNED, BANK),
+                    (b, ii) == (0, 0), (b, ii) == (1, 1),
+                )
+
+        def last_gain(c):
             cols = slice(c * BANK, (c + 1) * BANK)
-            engine.tensor_tensor(z_slot[7][:, c, :], pages[PAGE_OF[7]][:, cols], last_gains[c], MULT)
+            nc.vector.tensor_tensor(z_slot[7][:, c, :], pages[PAGE_OF[7]][:, cols], last_gains[c], MULT)
             place_high(c)
 
         def add_and_store(c, i):
@@ -351,39 +412,56 @@ def tile_list_transformer_overload_board_kernel(
                 rows = out[(i - 1) * P : (i + 1) * P, cols].rearrange("(i p) m -> p i m", p=P)
                 nc.sync.dma_start(rows, ambs[c][:, i - 1 : i + 1, :])
 
-        def products(b, c, tag):
-            codes, scales = quantize(z_words[b, c], "zq%d%d" % (b, c), tag)
-            zq[b, c] = (codes[:], scales[:])
-            for i in range(N_TILES):
-                stage2_pass(b, c, i)
+        def quantize_z(b, c, codes):
+            zq[b, c] = quantize(z_words[b, c], "zq%d%d" % (b, c), codes)
 
         def quantize_w3(b, tag):
-            codes, scales = quantize(w3_bf[b], "w3q%d" % b, tag)
-            w3q.append((codes[:], scales[:]))
+            w3q.append(quantize(w3_bf[b], "w3q%d" % b, codes_on(tag)))
 
-        last_gain(0, nc.vector)
-        last_gain(1, nc.vector)
+        last_gain(0)
+        last_gain(1)
         quantize_w3(0, "last_gain0")
-        products(0, 0, "last_gain1")
-        last_gain(2, nc.vector)
+        quantize_z(0, 0, codes_on("last_gain1"))
+        first_passes(0)
+        last_gain(2)
         quantize_w3(1, "z_words00")
-        products(1, 0, "h0")
-        products(0, 1, "w3_bf1")
-        products(0, 2, "z_words10")
-        products(1, 1, "h4")
-        add_and_store(0, 0)
-        products(1, 2, "h5")
-        last = CHUNKS - 1
-        cols = slice(last * BANK, T2)
-        z_last = keep.tile([P, 2, BANK], BF16, name="z_last", tag="z_words12", align_bytes=64)
-        for t, gain_k in enumerate((gains[SLICES - 2][:, cols], last_gains[last])):
+        quantize_z(1, 0, codes_on("h0"))
+        first_passes(1)
+        y_t = keep.tile([P, 2, N], F32, name="y_t", tag="h3", align_bytes=64)
+        for mj in range(2):
+            nc.scalar.copy(y_t[:, mj, :], y_acc["turned", mj][:])
+        quantize_z(0, 1, codes_on("w3_bf1"))
+        quantize_z(0, 2, codes_on("z_words10"))
+        quantize_z(1, 1, codes_on("h4"))
+        for pair in range(2):
+            res = ambs[0][:, 2 * pair : 2 * pair + 2, :]
+            nc.vector.tensor_tensor(res, y_acc[0, pair][:], res, ADD)
+        nc.sync.dma_start(out[:, TURNED:BANK].rearrange("(i p) m -> p i m", p=P), ambs[0][:])
+        for b in range(2):
+            passes(b, 1, (0, 1))
+        turn_into_sums(y_t, False)
+        for i in (2, 3):
+            for b in range(2):
+                passes(b, 1, (i,))
+        for pair in range(2):
+            nc.scalar.copy(amb_first[:, 2 * pair : 2 * pair + 2, :], sums[pair][:])
+        for i in range(N_TILES):
+            add_and_store(1, i)
+            if i == 1:
+                nc.sync.dma_start(out[:, 0:TURNED].rearrange("(i p) m -> p i m", p=P), amb_first[:])
+        passes(0, 2)
+        cols = slice(LAST * BANK, T2)
+        z_last = keep.tile([P, 2, BANK], BF16, name="z_last", tag="z_words11", align_bytes=64)
+        for t, gain_k in enumerate((gains[SLICES - 2][:, cols], last_gains[LAST])):
             nc.gpsimd.tensor_tensor(z_last[:, t, :], pages[PAGE_OF[SLICES - 2 + t]][:, cols], gain_k, MULT)
-        z_words[1, last] = keep.tile([P, 2048], BF16, name="z_words", tag="z_words02", align_bytes=64)[:]
-        place_low(last)
-        place_pair(last, 1, z_last[:])
-        for c, i in [(c, i) for c in range(CHUNKS) for i in range(N_TILES)][1:]:
-            if (c, i) == (1, 3):
-                products(0, last, "gain_rest")
-            if (c, i) == (2, 2):
-                products(1, last, "h6")
-            add_and_store(c, i)
+        place_pair(LAST, 1, z_last[:])
+        for u, (b, c) in enumerate(((1, 2), (0, LAST))):
+            quantize_z(b, c, arena.tile([P, BANK], U32, name="late_codes%d" % u, align_bytes=64, offset=20480 + 2048 * u))
+            passes(b, c)
+        for i in range(N_TILES - 1):
+            add_and_store(2, i)
+        quantize_z(1, LAST, codes_on("h6"))
+        passes(1, LAST)
+        add_and_store(2, N_TILES - 1)
+        for i in range(N_TILES):
+            add_and_store(LAST, i)

@@ -57,7 +57,7 @@ def tile_list_transformer_overload_board_kernel(
         w2_s_raw = keep.tile([P, H], U8, name="w2_s_raw", tag="w2_s_raw", align_bytes=64)
         nc.gpsimd.memset(tab_s[:].bitcast(I32), 0)
         nc.gpsimd.memset(w2_s_raw[:].bitcast(I32), 0)
-        pages = [keep.tile([P, T2], F32, name="page%d" % i) for i in range(3)]
+        pages = [keep.tile([P, T2], F32, name="page", tag="page%d" % i, align_bytes=64) for i in range(3)]
         for page in pages:
             nc.gpsimd.memset(page[:], 0.0)
 
@@ -104,11 +104,18 @@ def tile_list_transformer_overload_board_kernel(
         gains = {}
         w3_raw = []
         ambs = {}
+        amb_apart = {}
 
         def load_amb(c):
             cols = slice(max(c * BANK, TURNED), (c + 1) * BANK)
             ambs[c] = stage.tile([P, N_TILES, cols.stop - cols.start], F32, name="amb%d" % c, tag="rows")
-            nc.sync.dma_start(ambs[c][:], amb[:, cols].rearrange("(i p) m -> p i m", p=P))
+            rows = amb[:, cols].rearrange("(i p) m -> p i m", p=P)
+            if c == 2:
+                amb_apart[c, 0] = keep.tile([P, BANK], F32, name="amb_apart", tag="amb_apart", align_bytes=64)[:]
+                nc.sync.dma_start(amb_apart[c, 0], rows[:, 0, :])
+                nc.sync.dma_start(ambs[c][:, 1:N_TILES, :], rows[:, 1:N_TILES, :])
+            else:
+                nc.sync.dma_start(ambs[c][:], rows)
 
         for k in range(SLICES):
             rows = gain_rows[k // PACK, k % PACK]
@@ -116,13 +123,13 @@ def tile_list_transformer_overload_board_kernel(
                 gains[k] = load_rows(rows, F32, "gain%d" % k)
             else:
                 last_gains = []
-                for c in range(2):
+                for c in range(LAST):
                     g_sb = keep.tile([P, BANK], F32, name="last_gain", tag="last_gain%d" % c, align_bytes=64)
                     nc.sync.dma_start(g_sb[:], rows[:, c * BANK : (c + 1) * BANK])
                     last_gains.append(g_sb[:])
-                gain_rest = arena.tile([P, 2, BANK], F32, name="gain_rest", align_bytes=64, offset=20480)
-                nc.sync.dma_start(gain_rest[:], rows[:, 2 * BANK : T2].rearrange("p (c m) -> p c m", c=2))
-                last_gains.extend(gain_rest[:, c, :] for c in range(2))
+                held_pair = keep.tile([P, 2, BANK], F32, name="held_pair", align_bytes=64)
+                nc.sync.dma_start(held_pair[:, 1, :], rows[:, LAST * BANK : T2])
+                last_gains.append(held_pair[:, 1, :])
             if k == 5:
                 w3_raw.extend(load_k_first(w3[512 * b : 512 * (b + 1), :], "w3_raw%d" % b) for b in range(2))
                 amb_first = keep.tile([P, N_TILES, TURNED], F32, name="amb_first", align_bytes=64)
@@ -130,10 +137,11 @@ def tile_list_transformer_overload_board_kernel(
         for c in range(CHUNKS):
             load_amb(c)
 
-        def quantize(src_bf16, name, codes):
-            scales = keep.tile([P, BANK], U8, name=name + "_scales", align_bytes=64)
-            nc.vector.quantize_mx(out=codes[:].bitcast(FP8X4), scales=scales[:], in_=src_bf16)
-            return codes[:], scales[:]
+        def quantize(src_bf16, name, codes, scales=None):
+            if scales is None:
+                scales = keep.tile([P, BANK], U8, name=name + "_scales", align_bytes=64)[:]
+            nc.vector.quantize_mx(out=codes[:].bitcast(FP8X4), scales=scales, in_=src_bf16)
+            return codes[:], scales
 
         def codes_on(tag):
             return keep.tile([P, BANK], U32, name="codes", tag=tag, align_bytes=64)
@@ -209,15 +217,17 @@ def tile_list_transformer_overload_board_kernel(
                 start=True,
                 stop=False,
             )
-            nc.tensor.matmul_mx(
-                out=acc[:, 0:width],
-                lhsT=w2_p[:, 2 * col : 2 * (col + P)].bitcast(FP4X4),
-                lhsT_scale=w2_s[:, col : col + P],
-                rhs=words1[jh][:, lo : lo + width].bitcast(FP8X4),
-                rhs_scale=g_scales[SCALE_ROW[1] : P, js],
-                start=False,
-                stop=True,
-            )
+            step = BANK if width == BANK else P
+            for n0 in range(0, width, step):
+                nc.tensor.matmul_mx(
+                    out=acc[:, n0 : n0 + step],
+                    lhsT=w2_p[:, 2 * col : 2 * (col + P)].bitcast(FP4X4),
+                    lhsT_scale=w2_s[:, col : col + P],
+                    rhs=words1[jh][:, lo + n0 : lo + n0 + step].bitcast(FP8X4),
+                    rhs_scale=g_scales[SCALE_ROW[1] : P, js.start + n0 : js.start + n0 + step],
+                    start=False,
+                    stop=(n0 + step == width),
+                )
             nc.scalar.activation(dst, acc[:, 0:width], GELU)
 
         def stage1(k, jhs=(0, 1)):
@@ -241,9 +251,9 @@ def tile_list_transformer_overload_board_kernel(
 
         z_slot = {}
 
-        def times_gain(k, chunks):
+        def times_gain(k, chunks, dst=None):
             nc.gpsimd.tensor_tensor(
-                z_slot[k][:, chunks, :],
+                z_slot[k][:, chunks, :] if dst is None else dst,
                 pages[PAGE_OF[k]][:].rearrange("p (c m) -> p c m", c=CHUNKS)[:, chunks, :],
                 gains[k][:].rearrange("p (c m) -> p c m", c=CHUNKS)[:, chunks, :],
                 MULT,
@@ -283,9 +293,10 @@ def tile_list_transformer_overload_board_kernel(
         for k in range(4, SLICES):
             stage1(k)
         z_low = keep.tile([P, 2, T2], BF16, name="z_low", align_bytes=64)
-        z_high = keep.tile([P, 5 * BANK + 2048], BF16, name="z_high", align_bytes=64)
+        z_high = keep.tile([P, 2, 2, BANK], BF16, name="z_high", tag="z_high", align_bytes=64)
+        z_high2 = keep.tile([P, BANK + 2048], BF16, name="z_high2", align_bytes=64)
         w3_bf1 = keep.tile([P, 2048], BF16, name="w3_bf1", tag="w3_bf1", align_bytes=64)
-        w3_bf = [z_high[:, 5 * BANK : 5 * BANK + 2048], w3_bf1[:]]
+        w3_bf = [z_high2[:, BANK : BANK + 2048], w3_bf1[:]]
         for b in range(2):
             cast_w3(b, w3_bf[b])
 
@@ -294,7 +305,7 @@ def tile_list_transformer_overload_board_kernel(
             z_slot[t] = z_pairs[:].rearrange("p (c u m e) -> p c u m e", c=CHUNKS, u=2, e=2)[:, :, t // 2, :, t % 2]
         for t in range(2):
             z_slot[4 + t] = z_low[:, t, :].rearrange("p (c m) -> p c m", c=CHUNKS)
-            z_slot[6 + t] = z_high[:, 0 : 6 * BANK].rearrange("p (c t m) -> p c t m", t=2, m=BANK)[:, :, t, :]
+        high_rows = [z_high[:, 0], z_high[:, 1], z_high2[:, 0 : 2 * BANK].rearrange("p (t m) -> p t m", t=2)]
         z_words = {
             (b, c): keep.tile([P, 2048], BF16, name="z_words", tag="z_words%d%d" % (b, c), align_bytes=64)[:]
             for b in range(2)
@@ -317,7 +328,7 @@ def tile_list_transformer_overload_board_kernel(
             place_pair(c, 0, z_low[:, :, c * BANK : (c + 1) * BANK])
 
         def place_high(c):
-            place_pair(c, 1, z_high[:, 2 * c * BANK : 2 * (c + 1) * BANK].rearrange("p (t m) -> p t m", t=2))
+            place_pair(c, 1, high_rows[c])
 
         sums = {}
 
@@ -350,8 +361,11 @@ def tile_list_transformer_overload_board_kernel(
             if k - 1 == 5:
                 times_gain(5, slice(0, 2))
                 times_gain(5, slice(2, CHUNKS))
+            elif k - 1 == 6:
+                times_gain(6, slice(0, 2), z_high[:, :, 0, :])
+                times_gain(6, slice(2, 3), high_rows[2][:, 0:1, :])
             else:
-                times_gain(k - 1, slice(0, LAST if k - 1 == 6 else CHUNKS))
+                times_gain(k - 1, slice(0, CHUNKS))
             if k + 3 < SLICES:
                 weigh(k + 3)
             if k == 4:
@@ -366,7 +380,7 @@ def tile_list_transformer_overload_board_kernel(
         zq = {}
         w3q = []
         y_acc = {}
-        banks_of = {1: (2, 3, 4, 5), 2: (0, 1, 6, 7), 3: (2, 3, 4, 5)}
+        banks_of = {1: (2, 3, 4, 5), 2: (0, 1, 2, 3), 3: (4, 5, 6, 7)}
 
         def mx_pass(acc, lhs, lhs_cols, rhs, rhs_cols, start, stop):
             nc.tensor.matmul_mx(
@@ -401,19 +415,20 @@ def tile_list_transformer_overload_board_kernel(
 
         def last_gain(c):
             cols = slice(c * BANK, (c + 1) * BANK)
-            nc.vector.tensor_tensor(z_slot[7][:, c, :], pages[PAGE_OF[7]][:, cols], last_gains[c], MULT)
+            nc.vector.tensor_tensor(high_rows[c][:, 1, :], pages[PAGE_OF[7]][:, cols], last_gains[c], MULT)
             place_high(c)
 
+        held = {(1, 1): held_pair[:]}
+
         def add_and_store(c, i):
-            res = ambs[c][:, i, :]
-            nc.vector.tensor_tensor(res, y_acc[c, i][:], res, ADD)
+            pair = held.get((c, i // 2), ambs[c][:, i - i % 2 : i - i % 2 + 2, :])
+            nc.vector.tensor_tensor(pair[:, i % 2, :], y_acc[c, i][:], amb_apart.get((c, i), ambs[c][:, i, :]), ADD)
             cols = slice(c * BANK, (c + 1) * BANK)
             if i % 2 == 1:
-                rows = out[(i - 1) * P : (i + 1) * P, cols].rearrange("(i p) m -> p i m", p=P)
-                nc.sync.dma_start(rows, ambs[c][:, i - 1 : i + 1, :])
+                nc.sync.dma_start(out[(i - 1) * P : (i + 1) * P, cols].rearrange("(i p) m -> p i m", p=P), pair)
 
-        def quantize_z(b, c, codes):
-            zq[b, c] = quantize(z_words[b, c], "zq%d%d" % (b, c), codes)
+        def quantize_z(b, c, codes, scales=None):
+            zq[b, c] = quantize(z_words[b, c], "zq%d%d" % (b, c), codes, scales)
 
         def quantize_w3(b, tag):
             w3q.append(quantize(w3_bf[b], "w3q%d" % b, codes_on(tag)))
@@ -433,35 +448,50 @@ def tile_list_transformer_overload_board_kernel(
         quantize_z(0, 1, codes_on("w3_bf1"))
         quantize_z(0, 2, codes_on("z_words10"))
         quantize_z(1, 1, codes_on("h4"))
-        for pair in range(2):
-            res = ambs[0][:, 2 * pair : 2 * pair + 2, :]
-            nc.vector.tensor_tensor(res, y_acc[0, pair][:], res, ADD)
-        nc.sync.dma_start(out[:, TURNED:BANK].rearrange("(i p) m -> p i m", p=P), ambs[0][:])
+
+        def add_first(pair):
+            tiles = slice(2 * pair, 2 * pair + 2)
+            nc.vector.tensor_tensor(res_first[:, tiles, :], y_acc[0, pair][:], ambs[0][:, tiles, :], ADD)
+
+        res_first = keep.tile([P, N_TILES, BANK - TURNED], F32, name="res_first", tag="z_high", align_bytes=64)
+        add_first(0)
+        add_first(1)
+        nc.sync.dma_start(out[:, TURNED:BANK].rearrange("(i p) m -> p i m", p=P), res_first[:])
         for b in range(2):
             passes(b, 1, (0, 1))
-        turn_into_sums(y_t, False)
         for i in (2, 3):
             for b in range(2):
                 passes(b, 1, (i,))
+            if i == 2:
+                turn_into_sums(y_t, False)
+        last_rows = keep.tile([P, 6, BANK], BF16, name="last_rows", tag="z_words11", align_bytes=64)
+        res_turned = last_rows[:, 1:5, :].bitcast(F32)
         for pair in range(2):
-            nc.scalar.copy(amb_first[:, 2 * pair : 2 * pair + 2, :], sums[pair][:])
-        for i in range(N_TILES):
+            nc.scalar.copy(res_turned[:, 2 * pair : 2 * pair + 2, :], sums[pair][:])
+        for i in range(N_TILES - 1):
             add_and_store(1, i)
-            if i == 1:
-                nc.sync.dma_start(out[:, 0:TURNED].rearrange("(i p) m -> p i m", p=P), amb_first[:])
+        nc.sync.dma_start(out[:, 0:TURNED].rearrange("(i p) m -> p i m", p=P), res_turned)
         passes(0, 2)
         cols = slice(LAST * BANK, T2)
-        z_last = keep.tile([P, 2, BANK], BF16, name="z_last", tag="z_words11", align_bytes=64)
+        z_last = last_rows[:, 0:6:5, :]
         for t, gain_k in enumerate((gains[SLICES - 2][:, cols], last_gains[LAST])):
             nc.gpsimd.tensor_tensor(z_last[:, t, :], pages[PAGE_OF[SLICES - 2 + t]][:, cols], gain_k, MULT)
-        place_pair(LAST, 1, z_last[:])
-        for u, (b, c) in enumerate(((1, 2), (0, LAST))):
-            quantize_z(b, c, arena.tile([P, BANK], U32, name="late_codes%d" % u, align_bytes=64, offset=20480 + 2048 * u))
-            passes(b, c)
-        for i in range(N_TILES - 1):
+        place_pair(LAST, 1, z_last)
+        late_scales = keep.tile([P, 2, BANK], U8, name="late_scales", tag="page%d" % PAGE_OF[7], align_bytes=64)
+        quantize_z(1, 2, codes_on("h5"), late_scales[:, 0, :])
+        passes(1, 2)
+        quantize_z(0, LAST, codes_on("h2"), late_scales[:, 1, :])
+        add_and_store(1, N_TILES - 1)
+        passes(0, LAST, (0, 1))
+        for i in range(2):
             add_and_store(2, i)
-        quantize_z(1, LAST, codes_on("h6"))
-        passes(1, LAST)
-        add_and_store(2, N_TILES - 1)
+        last_scales = keep.tile([P, BANK], U8, name="last_scales", tag="amb_apart", align_bytes=64)
+        quantize_z(1, LAST, codes_on("h6"), last_scales[:])
+        passes(1, LAST, (0, 1))
+        for i in (2, 3):
+            for b in range(2):
+                passes(b, LAST, (i,))
+        for i in range(2, N_TILES):
+            add_and_store(2, i)
         for i in range(N_TILES):
             add_and_store(LAST, i)

@@ -53,11 +53,11 @@ def tile_list_transformer_overload_board_kernel(
             nc.sync.dma_start(t[:], src.rearrange("(p j) c -> p j c", j=PACK))
             return t
 
-        tab_s = keep.tile([P, T], U8, name="tab_s", align_bytes=64)
-        w2_s_raw = keep.tile([P, H], U8, name="w2_s_raw", tag="w2_s_raw", align_bytes=64)
-        nc.gpsimd.memset(tab_s[:].bitcast(I32), 0)
+        w2_s_raw = keep.tile([P, H], U8, name="w2_s_raw", tag="page2", align_bytes=64)
+        tab_s = keep.tile([P, T], U8, name="tab_s", tag="tab_s", align_bytes=64)
         nc.gpsimd.memset(w2_s_raw[:].bitcast(I32), 0)
-        pages = [keep.tile([P, T2], F32, name="page", tag="page%d" % i, align_bytes=64) for i in range(3)]
+        nc.gpsimd.memset(tab_s[:].bitcast(I32), 0)
+        pages = [keep.tile([P, T2], F32, name="page", tag="page%d" % i, align_bytes=64) for i in range(2)]
         for page in pages:
             nc.gpsimd.memset(page[:], 0.0)
 
@@ -75,23 +75,22 @@ def tile_list_transformer_overload_board_kernel(
                 w2_scales[0, 4 * q : 4 * q + 4, :].bitcast(I32),
             )
 
+        def load_table(a):
+            return load_rows(tab_words[a].rearrange("p t i -> p (t i)").bitcast(I32), I32, "tab%d" % a)
+
         idx = keep.tile([P, S // 16], U16, name="idx")
         nc.sync.dma_start(idx[:], offs)
-        tab0 = load_rows(tab_words[0].rearrange("p t i -> p (t i)").bitcast(I32), I32, "tab0")
-        tab1 = stage.tile([P, T], I32, name="tab1", tag="rows")
-        tab1_src = tab_words[1].rearrange("p t i -> p (t i)").bitcast(I32)
-        for run in range(5):
-            load_tab_scales(run)
-        nc.sync.dma_start(tab1[:, 0 : T // 2], tab1_src[:, 0 : T // 2])
-        for run in range(5, 8):
-            load_tab_scales(run)
-        w1_raw = [load_k_first(w1[:, 0:512], "w1_raw0")]
-        w2_raw = keep.tile([P, 2 * H], U8, name="w2_raw")
-        nc.sync.dma_start(w2_raw[:].bitcast(I32), w2_words[0].bitcast(I32))
+        tabs = [load_table(0)]
         for q in range(4):
             load_w2_scales(q)
-        nc.sync.dma_start(tab1[:, T // 2 : T], tab1_src[:, T // 2 : T])
-        tabs = [tab0, tab1]
+        for run in range(2):
+            load_tab_scales(run)
+        w1_raw = [load_k_first(w1[:, 0:512], "w1_raw0")]
+        for run in range(2, 8):
+            load_tab_scales(run)
+        tabs.append(load_table(1))
+        w2_raw = [keep.tile([P, H], U8, name="w2_raw%d" % b) for b in range(2)]
+        nc.sync.dma_start(w2_raw[0][:].bitcast(I32), w2_words[0][:, 0:H].bitcast(I32))
         wgs_sb = keep.tile([P, S], F32, name="wgs_sb")
         nc.sync.dma_start(wgs_sb[:], wgs)
         idx2 = keep.tile([P, S // 16], U16, name="idx2")
@@ -99,6 +98,7 @@ def tile_list_transformer_overload_board_kernel(
         w1_raw1 = arena.tile([P, PACK, 512], F32, name="w1_raw1", align_bytes=64, offset=0)
         nc.sync.dma_start(w1_raw1[:], w1[:, 512:1024].rearrange("(p j) c -> p j c", j=PACK))
         w1_raw.append(w1_raw1)
+        nc.sync.dma_start(w2_raw[1][:].bitcast(I32), w2_words[0][:, H : 2 * H].bitcast(I32))
 
         gain_rows = gain.rearrange("(b p j) m -> b j p m", b=2, j=PACK)
         gains = {}
@@ -166,20 +166,23 @@ def tile_list_transformer_overload_board_kernel(
         w1_bf0 = [keep.tile([P, 1024], BF16, name="w1_bf0", tag="w1_then_words%d" % u, align_bytes=64) for u in range(2)]
         for u in range(2):
             cast_w1(0, w1_bf0[u][:], slice(2 * u, 2 * u + 2))
+        for b in range(2):
+            nc.scalar.copy(
+                w2_p[:].bitcast(U16).rearrange("p (b t m) -> p b t m", b=2, t=PACK)[:, b],
+                w2_raw[b][:].bitcast(U16).rearrange("p (m t) -> p t m", t=PACK),
+            )
         nc.vector.tensor_copy(words0[:], tabs[0][:].bitcast(U32).indirect(idx[:]))
-        nc.vector.tensor_copy(g_scales[:], tab_s[:].indirect(idx[:]))
-        nc.vector.tensor_copy(
-            w2_p[:].bitcast(U16).rearrange("p (b t m) -> p b t m", b=2, t=PACK),
-            w2_raw[:].bitcast(U16).rearrange("p (b m t) -> p b t m", b=2, t=PACK),
-        )
         nc.vector.tensor_copy(
             w2_s[:].rearrange("p (b t m) -> p b t m", b=2, t=PACK),
             w2_s_raw[:].rearrange("p (b m t) -> p b t m", b=2, t=PACK),
         )
-        ident = keep.tile([P, P], F32, name="ident", tag="w2_s_raw", align_bytes=64)
+        nc.vector.tensor_copy(g_scales[:], tab_s[:].indirect(idx[:]))
+        pages.append(keep.tile([P, T2], F32, name="page2", tag="page2", align_bytes=64))
+        nc.gpsimd.memset(pages[2][:], 0.0)
+        ident = keep.tile([P, P], F32, name="ident", align_bytes=64)
         make_identity(nc, ident[:])
         w1_codes = keep.tile([P, H], U32, name="w1_codes", align_bytes=64)
-        w1_scales = keep.tile([P, H], U8, name="w1_scales", align_bytes=64)
+        w1_scales = keep.tile([P, H], U8, name="w1_scales", tag="tab_s", align_bytes=64)
 
         def quantize_w1(src, col):
             cols = slice(col, col + src.shape[1] // PACK)
@@ -210,24 +213,22 @@ def tile_list_transformer_overload_board_kernel(
             acc = bank_tile(bank, "e_acc")
             nc.tensor.matmul_mx(
                 out=acc[:, 0:width],
+                lhsT=w2_p[:, 2 * col : 2 * (col + P)].bitcast(FP4X4),
+                lhsT_scale=w2_s[:, col : col + P],
+                rhs=words1[jh][:, lo : lo + width].bitcast(FP8X4),
+                rhs_scale=g_scales[SCALE_ROW[1] : P, js],
+                start=True,
+                stop=False,
+            )
+            nc.tensor.matmul_mx(
+                out=acc[:, 0:width],
                 lhsT=w1_codes[:, col : col + P].bitcast(FP8X4),
                 lhsT_scale=w1_scales[:, col : col + P],
                 rhs=words0[:, js].bitcast(FP8X4),
                 rhs_scale=g_scales[SCALE_ROW[0] : P, js],
-                start=True,
-                stop=False,
+                start=False,
+                stop=True,
             )
-            step = BANK if width == BANK else P
-            for n0 in range(0, width, step):
-                nc.tensor.matmul_mx(
-                    out=acc[:, n0 : n0 + step],
-                    lhsT=w2_p[:, 2 * col : 2 * (col + P)].bitcast(FP4X4),
-                    lhsT_scale=w2_s[:, col : col + P],
-                    rhs=words1[jh][:, lo + n0 : lo + n0 + step].bitcast(FP8X4),
-                    rhs_scale=g_scales[SCALE_ROW[1] : P, js.start + n0 : js.start + n0 + step],
-                    start=False,
-                    stop=(n0 + step == width),
-                )
             nc.scalar.activation(dst, acc[:, 0:width], GELU)
 
         def stage1(k, jhs=(0, 1)):

@@ -294,10 +294,10 @@ def tile_list_transformer_overload_board_kernel(
         for k in range(4, SLICES):
             stage1(k)
         z_low = keep.tile([P, 2, T2], BF16, name="z_low", align_bytes=64)
-        z_high = keep.tile([P, 2, 2, BANK], BF16, name="z_high", tag="z_high", align_bytes=64)
-        z_high2 = keep.tile([P, BANK + 2048], BF16, name="z_high2", align_bytes=64)
+        z_high0 = keep.tile([P, 2, BANK], BF16, name="z_high0", tag="z_high0", align_bytes=64)
+        z_high = keep.tile([P, 3 * BANK + 2048], BF16, name="z_high", align_bytes=64)
         w3_bf1 = keep.tile([P, 2048], BF16, name="w3_bf1", tag="w3_bf1", align_bytes=64)
-        w3_bf = [z_high2[:, BANK : BANK + 2048], w3_bf1[:]]
+        w3_bf = [z_high[:, 3 * BANK : 3 * BANK + 2048], w3_bf1[:]]
         for b in range(2):
             cast_w3(b, w3_bf[b])
 
@@ -306,7 +306,8 @@ def tile_list_transformer_overload_board_kernel(
             z_slot[t] = z_pairs[:].rearrange("p (c u m e) -> p c u m e", c=CHUNKS, u=2, e=2)[:, :, t // 2, :, t % 2]
         for t in range(2):
             z_slot[4 + t] = z_low[:, t, :].rearrange("p (c m) -> p c m", c=CHUNKS)
-        high_rows = [z_high[:, 0], z_high[:, 1], z_high2[:, 0 : 2 * BANK].rearrange("p (t m) -> p t m", t=2)]
+        later_rows = z_high[:, 0 : 4 * BANK].rearrange("p (c t m) -> p c t m", c=2, t=2)
+        high_rows = [z_high0[:], later_rows[:, 0], later_rows[:, 1]]
         z_words = {
             (b, c): keep.tile([P, 2048], BF16, name="z_words", tag="z_words%d%d" % (b, c), align_bytes=64)[:]
             for b in range(2)
@@ -363,8 +364,8 @@ def tile_list_transformer_overload_board_kernel(
                 times_gain(5, slice(0, 2))
                 times_gain(5, slice(2, CHUNKS))
             elif k - 1 == 6:
-                times_gain(6, slice(0, 2), z_high[:, :, 0, :])
-                times_gain(6, slice(2, 3), high_rows[2][:, 0:1, :])
+                times_gain(6, slice(0, 1), z_high0[:, 0:1, :])
+                times_gain(6, slice(1, 3), later_rows[:, :, 0, :])
             else:
                 times_gain(k - 1, slice(0, CHUNKS))
             if k + 3 < SLICES:
@@ -446,15 +447,16 @@ def tile_list_transformer_overload_board_kernel(
         y_t = keep.tile([P, 2, N], F32, name="y_t", tag="h3", align_bytes=64)
         for mj in range(2):
             nc.scalar.copy(y_t[:, mj, :], y_acc["turned", mj][:])
-        quantize_z(0, 1, codes_on("w3_bf1"))
-        quantize_z(0, 2, codes_on("z_words10"))
+        early_scales = keep.tile([P, 2, BANK], U8, name="early_scales", tag="z_high0", align_bytes=64)
+        quantize_z(0, 1, codes_on("w3_bf1"), early_scales[:, 0, :])
+        quantize_z(0, 2, codes_on("h7"), early_scales[:, 1, :])
         quantize_z(1, 1, codes_on("h4"))
 
         def add_first(pair):
             tiles = slice(2 * pair, 2 * pair + 2)
             nc.vector.tensor_tensor(res_first[:, tiles, :], y_acc[0, pair][:], ambs[0][:, tiles, :], ADD)
 
-        res_first = keep.tile([P, N_TILES, BANK - TURNED], F32, name="res_first", tag="z_high", align_bytes=64)
+        res_first = keep.tile([P, N_TILES, BANK - TURNED], F32, name="res_first", tag="z_words01", align_bytes=64)
         add_first(0)
         add_first(1)
         nc.sync.dma_start(out[:, TURNED:BANK].rearrange("(i p) m -> p i m", p=P), res_first[:])

@@ -123,13 +123,10 @@ def tile_list_transformer_overload_board_kernel(
                 gains[k] = load_rows(rows, F32, "gain%d" % k)
             else:
                 last_gains = []
-                for c in range(LAST):
+                for c in range(CHUNKS):
                     g_sb = keep.tile([P, BANK], F32, name="last_gain", tag="last_gain%d" % c, align_bytes=64)
                     nc.sync.dma_start(g_sb[:], rows[:, c * BANK : (c + 1) * BANK])
                     last_gains.append(g_sb[:])
-                held_pair = keep.tile([P, 2, BANK], F32, name="held_pair", align_bytes=64)
-                nc.sync.dma_start(held_pair[:, 1, :], rows[:, LAST * BANK : T2])
-                last_gains.append(held_pair[:, 1, :])
             if k == 5:
                 w3_raw.extend(load_k_first(w3[512 * b : 512 * (b + 1), :], "w3_raw%d" % b) for b in range(2))
                 amb_first = keep.tile([P, N_TILES, TURNED], F32, name="amb_first", align_bytes=64)
@@ -420,10 +417,8 @@ def tile_list_transformer_overload_board_kernel(
             nc.vector.tensor_tensor(high_rows[c][:, 1, :], pages[PAGE_OF[7]][:, cols], last_gains[c], MULT)
             place_high(c)
 
-        held = {(1, 1): held_pair[:]}
-
         def add_and_store(c, i):
-            pair = held.get((c, i // 2), ambs[c][:, i - i % 2 : i - i % 2 + 2, :])
+            pair = ambs[c][:, i - i % 2 : i - i % 2 + 2, :]
             nc.vector.tensor_tensor(pair[:, i % 2, :], y_acc[c, i][:], amb_apart.get((c, i), ambs[c][:, i, :]), ADD)
             cols = slice(c * BANK, (c + 1) * BANK)
             if i % 2 == 1:
@@ -471,7 +466,7 @@ def tile_list_transformer_overload_board_kernel(
         res_turned = last_rows[:, 1:5, :].bitcast(F32)
         for pair in range(2):
             nc.scalar.copy(res_turned[:, 2 * pair : 2 * pair + 2, :], sums[pair][:])
-        for i in range(N_TILES - 1):
+        for i in range(N_TILES):
             add_and_store(1, i)
         nc.sync.dma_start(out[:, 0:TURNED].rearrange("(i p) m -> p i m", p=P), res_turned)
         passes(0, 2)
@@ -484,7 +479,6 @@ def tile_list_transformer_overload_board_kernel(
         quantize_z(1, 2, codes_on("h5"), late_scales[:, 0, :])
         passes(1, 2)
         quantize_z(0, LAST, codes_on("h2"), late_scales[:, 1, :])
-        add_and_store(1, N_TILES - 1)
         passes(0, LAST, (0, 1))
         for i in range(2):
             add_and_store(2, i)

@@ -62,18 +62,14 @@ def tile_list_transformer_overload_board_kernel(
             nc.gpsimd.memset(page[:], 0.0)
 
         def load_tab_scales(run):
-            a, q = divmod(run, 4)
-            row = 32 * q + SCALE_ROW[a]
+            r, a = divmod(run, 2)
             nc.sync.dma_start(
-                tab_s[row : row + 4, :].bitcast(I32),
-                tab_scales[a, 4 * q : 4 * q + 4, :].bitcast(I32),
+                tab_s[SCALE_ROW[a] + r : P : 32, :].bitcast(I32),
+                tab_scales[a, r:16:4, :].bitcast(I32),
             )
 
-        def load_w2_scales(q):
-            nc.sync.dma_start(
-                w2_s_raw[32 * q : 32 * q + 4, :].bitcast(I32),
-                w2_scales[0, 4 * q : 4 * q + 4, :].bitcast(I32),
-            )
+        def load_w2_scales(r):
+            nc.sync.dma_start(w2_s_raw[r:P:32, :].bitcast(I32), w2_scales[0, r:16:4, :].bitcast(I32))
 
         def load_table(a):
             return load_rows(tab_words[a].rearrange("p t i -> p (t i)").bitcast(I32), I32, "tab%d" % a)
@@ -81,8 +77,8 @@ def tile_list_transformer_overload_board_kernel(
         idx = keep.tile([P, S // 16], U16, name="idx")
         nc.sync.dma_start(idx[:], offs)
         tabs = [load_table(0)]
-        for q in range(4):
-            load_w2_scales(q)
+        for r in range(4):
+            load_w2_scales(r)
         for run in range(2):
             load_tab_scales(run)
         w1_raw = [load_k_first(w1[:, 0:512], "w1_raw0")]

@@ -156,9 +156,8 @@ def tile_list_transformer_overload_board_kernel(
         w2_p = keep.tile([P, 2 * H], U8, name="w2_p", align_bytes=64)
         w2_s = keep.tile([P, H], U8, name="w2_s", align_bytes=64)
 
-        w1_bf0 = [keep.tile([P, 1024], BF16, name="w1_bf0", tag="w1_then_words%d" % u, align_bytes=64) for u in range(2)]
-        for u in range(2):
-            cast_w1(0, w1_bf0[u][:], slice(2 * u, 2 * u + 2))
+        w1_bf0 = keep.tile([P, 2048], BF16, name="w1_bf0", tag="w1_then_words1", align_bytes=64)
+        cast_w1(0, w1_bf0[:], slice(0, PACK))
         for b in range(2):
             nc.scalar.copy(
                 w2_p[:].bitcast(U16).rearrange("p (b t m) -> p b t m", b=2, t=PACK)[:, b],
@@ -175,15 +174,15 @@ def tile_list_transformer_overload_board_kernel(
         ident = keep.tile([P, P], F32, name="ident", align_bytes=64)
         make_identity(nc, ident[:])
         w1_codes = keep.tile([P, H], U32, name="w1_codes", align_bytes=64)
-        w1_scales = keep.tile([P, H], U8, name="w1_scales", tag="tab_s", align_bytes=64)
+        w1_scales = keep.tile([P, H], U8, name="w1_scales", align_bytes=64)
 
         def quantize_w1(src, col):
             cols = slice(col, col + src.shape[1] // PACK)
             nc.vector.quantize_mx(out=w1_codes[:, cols].bitcast(FP8X4), scales=w1_scales[:, cols], in_=src)
 
         words1 = []
+        quantize_w1(w1_bf0[:], 0)
         for jh in range(HALVES):
-            quantize_w1(w1_bf0[jh][:], 256 * jh)
             words1.append(keep.tile([P, BANK], U32, name="words1", tag="w1_then_words%d" % jh, align_bytes=64))
             for lo in range(0, BANK, FIRST if jh == 0 else BANK):
                 js = slice(jh * BANK + lo, jh * BANK + lo + (FIRST if jh == 0 else BANK))

@@ -153,16 +153,20 @@ def tile_list_transformer_overload_board_kernel(
 
         words0 = keep.tile([P, S], U32, name="words0", align_bytes=64)
         g_scales = keep.tile([P, S], U8, name="g_scales", align_bytes=64)
-        w2_p = keep.tile([P, 2 * H], U8, name="w2_p", align_bytes=64)
+        w2_p = [keep.tile([P, H], U8, name="w2_p0", align_bytes=64)]
+
+        def deal_w2(b, ts):
+            nc.scalar.copy(
+                w2_p[b][:].bitcast(U16).rearrange("p (t m) -> p t m", t=PACK)[:, ts],
+                w2_raw[b][:].bitcast(U16).rearrange("p (m t) -> p t m", t=PACK)[:, ts],
+            )
+
         w2_s = keep.tile([P, H], U8, name="w2_s", align_bytes=64)
 
         w1_bf0 = keep.tile([P, 2048], BF16, name="w1_bf0", tag="w1_then_words1", align_bytes=64)
         cast_w1(0, w1_bf0[:], slice(0, PACK))
-        for b in range(2):
-            nc.scalar.copy(
-                w2_p[:].bitcast(U16).rearrange("p (b t m) -> p b t m", b=2, t=PACK)[:, b],
-                w2_raw[b][:].bitcast(U16).rearrange("p (m t) -> p t m", t=PACK),
-            )
+        for ts in (slice(0, 1), slice(1, PACK)):
+            deal_w2(0, ts)
         nc.vector.tensor_copy(words0[:], tabs[0][:].bitcast(U32).indirect(idx[:]))
         nc.vector.tensor_copy(
             w2_s[:].rearrange("p (b t m) -> p b t m", b=2, t=PACK),
@@ -203,24 +207,29 @@ def tile_list_transformer_overload_board_kernel(
             width = js.stop - js.start
             jh, lo = divmod(js.start, BANK)
             acc = bank_tile(bank, "e_acc")
-            nc.tensor.matmul_mx(
-                out=acc[:, 0:width],
-                lhsT=w2_p[:, 2 * col : 2 * (col + P)].bitcast(FP4X4),
-                lhsT_scale=w2_s[:, col : col + P],
-                rhs=words1[jh][:, lo : lo + width].bitcast(FP8X4),
-                rhs_scale=g_scales[SCALE_ROW[1] : P, js],
-                start=True,
-                stop=False,
+            squares = (
+                w2_p[b][:, 2 * t * P : 2 * (t + 1) * P].bitcast(FP4X4),
+                w2_s[:, col : col + P],
+                words1[jh][:, lo : lo + width],
+                g_scales[SCALE_ROW[1] : P, js],
             )
-            nc.tensor.matmul_mx(
-                out=acc[:, 0:width],
-                lhsT=w1_codes[:, col : col + P].bitcast(FP8X4),
-                lhsT_scale=w1_scales[:, col : col + P],
-                rhs=words0[:, js].bitcast(FP8X4),
-                rhs_scale=g_scales[SCALE_ROW[0] : P, js],
-                start=False,
-                stop=True,
+            currents = (
+                w1_codes[:, col : col + P].bitcast(FP8X4),
+                w1_scales[:, col : col + P],
+                words0[:, js],
+                g_scales[SCALE_ROW[0] : P, js],
             )
+            order = (currents, squares) if width == FIRST else (squares, currents)
+            for n, (weights, weight_scales, words, word_scales) in enumerate(order):
+                nc.tensor.matmul_mx(
+                    out=acc[:, 0:width],
+                    lhsT=weights,
+                    lhsT_scale=weight_scales,
+                    rhs=words.bitcast(FP8X4),
+                    rhs_scale=word_scales,
+                    start=n == 0,
+                    stop=n == 1,
+                )
             nc.scalar.activation(dst, acc[:, 0:width], GELU)
 
         def stage1(k, jhs=(0, 1)):
@@ -257,7 +266,7 @@ def tile_list_transformer_overload_board_kernel(
         raw0 = keep.tile([P, BANK], F32, name="raw0", tag="h1", align_bytes=64)
         for bank, js in enumerate((slice(0, FIRST), slice(FIRST, BANK))):
             heat(0, js, bank, raw0[:, js])
-        raw1 = keep.tile([P, BANK], F32, name="raw1", align_bytes=64)
+        raw1 = arena.tile([P, BANK], F32, name="raw1", align_bytes=64, offset=8192)
         raw[1, 0] = raw1[:]
         stage1(1, (0,))
         heat(0, high, 2, hs[0][:, high])
@@ -269,6 +278,8 @@ def tile_list_transformer_overload_board_kernel(
         for k in (1, 2, 3):
             raw[k, 1] = late[:, k - 1, :]
             stage1(k, (1,))
+        w2_p.append(arena.tile([P, H], U8, name="w2_p1", align_bytes=64, offset=0))
+        deal_w2(1, slice(0, PACK))
         for js in (slice(0, FIRST), slice(FIRST, BANK)):
             nc.vector.tensor_tensor(hs[0][:, js], raw0[:, js], wgs_sb[:, js], MULT)
         for js in (slice(0, FIRST), slice(FIRST, BANK)):

@@ -165,7 +165,7 @@ def tile_list_transformer_overload_board_kernel(
 
         w1_bf0 = keep.tile([P, 2048], BF16, name="w1_bf0", tag="w1_then_words1", align_bytes=64)
         cast_w1(0, w1_bf0[:], slice(0, PACK))
-        for ts in (slice(0, 1), slice(1, PACK)):
+        for ts in (slice(0, 2), slice(2, PACK)):
             deal_w2(0, ts)
         nc.vector.tensor_copy(words0[:], tabs[0][:].bitcast(U32).indirect(idx[:]))
         nc.vector.tensor_copy(

@@ -29,7 +29,7 @@ SLICES = 8
 FIRST = 256
 SCALE_ROW = (4, 0)
 PAGE_OF = (0, 1, 2, 0, 1, 2, 0, 1)
-TURNED = 2 * P
+TURNED = 2
 LAST = CHUNKS - 1
 
 
@@ -103,9 +103,9 @@ def tile_list_transformer_overload_board_kernel(
         amb_apart = {}
 
         def load_amb(c):
-            cols = slice(max(c * BANK, TURNED), (c + 1) * BANK)
-            ambs[c] = stage.tile([P, N_TILES, cols.stop - cols.start], F32, name="amb%d" % c, tag="rows")
-            rows = amb[:, cols].rearrange("(i p) m -> p i m", p=P)
+            first = TURNED if c == 0 else 0
+            ambs[c] = stage.tile([P, N_TILES - first, BANK], F32, name="amb%d" % c, tag="rows")
+            rows = amb[first * P : N, c * BANK : (c + 1) * BANK].rearrange("(i p) m -> p i m", p=P)
             if c == 2:
                 amb_apart[c, 0] = keep.tile([P, BANK], F32, name="amb_apart", tag="amb_apart", align_bytes=64)[:]
                 nc.sync.dma_start(amb_apart[c, 0], rows[:, 0, :])
@@ -125,8 +125,8 @@ def tile_list_transformer_overload_board_kernel(
                     last_gains.append(g_sb[:])
             if k == 5:
                 w3_raw.extend(load_k_first(w3[512 * b : 512 * (b + 1), :], "w3_raw%d" % b) for b in range(2))
-                amb_first = keep.tile([P, N_TILES, TURNED], F32, name="amb_first", align_bytes=64)
-                nc.sync.dma_start(amb_first[:], amb[:, 0:TURNED].rearrange("(i p) m -> p i m", p=P))
+                amb_first = keep.tile([P, TURNED, BANK], F32, name="amb_first", align_bytes=64)
+                nc.sync.dma_start(amb_first[:], amb[0 : TURNED * P, 0:BANK].rearrange("(i p) m -> p i m", p=P))
         for c in range(CHUNKS):
             load_amb(c)
 
@@ -338,27 +338,28 @@ def tile_list_transformer_overload_board_kernel(
         sums = {}
 
         def turn_into_sums(src, first):
-            for mj in range(2):
-                for i in range(N_TILES):
-                    pair, ii = divmod(i, 2)
-                    if first and (mj, ii) == (0, 0):
-                        sums[pair] = bank_tile(6 + pair, "sum_acc", (P, 2, TURNED))
+            for i in range(TURNED):
+                if first:
+                    sums[i] = bank_tile(6 + i, "sum_acc")
+                for mj in range(PACK):
                     nc.tensor.matmul(
-                        sums[pair][:, ii, mj * P : (mj + 1) * P],
+                        sums[i][:, mj * P : (mj + 1) * P],
                         lhsT=src[:, mj, i * P : (i + 1) * P],
                         rhs=ident[:],
-                        start=first and (mj, ii) == (0, 0),
-                        stop=not first and (mj, ii) == (1, 1),
+                        start=first and mj == 0,
+                        stop=not first and mj == PACK - 1,
                         is_transpose=True,
                     )
 
         def turn_amb():
-            amb_t = keep.tile([P, 2, N], F32, name="amb_t", tag="h1", align_bytes=64)
-            for mj in range(2):
-                acc = bank_tile(4 + mj, "amb_acc")
-                for i in range(N_TILES):
-                    nc.tensor.transpose(acc[:, i * P : (i + 1) * P], amb_first[:, i, mj * P : (mj + 1) * P], ident[:])
-                nc.scalar.copy(amb_t[:, mj, :], acc[:])
+            amb_t = keep.tile([P, PACK, TURNED * P], F32, name="amb_t", tag="h1", align_bytes=64)
+            for half in range(2):
+                acc = bank_tile(4 + half, "amb_acc", (P, 2, TURNED * P))
+                for mm in range(2):
+                    for i in range(TURNED):
+                        m_cols = slice((2 * half + mm) * P, (2 * half + mm + 1) * P)
+                        nc.tensor.transpose(acc[:, mm, i * P : (i + 1) * P], amb_first[:, i, m_cols], ident[:])
+                nc.scalar.copy(amb_t[:, 2 * half : 2 * half + 2, :], acc[:])
             turn_into_sums(amb_t, True)
 
         for k in range(1, SLICES):
@@ -385,7 +386,7 @@ def tile_list_transformer_overload_board_kernel(
         zq = {}
         w3q = []
         y_acc = {}
-        banks_of = {1: (2, 3, 4, 5), 2: (0, 1, 2, 3), 3: (4, 5, 6, 7)}
+        banks_of = {0: (None, None, 0, 1), 1: (2, 3, 4, 5), 2: (0, 1, 2, 3), 3: (4, 5, 6, 7)}
 
         def mx_pass(acc, lhs, lhs_cols, rhs, rhs_cols, start, stop):
             nc.tensor.matmul_mx(
@@ -405,18 +406,15 @@ def tile_list_transformer_overload_board_kernel(
                 mx_pass(y_acc[c, i][:], w3q[b], slice(i * P, (i + 1) * P), zq[b, c], slice(0, BANK), b == 0, b == 1)
 
         def first_passes(b):
-            for mj in range(2):
-                if b == 0:
-                    y_acc["turned", mj] = bank_tile(4 + mj, "yt_acc")
-                mx_pass(y_acc["turned", mj][:], zq[b, 0], slice(mj * P, (mj + 1) * P), w3q[b], slice(0, N), b == 0, b == 1)
-            for i in range(N_TILES):
-                pair, ii = divmod(i, 2)
-                if (b, ii) == (0, 0):
-                    y_acc[0, pair] = bank_tile(pair, "y_acc", (P, 2, BANK - TURNED))
+            for mj in range(PACK):
+                half, mm = divmod(mj, 2)
+                if (b, mm) == (0, 0):
+                    y_acc["turned", half] = bank_tile(4 + half, "yt_acc", (P, 2, TURNED * P))
                 mx_pass(
-                    y_acc[0, pair][:, ii, :], w3q[b], slice(i * P, (i + 1) * P), zq[b, 0], slice(TURNED, BANK),
-                    (b, ii) == (0, 0), (b, ii) == (1, 1),
+                    y_acc["turned", half][:, mm, :], zq[b, 0], slice(mj * P, (mj + 1) * P), w3q[b], slice(0, TURNED * P),
+                    (b, mm) == (0, 0), (b, mm) == (1, 1),
                 )
+            passes(b, 0, range(TURNED, N_TILES))
 
         def last_gain(c):
             cols = slice(c * BANK, (c + 1) * BANK)
@@ -445,22 +443,18 @@ def tile_list_transformer_overload_board_kernel(
         quantize_w3(1, "z_words00")
         quantize_z(1, 0, codes_on("h0"))
         first_passes(1)
-        y_t = keep.tile([P, 2, N], F32, name="y_t", tag="h3", align_bytes=64)
-        for mj in range(2):
-            nc.scalar.copy(y_t[:, mj, :], y_acc["turned", mj][:])
+        y_t = keep.tile([P, PACK, TURNED * P], F32, name="y_t", tag="h3", align_bytes=64)
+        for half in range(2):
+            nc.scalar.copy(y_t[:, 2 * half : 2 * half + 2, :], y_acc["turned", half][:])
         early_scales = keep.tile([P, 2, BANK], U8, name="early_scales", tag="z_high0", align_bytes=64)
         quantize_z(0, 1, codes_on("w3_bf1"), early_scales[:, 0, :])
         quantize_z(0, 2, codes_on("h7"), early_scales[:, 1, :])
         quantize_z(1, 1, codes_on("h4"))
 
-        def add_first(pair):
-            tiles = slice(2 * pair, 2 * pair + 2)
-            nc.vector.tensor_tensor(res_first[:, tiles, :], y_acc[0, pair][:], ambs[0][:, tiles, :], ADD)
-
-        res_first = keep.tile([P, N_TILES, BANK - TURNED], F32, name="res_first", tag="z_words01", align_bytes=64)
-        add_first(0)
-        add_first(1)
-        nc.sync.dma_start(out[:, TURNED:BANK].rearrange("(i p) m -> p i m", p=P), res_first[:])
+        res_first = keep.tile([P, N_TILES - TURNED, BANK], F32, name="res_first", tag="z_words01", align_bytes=64)
+        for i in range(TURNED, N_TILES):
+            nc.vector.tensor_tensor(res_first[:, i - TURNED, :], y_acc[0, i][:], ambs[0][:, i - TURNED, :], ADD)
+        nc.sync.dma_start(out[TURNED * P : N, 0:BANK].rearrange("(i p) m -> p i m", p=P), res_first[:])
         for b in range(2):
             passes(b, 1, (0, 1))
         for i in (2, 3):
@@ -469,12 +463,12 @@ def tile_list_transformer_overload_board_kernel(
             if i == 2:
                 turn_into_sums(y_t, False)
         last_rows = keep.tile([P, 6, BANK], BF16, name="last_rows", tag="z_words11", align_bytes=64)
-        res_turned = last_rows[:, 1:5, :].bitcast(F32)
-        for pair in range(2):
-            nc.scalar.copy(res_turned[:, 2 * pair : 2 * pair + 2, :], sums[pair][:])
+        res_turned = last_rows[:, 1:5, :].rearrange("p (i u) m -> p i (u m)", u=2).bitcast(F32)
+        for i in range(TURNED):
+            nc.scalar.copy(res_turned[:, i, :], sums[i][:])
         for i in range(N_TILES):
             add_and_store(1, i)
-        nc.sync.dma_start(out[:, 0:TURNED].rearrange("(i p) m -> p i m", p=P), res_turned)
+        nc.sync.dma_start(out[0 : TURNED * P, 0:BANK].rearrange("(i p) m -> p i m", p=P), res_turned)
         passes(0, 2)
         cols = slice(LAST * BANK, T2)
         z_last = last_rows[:, 0:6:5, :]

from contextlib import ExitStack

import concourse.mybir as mybir
from concourse.masks import make_identity

K1, H, N, T, S, T2 = 512, 1024, 512, 2048, 1024, 2048
FLOPS = 2 * (2 * K1) * H * S + 2 * H * N * T2

F32 = mybir.dt.float32
BF16 = mybir.dt.bfloat16
I32 = mybir.dt.int32
U32 = mybir.dt.uint32
U16 = mybir.dt.uint16
U8 = mybir.dt.uint8
FP8X4 = mybir.dt.float8_e4m3fn_x4
FP4X4 = mybir.dt.float4_e2m1fn_x4
MULT = mybir.AluOpType.mult
ADD = mybir.AluOpType.add
GELU = mybir.ActivationFunctionType.Gelu_apprx_tanh

P = 128
PACK = 4
BANK = 512
BANKS = 8
HALVES = S // BANK
CHUNKS = T2 // BANK
N_TILES = N // P
SLICES = 8
FIRST = 256
SCALE_ROW = (4, 0)
PAGE_OF = (0, 1, 2, 0, 1, 2, 0, 1)
TURNED = 2
LAST = CHUNKS - 1


def tile_list_transformer_overload_board_kernel(
    tc, tab_words, tab_scales, offs, w1, w2_words, w2_scales, wgs, offs2, gain, w3, amb, out
):
    nc = tc.nc
    with ExitStack() as ctx:
        keep = ctx.enter_context(tc.tile_pool(name="keep", bufs=1))
        stage = ctx.enter_context(tc.tile_pool(name="stage", bufs=6))
        arena = ctx.enter_context(tc.tile_pool(name="arena", bufs=1))
        psum = ctx.enter_context(tc.psum_pool(name="psum", bufs=1))

        def load_rows(src, dtype, name):
            t = stage.tile([P, 2048], dtype, name=name, tag="rows")
            nc.sync.dma_start(t[:], src)
            return t

        def load_k_first(src, name):
            t = stage.tile([P, PACK, 512], F32, name=name, tag="rows")
            nc.sync.dma_start(t[:], src.rearrange("(p j) c -> p j c", j=PACK))
            return t

        w2_s_raw = keep.tile([P, H], U8, name="w2_s_raw", tag="page2", align_bytes=64)
        tab_s = keep.tile([P, T], U8, name="tab_s", tag="tab_s", align_bytes=64)
        nc.gpsimd.memset(w2_s_raw[:].bitcast(I32), 0)
        nc.gpsimd.memset(tab_s[:].bitcast(I32), 0)
        pages = [keep.tile([P, T2], F32, name="page", tag="page%d" % i, align_bytes=64) for i in range(2)]
        for page in pages:
            nc.gpsimd.memset(page[:], 0.0)

        def load_tab_scales(run):
            r, a = divmod(run, 2)
            nc.sync.dma_start(
                tab_s[SCALE_ROW[a] + r : P : 32, :].bitcast(I32),
                tab_scales[a, r:16:4, :].bitcast(I32),
            )

        def load_w2_scales(r):
            nc.sync.dma_start(w2_s_raw[r:P:32, :].bitcast(I32), w2_scales[0, r:16:4, :].bitcast(I32))

        def load_table(a):
            return load_rows(tab_words[a].rearrange("p t i -> p (t i)").bitcast(I32), I32, "tab%d" % a)

        idx = keep.tile([P, S // 16], U16, name="idx")
        nc.sync.dma_start(idx[:], offs)
        tabs = [load_table(0)]
        for r in range(4):
            load_w2_scales(r)
        for run in range(2):
            load_tab_scales(run)
        w1_raw = [load_k_first(w1[:, 0:512], "w1_raw0")]
        for run in range(2, 8):
            load_tab_scales(run)
        tabs.append(load_table(1))
        w2_raw = [keep.tile([P, H], U8, name="w2_raw%d" % b) for b in range(2)]
        nc.sync.dma_start(w2_raw[0][:].bitcast(I32), w2_words[0][:, 0:H].bitcast(I32))
        wgs_sb = keep.tile([P, S], F32, name="wgs_sb")
        nc.sync.dma_start(wgs_sb[:], wgs)
        idx2 = keep.tile([P, S // 16], U16, name="idx2")
        nc.sync.dma_start(idx2[:], offs2)
        w1_raw1 = arena.tile([P, PACK, 512], F32, name="w1_raw1", align_bytes=64, offset=0)
        nc.sync.dma_start(w1_raw1[:], w1[:, 512:1024].rearrange("(p j) c -> p j c", j=PACK))
        w1_raw.append(w1_raw1)
        nc.sync.dma_start(w2_raw[1][:].bitcast(I32), w2_words[0][:, H : 2 * H].bitcast(I32))

        gain_rows = gain.rearrange("(b p j) m -> b j p m", b=2, j=PACK)
        gains = {}
        w3_raw = []
        ambs = {}
        amb_apart = {}

        def load_amb(c):
            first = TURNED if c == 0 else 0
            ambs[c] = stage.tile([P, N_TILES - first, BANK], F32, name="amb%d" % c, tag="rows")
            rows = amb[first * P : N, c * BANK : (c + 1) * BANK].rearrange("(i p) m -> p i m", p=P)
            if c == 2:
                amb_apart[c, 0] = keep.tile([P, BANK], F32, name="amb_apart", tag="amb_apart", align_bytes=64)[:]
                nc.sync.dma_start(amb_apart[c, 0], rows[:, 0, :])
                nc.sync.dma_start(ambs[c][:, 1:N_TILES, :], rows[:, 1:N_TILES, :])
            else:
                nc.sync.dma_start(ambs[c][:], rows)

        for k in range(SLICES):
            rows = gain_rows[k // PACK, k % PACK]
            if k < SLICES - 1:
                gains[k] = load_rows(rows, F32, "gain%d" % k)
            else:
                last_gains = []
                for c in range(CHUNKS):
                    g_sb = keep.tile([P, BANK], F32, name="last_gain", tag="last_gain%d" % c, align_bytes=64)
                    nc.sync.dma_start(g_sb[:], rows[:, c * BANK : (c + 1) * BANK])
                    last_gains.append(g_sb[:])
            if k == 5:
                w3_raw.extend(load_k_first(w3[512 * b : 512 * (b + 1), :], "w3_raw%d" % b) for b in range(2))
                amb_first = keep.tile([P, TURNED, BANK], F32, name="amb_first", align_bytes=64)
                nc.sync.dma_start(amb_first[:], amb[0 : TURNED * P, 0:BANK].rearrange("(i p) m -> p i m", p=P))
        for c in range(CHUNKS):
            load_amb(c)

        def quantize(src_bf16, name, codes, scales=None):
            if scales is None:
                scales = keep.tile([P, BANK], U8, name=name + "_scales", align_bytes=64)[:]
            nc.vector.quantize_mx(out=codes[:].bitcast(FP8X4), scales=scales, in_=src_bf16)
            return codes[:], scales

        def codes_on(tag):
            return keep.tile([P, BANK], U32, name="codes", tag=tag, align_bytes=64)

        def cast_w1(b, dst, ts):
            nc.scalar.copy(
                dst.rearrange("p (t m j) -> p m j t", m=P, j=PACK),
                w1_raw[b][:].rearrange("p j (m t) -> p m j t", t=PACK)[:, :, :, ts],
            )

        def cast_w3(b, dst):
            nc.scalar.copy(
                dst.rearrange("p (c i j) -> p c j i", i=4, j=PACK),
                w3_raw[b][:].rearrange("p j (c i) -> p c j i", i=4),
            )

        words0 = keep.tile([P, S], U32, name="words0", align_bytes=64)
        g_scales = keep.tile([P, S], U8, name="g_scales", align_bytes=64)
        w2_p = [keep.tile([P, H], U8, name="w2_p0", align_bytes=64)]

        def deal_w2(b, ts):
            nc.scalar.copy(
                w2_p[b][:].bitcast(U16).rearrange("p (t m) -> p t m", t=PACK)[:, ts],
                w2_raw[b][:].bitcast(U16).rearrange("p (m t) -> p t m", t=PACK)[:, ts],
            )

        w2_s = keep.tile([P, H], U8, name="w2_s", align_bytes=64)

        w1_bf0 = keep.tile([P, 2048], BF16, name="w1_bf0", tag="w1_then_words1", align_bytes=64)
        cast_w1(0, w1_bf0[:], slice(0, PACK))
        for ts in (slice(0, 2), slice(2, PACK)):
            deal_w2(0, ts)
        nc.vector.tensor_copy(words0[:], tabs[0][:].bitcast(U32).indirect(idx[:]))
        nc.vector.tensor_copy(
            w2_s[:].rearrange("p (b t m) -> p b t m", b=2, t=PACK),
            w2_s_raw[:].rearrange("p (b m t) -> p b t m", b=2, t=PACK),
        )
        nc.vector.tensor_copy(g_scales[:], tab_s[:].indirect(idx[:]))
        pages.append(keep.tile([P, T2], F32, name="page2", tag="page2", align_bytes=64))
        nc.gpsimd.memset(pages[2][:], 0.0)
        ident = keep.tile([P, P], F32, name="ident", align_bytes=64)
        make_identity(nc, ident[:])
        w1_codes = keep.tile([P, H], U32, name="w1_codes", align_bytes=64)
        w1_scales = keep.tile([P, H], U8, name="w1_scales", align_bytes=64)

        def quantize_w1(src, col):
            cols = slice(col, col + src.shape[1] // PACK)
            nc.vector.quantize_mx(out=w1_codes[:, cols].bitcast(FP8X4), scales=w1_scales[:, cols], in_=src)

        words1 = []
        quantize_w1(w1_bf0[:], 0)
        for jh in range(HALVES):
            words1.append(keep.tile([P, BANK], U32, name="words1", tag="w1_then_words%d" % jh, align_bytes=64))
            for lo in range(0, BANK, FIRST if jh == 0 else BANK):
                js = slice(jh * BANK + lo, jh * BANK + lo + (FIRST if jh == 0 else BANK))
                nc.vector.tensor_copy(
                    words1[jh][:, lo : lo + js.stop - js.start],
                    tabs[1][:].bitcast(U32).indirect(idx[:, js.start // 16 : js.stop // 16]),
                )

        hs = {}
        raw = {}

        def bank_tile(bank, name, shape=(P, BANK)):
            return psum.tile(list(shape), F32, name=name, tag="bank%d" % bank)

        def heat(k, js, bank, dst):
            b, t = divmod(k, PACK)
            col = b * 512 + t * P
            width = js.stop - js.start
            jh, lo = divmod(js.start, BANK)
            acc = bank_tile(bank, "e_acc")
            squares = (
                w2_p[b][:, 2 * t * P : 2 * (t + 1) * P].bitcast(FP4X4),
                w2_s[:, col : col + P],
                words1[jh][:, lo : lo + width],
                g_scales[SCALE_ROW[1] : P, js],
            )
            currents = (
                w1_codes[:, col : col + P].bitcast(FP8X4),
                w1_scales[:, col : col + P],
                words0[:, js],
                g_scales[SCALE_ROW[0] : P, js],
            )
            order = (currents, squares) if width == FIRST else (squares, currents)
            for n, (weights, weight_scales, words, word_scales) in enumerate(order):
                nc.tensor.matmul_mx(
                    out=acc[:, 0:width],
                    lhsT=weights,
                    lhsT_scale=weight_scales,
                    rhs=words.bitcast(FP8X4),
                    rhs_scale=word_scales,
                    start=n == 0,
                    stop=n == 1,
                )
            nc.scalar.activation(dst, acc[:, 0:width], GELU)

        def stage1(k, jhs=(0, 1)):
            if k not in hs:
                hs[k] = keep.tile([P, S], F32, name="h", tag="h%d" % k, align_bytes=64)
            for jh in jhs:
                js = slice(jh * BANK, (jh + 1) * BANK)
                raw.setdefault((k, jh), hs[k][:, js])
                heat(k, js, (2 * k + 1 + jh) % BANKS, raw[k, jh])

        def weigh(k):
            nc.gpsimd.tensor_tensor(hs[k][:], hs[k][:], wgs_sb[:], MULT)

        def weigh_half(k, jh):
            js = slice(jh * BANK, (jh + 1) * BANK)
            nc.gpsimd.tensor_tensor(hs[k][:, js], raw[k, jh], wgs_sb[:, js], MULT)

        def scatter(k, js=slice(0, S)):
            offsets = idx2[:, js.start // 16 : js.stop // 16]
            nc.vector.tensor_copy(pages[PAGE_OF[k]][:].indirect(offsets), hs[k][:, js])

        z_slot = {}

        def times_gain(k, chunks, dst=None):
            nc.gpsimd.tensor_tensor(
                z_slot[k][:, chunks, :] if dst is None else dst,
                pages[PAGE_OF[k]][:].rearrange("p (c m) -> p c m", c=CHUNKS)[:, chunks, :],
                gains[k][:].rearrange("p (c m) -> p c m", c=CHUNKS)[:, chunks, :],
                MULT,
            )

        hs[0] = keep.tile([P, S], F32, name="h", tag="h0", align_bytes=64)
        low, high = slice(0, BANK), slice(BANK, S)
        raw0 = keep.tile([P, BANK], F32, name="raw0", tag="h1", align_bytes=64)
        for bank, js in enumerate((slice(0, FIRST), slice(FIRST, BANK))):
            heat(0, js, bank, raw0[:, js])
        raw1 = arena.tile([P, BANK], F32, name="raw1", align_bytes=64, offset=8192)
        raw[1, 0] = raw1[:]
        stage1(1, (0,))
        heat(0, high, 2, hs[0][:, high])
        for k in (2, 3):
            stage1(k, (0,))
        w1_bf1 = arena.tile([P, 2048], BF16, name="w1_bf1", align_bytes=64, offset=8192)
        cast_w1(1, w1_bf1[:], slice(0, PACK))
        late = arena.tile([P, 3, BANK], F32, name="late", align_bytes=64, offset=2048)
        for k in (1, 2, 3):
            raw[k, 1] = late[:, k - 1, :]
            stage1(k, (1,))
        w2_p.append(arena.tile([P, H], U8, name="w2_p1", align_bytes=64, offset=0))
        deal_w2(1, slice(0, PACK))
        for js in (slice(0, FIRST), slice(FIRST, BANK)):
            nc.vector.tensor_tensor(hs[0][:, js], raw0[:, js], wgs_sb[:, js], MULT)
        for js in (slice(0, FIRST), slice(FIRST, BANK)):
            scatter(0, js)
        weigh_half(1, 0)
        scatter(1, low)
        raw[0, 1] = hs[0][:, high]
        weigh_half(0, 1)
        scatter(0, high)
        for k in (2, 3):
            weigh_half(k, 0)
        quantize_w1(w1_bf1[:], 512)
        for k in (1, 2, 3):
            weigh_half(k, 1)
        for k in range(4, SLICES):
            stage1(k)
        z_low = keep.tile([P, 2, T2], BF16, name="z_low", align_bytes=64)
        z_high0 = keep.tile([P, 2, BANK], BF16, name="z_high0", tag="z_high0", align_bytes=64)
        z_high = keep.tile([P, 3 * BANK + 2048], BF16, name="z_high", align_bytes=64)
        w3_bf1 = keep.tile([P, 2048], BF16, name="w3_bf1", tag="w3_bf1", align_bytes=64)
        w3_bf = [z_high[:, 3 * BANK : 3 * BANK + 2048], w3_bf1[:]]
        for b in range(2):
            cast_w3(b, w3_bf[b])

        z_pairs = arena.tile([P, 4 * T2], BF16, name="z_pairs", align_bytes=64, offset=4096)
        for t in range(PACK):
            z_slot[t] = z_pairs[:].rearrange("p (c u m e) -> p c u m e", c=CHUNKS, u=2, e=2)[:, :, t // 2, :, t % 2]
        for t in range(2):
            z_slot[4 + t] = z_low[:, t, :].rearrange("p (c m) -> p c m", c=CHUNKS)
        later_rows = z_high[:, 0 : 4 * BANK].rearrange("p (c t m) -> p c t m", c=2, t=2)
        high_rows = [z_high0[:], later_rows[:, 0], later_rows[:, 1]]
        z_words = {
            (b, c): keep.tile([P, 2048], BF16, name="z_words", tag="z_words%d%d" % (b, c), align_bytes=64)[:]
            for b in range(2)
            for c in range(CHUNKS)
        }

        def weave_pass0(c):
            nc.scalar.copy(
                z_words[0, c].bitcast(F32).rearrange("p (m u) -> p m u", u=2),
                z_pairs[:, c * 2048 : (c + 1) * 2048].bitcast(F32).rearrange("p (u m) -> p m u", u=2),
            )

        def place_pair(c, u, rows):
            nc.scalar.copy(
                z_words[1, c].rearrange("p (m i t) -> p m t i", i=4, t=PACK)[:, :, 2 * u : 2 * u + 2, :],
                rows.rearrange("p t (m i) -> p m t i", i=4),
            )

        def place_low(c):
            place_pair(c, 0, z_low[:, :, c * BANK : (c + 1) * BANK])

        def place_high(c):
            place_pair(c, 1, high_rows[c])

        sums = {}

        def turn_into_sums(src, first):
            for i in range(TURNED):
                if first:
                    sums[i] = bank_tile(6 + i, "sum_acc")
                for mj in range(PACK):
                    nc.tensor.matmul(
                        sums[i][:, mj * P : (mj + 1) * P],
                        lhsT=src[:, mj, i * P : (i + 1) * P],
                        rhs=ident[:],
                        start=first and mj == 0,
                        stop=not first and mj == PACK - 1,
                        is_transpose=True,
                    )

        def turn_amb():
            amb_t = keep.tile([P, PACK, TURNED * P], F32, name="amb_t", tag="h1", align_bytes=64)
            for half in range(2):
                acc = bank_tile(4 + half, "amb_acc", (P, 2, TURNED * P))
                for mm in range(2):
                    for i in range(TURNED):
                        m_cols = slice((2 * half + mm) * P, (2 * half + mm + 1) * P)
                        nc.tensor.transpose(acc[:, mm, i * P : (i + 1) * P], amb_first[:, i, m_cols], ident[:])
                nc.scalar.copy(amb_t[:, 2 * half : 2 * half + 2, :], acc[:])
            turn_into_sums(amb_t, True)

        for k in range(1, SLICES):
            scatter(k, high if k == 1 else slice(0, S))
            if k - 1 == 5:
                times_gain(5, slice(0, 2))
                times_gain(5, slice(2, CHUNKS))
            elif k - 1 == 6:
                times_gain(6, slice(0, 1), z_high0[:, 0:1, :])
                times_gain(6, slice(1, 3), later_rows[:, :, 0, :])
            else:
                times_gain(k - 1, slice(0, CHUNKS))
            if k + 3 < SLICES:
                weigh(k + 3)
            if k == 4:
                for c in range(CHUNKS):
                    weave_pass0(c)
            if k == 5:
                turn_amb()
            if k == 6:
                for c in range(CHUNKS):
                    place_low(c)

        zq = {}
        w3q = []
        y_acc = {}
        banks_of = {0: (None, None, 0, 1), 1: (2, 3, 4, 5), 2: (0, 1, 2, 3), 3: (4, 5, 6, 7)}

        def mx_pass(acc, lhs, lhs_cols, rhs, rhs_cols, start, stop):
            nc.tensor.matmul_mx(
                out=acc,
                lhsT=lhs[0][:, lhs_cols].bitcast(FP8X4),
                lhsT_scale=lhs[1][:, lhs_cols],
                rhs=rhs[0][:, rhs_cols].bitcast(FP8X4),
                rhs_scale=rhs[1][:, rhs_cols],
                start=start,
                stop=stop,
            )

        def passes(b, c, tiles=range(N_TILES)):
            for i in tiles:
                if b == 0:
                    y_acc[c, i] = bank_tile(banks_of[c][i], "y_acc")
                mx_pass(y_acc[c, i][:], w3q[b], slice(i * P, (i + 1) * P), zq[b, c], slice(0, BANK), b == 0, b == 1)

        def first_passes(b):
            for mj in range(PACK):
                half, mm = divmod(mj, 2)
                if (b, mm) == (0, 0):
                    y_acc["turned", half] = bank_tile(4 + half, "yt_acc", (P, 2, TURNED * P))
                mx_pass(
                    y_acc["turned", half][:, mm, :], zq[b, 0], slice(mj * P, (mj + 1) * P), w3q[b], slice(0, TURNED * P),
                    (b, mm) == (0, 0), (b, mm) == (1, 1),
                )
            passes(b, 0, range(TURNED, N_TILES))

        def last_gain(c):
            cols = slice(c * BANK, (c + 1) * BANK)
            nc.vector.tensor_tensor(high_rows[c][:, 1, :], pages[PAGE_OF[7]][:, cols], last_gains[c], MULT)
            place_high(c)

        def add_and_store(c, i):
            pair = ambs[c][:, i - i % 2 : i - i % 2 + 2, :]
            nc.vector.tensor_tensor(pair[:, i % 2, :], y_acc[c, i][:], amb_apart.get((c, i), ambs[c][:, i, :]), ADD)
            cols = slice(c * BANK, (c + 1) * BANK)
            if i % 2 == 1:
                nc.sync.dma_start(out[(i - 1) * P : (i + 1) * P, cols].rearrange("(i p) m -> p i m", p=P), pair)

        def quantize_z(b, c, codes, scales=None):
            zq[b, c] = quantize(z_words[b, c], "zq%d%d" % (b, c), codes, scales)

        def quantize_w3(b, tag):
            w3q.append(quantize(w3_bf[b], "w3q%d" % b, codes_on(tag)))

        last_gain(0)
        last_gain(1)
        quantize_w3(0, "last_gain0")
        quantize_z(0, 0, codes_on("last_gain1"))
        first_passes(0)
        last_gain(2)
        quantize_w3(1, "z_words00")
        quantize_z(1, 0, codes_on("h0"))
        first_passes(1)
        y_t = keep.tile([P, PACK, TURNED * P], F32, name="y_t", tag="h3", align_bytes=64)
        for half in range(2):
            nc.scalar.copy(y_t[:, 2 * half : 2 * half + 2, :], y_acc["turned", half][:])
        early_scales = keep.tile([P, 2, BANK], U8, name="early_scales", tag="z_high0", align_bytes=64)
        quantize_z(0, 1, codes_on("w3_bf1"), early_scales[:, 0, :])
        quantize_z(0, 2, codes_on("h7"), early_scales[:, 1, :])
        quantize_z(1, 1, codes_on("h4"))

        res_first = keep.tile([P, N_TILES - TURNED, BANK], F32, name="res_first", tag="z_words01", align_bytes=64)
        for i in range(TURNED, N_TILES):
            nc.vector.tensor_tensor(res_first[:, i - TURNED, :], y_acc[0, i][:], ambs[0][:, i - TURNED, :], ADD)
        nc.sync.dma_start(out[TURNED * P : N, 0:BANK].rearrange("(i p) m -> p i m", p=P), res_first[:])
        for b in range(2):
            passes(b, 1, (0, 1))
        for i in (2, 3):
            for b in range(2):
                passes(b, 1, (i,))
            if i == 2:
                turn_into_sums(y_t, False)
        last_rows = keep.tile([P, 6, BANK], BF16, name="last_rows", tag="z_words11", align_bytes=64)
        res_turned = last_rows[:, 1:5, :].rearrange("p (i u) m -> p i (u m)", u=2).bitcast(F32)
        for i in range(TURNED):
            nc.scalar.copy(res_turned[:, i, :], sums[i][:])
        for i in range(N_TILES):
            add_and_store(1, i)
        nc.sync.dma_start(out[0 : TURNED * P, 0:BANK].rearrange("(i p) m -> p i m", p=P), res_turned)
        passes(0, 2)
        cols = slice(LAST * BANK, T2)
        z_last = last_rows[:, 0:6:5, :]
        for t, gain_k in enumerate((gains[SLICES - 2][:, cols], last_gains[LAST])):
            nc.gpsimd.tensor_tensor(z_last[:, t, :], pages[PAGE_OF[SLICES - 2 + t]][:, cols], gain_k, MULT)
        place_pair(LAST, 1, z_last)
        late_scales = keep.tile([P, 2, BANK], U8, name="late_scales", tag="page%d" % PAGE_OF[7], align_bytes=64)
        quantize_z(1, 2, codes_on("h5"), late_scales[:, 0, :])
        passes(1, 2)
        quantize_z(0, LAST, codes_on("h2"), late_scales[:, 1, :])
        passes(0, LAST, (0, 1))
        for i in range(2):
            add_and_store(2, i)
        last_scales = keep.tile([P, BANK], U8, name="last_scales", tag="amb_apart", align_bytes=64)
        quantize_z(1, LAST, codes_on("h6"), last_scales[:])
        passes(1, LAST, (0, 1))
        for i in (2, 3):
            for b in range(2):
                passes(b, LAST, (i,))
        for i in range(2, N_TILES):
            add_and_store(2, i)
        for i in range(N_TILES):
            add_and_store(LAST, i)
